import numpy as np, ml_dtypes
CORES = [113,118,241,246]
N = 4
BF = ml_dtypes.bfloat16
def gentries(a):
    return np.ascontiguousarray(a.reshape(8, 16, -1).transpose(0, 2, 1)).reshape(8, -1)
def gtable(e):
    e = np.asarray(e); return np.ascontiguousarray(e.reshape(8, -1, 16).transpose(0, 2, 1)).reshape(128, -1).astype(np.int32)
GW, GH, M, RO, HP = 64, 32, 512, 3, 2
W, D = GW * GH, 255
def parts(rng):
    s = np.exp2(rng.permutation(np.arange(16) % 3 - 1)).astype(np.float32).reshape(1, 1, 16, 1)
    x = s * np.exp2(2 * rng.random((N, 8, 16, W), dtype=np.float32) - 1)
    eps = s * (0.17 + 0.34 * rng.random((N, 8, 16, 1)))
    fl = np.where(rng.random((N, 8, 1, W)) < 0.6, rng.integers(-48, 49, (N, 8, 4, W)), rng.integers(-D, D + 1, (N, 8, 4, W)))
    cor = rng.integers(0, W, (N, 8, 4, W))
    ms = np.ascontiguousarray(np.argsort(rng.random((N, 8, W)), axis=-1)[..., :M])
    return x, eps, fl, cor, ms
def pack(x, eps, fl, cor, ms):
    return {"x": np.clip(x, 2.0 ** -20, 4.0).astype(BF).reshape(N, 128, W), "eps": np.ascontiguousarray(eps).astype(np.float32).reshape(N, 128, 1),
            "fl": np.ascontiguousarray(fl.transpose(0, 2, 1, 3)).astype(np.int32).reshape(N, 32, W),
            "cor": np.stack([gtable(a.reshape(8, -1)) for a in cor]), "ms": np.stack([gtable(a) for a in ms])}
def setup_inputs(rng):
    return pack(*parts(rng))
def setup_inputs_calm(rng):
    x, eps, fl, cor, ms = parts(rng)
    v = (np.arange(N).reshape(N, 1, 1, 1) + np.arange(8).reshape(1, 8, 1, 1) + np.arange(4).reshape(1, 1, 4, 1)) % 4
    fl = v * np.where(rng.random((N, 8, 4, W)) < 0.5, 1, -1) * (rng.random((N, 8, 1, W)) < 0.8)
    return pack(x, eps, fl, cor, ms)
def setup_inputs_corners(rng):
    x, eps, fl, cor, ms = parts(rng); sh = int(rng.integers(0, 6)); clear = int(rng.integers(0, 8)); own = np.arange(W)
    for q in range(N):
        o = rng.permutation(8); u = [int(v) for v in rng.permutation(8)]
        j = u.index(2 + q % 3); u[j], u[clear] = u[clear], u[j]
        for g in range(8):
            k = 0 if g == clear else (q + g + sh) % 6
            if k in (1, 4):
                m = ms[q, g]; ms[q, g] = rng.permutation(np.concatenate([np.array([0, W - 1]), m[(m != 0) & (m != W - 1)]])[:M])
            m = ms[q, g]; there = np.ones(W, bool); there[m] = False; kno = np.flatnonzero(there)
            if k == 0: cor[q, g] = rng.choice(kno, (4, W))
            if k == 1:
                c = rng.choice(kno, (4, W)); c[rng.integers(0, 4, W), own] = rng.choice(m, W); cor[q, g] = c
            if k == 2: cor[q, g] = own
            if k == 3: cor[q, g] = rng.choice(np.array([0, W - 1]), (4, W))
            if k == 4: cor[q, g] = rng.choice(m, (4, W))
            if o[g] == 0: fl[q, g] = 0
            if o[g] == 1: fl[q, g] = rng.choice(np.array([-D, D]), (4, W))
            if o[g] == 2: fl[q, g] = rng.choice(np.array([-D, 0, D]), (4, W))
            n = (0, 8, 9, 15, 16, -1, -1, -1)[u[g]]
            if n >= 0: eps[q, g, :, 0] = rng.permutation(np.where(np.arange(16) < n, 4.0, 0.0))
    return pack(x, eps, fl, cor, ms)
def setup_inputs_ends(rng):
    x, eps, fl, cor, ms = parts(rng); h = M // 2; tips = np.array([0, GW - 1, W - GW, W - 1])
    x = np.where(rng.random(x.shape) < 0.5, np.float32(4), np.float32(2.0 ** -20))
    m = rng.random((N, 8, 1, W)) < 0.8; m[..., tips] = True
    fl = np.where(m, np.where(rng.random(fl.shape) < 0.5, D, -D), fl)
    cor = np.where(rng.random((N, 8, 1, W)) < 0.75, np.where(rng.random(cor.shape) < 0.5, 0, W - 1), cor)
    top = np.where(np.arange(16) % 2 == 0, 4.0, 4.0 - 2.0 ** -20)
    for q in range(N):
        o = rng.permutation(8)
        for g in range(8):
            lo, hi = (1, 1, 1, 1, 0, 1, 0, 0)[g], (1, 1, 1, 1, 0, 0, 1, 0)[g]
            s = np.concatenate([np.arange(lo, lo + h), np.arange(W - hi - h, W - hi)])
            ms[q, g] = np.concatenate([s[:1], rng.permutation(s[1:-1]), s[-1:]])
            if g >= 4 and q % 2 == 1: cor[q, g][:, tips[[0, 3]]] = rng.integers(h + 1, W - 1 - h, (4, 2))
            n = (16, 9, 8, 9, 8, 7, 12, 0)[int(o[g])]
            eps[q, g, :, 0] = rng.permutation(np.where(np.arange(16) < n, top, 0.0))
    return pack(x, eps, fl, cor, ms)
def setup_inputs_spread(rng):
    x, eps, fl, cor, ms = parts(rng)
    x = np.exp2(2 * rng.random((N, 8, 16, W), dtype=np.float32) - 1) * np.exp2(rng.integers(-1, 2, (N, 8, 1, W))).astype(np.float32)
    eps = np.exp2(4 * rng.random((N, 8, 16, 1)) - 2.5)
    fl = rng.integers(-D, D + 1, (N, 8, 4, W))
    v = np.minimum(np.exp2(rng.random((N, 4, 4, W)) * np.log2(D)).astype(np.int64), D)
    fl[:, 1::2] = v * np.where(rng.random((N, 4, 4, W)) < 0.5, 1, -1)
    cor[:, ::2] = np.minimum((W * rng.random((N, 4, 4, W)) ** 3).astype(np.int64), W - 1)
    return pack(x, eps, fl, cor, ms)
def setup_inputs_ties(rng):
    x, eps, fl, cor, ms = parts(rng)
    x = rng.integers(1, 9, (N, 8, 16, W)).astype(np.float32) * np.float32(0.5)
    eps = rng.choice(np.array([0.0, 1.0 - 2.0 ** -24, 1.0, 1.5, 2.0]), (N, 8, 16, 1))
    fl = np.where(rng.random((N, 8, 1, W)) < 0.8, np.maximum(fl // 4 * 4, 3 - D), fl)
    own = np.arange(W); pool = np.flatnonzero((own % GW % 2 == 0) & (own // GW % 2 == 0))
    for i, g in enumerate([int(v) for v in rng.permutation(8)[:3]]):
        pix = rng.permutation(pool)[:M]; kno = np.setdiff1d(own, pix); fx, fy = [int(v) for v in rng.integers(1, 4, 2)]
        x[:, g] = (128 + rng.integers(0, 128, (16, W))) * np.exp2(np.where(rng.random((16, W)) < 0.5, rng.integers(-8, -5, (16, W)), rng.integers(-27, -24, (16, W))))
        eps[:, g] = 0; t = rng.choice(kno, (4, W)); v = fl[:, g]
        v[:] = np.array([fx, fy, fx, fy + 4]).reshape(4, 1)
        if i == 0:
            n = M // 3; a, b, c = pix[:n], pix[n:2 * n], pix[2 * n:3 * n]
            t[:, a + GW] = t[:, a]; t[:, b + GW] = t[:, a]; t[:, c + GW] = t[:, a]
            t[:, b] = a; t[:, c] = b
        else:
            v[:, :, pix + (1, GW)[i - 1]] = np.array([fx + 4, fy, fx + 4, fy]).reshape(4, 1)
        cor[:, g] = t
        for q in range(N): ms[q, g] = rng.permutation(pix)
    return pack(x, eps, fl, cor, ms)
def check_ranges(d):
    bad = []
    for k, lo, hi in (("x", 2.0 ** -20, 4), ("eps", 0, 4), ("fl", -D, D), ("cor", 0, W - 1), ("ms", 0, W - 1)):
        v = np.asarray(d[k]).astype(np.float64)
        if not np.all((v >= lo) & (v <= hi)): bad.append("range of " + k)
    s = np.sort(np.stack([gentries(np.asarray(a)) for a in d["ms"]]), axis=-1)
    if np.any(s[..., 1:] == s[..., :-1]): bad.append("a number twice in a group of ms")
    return bad
def chase(a, way, xs, kn, fw, taps, mis, home):
    sg = 1 - 2 * way; lim = np.array([4 * GW - 1, 4 * GH - 1]).reshape(1, 2, 1)
    z = np.zeros((8, 16, M), np.float32); got = np.zeros((8, M), np.int64); end = np.zeros((8, 2, M), np.int64)
    pos = home[a]; step = np.take_along_axis(fw[a][:, 2 * way:2 * way + 2], mis[a][:, None, :], 2)
    for h in range(1, HP + 1):
        q = (a + sg * h) % N; gi = (np.arange(8) + sg * (h - 1)) % 8
        pos = np.minimum(np.maximum(pos + step, 0), lim)
        cell = (pos[:, 1] >> 2) * GW + (pos[:, 0] >> 2); part = (pos & 3).astype(np.float32) * np.float32(0.25)
        t = np.take_along_axis(taps[q][gi], cell[:, None, :], 2).reshape(8, 4 * M)
        ok = np.all(np.take_along_axis(kn[q][gi], t, 1).reshape(8, 4, M), axis=1)
        v = np.take_along_axis(xs[q][gi], t[:, None, :], 2).reshape(8, 16, 4, M)
        u0 = part[:, 0][:, None, :]; u1 = part[:, 1][:, None, :]
        up = v[:, :, 0] + u0 * (v[:, :, 1] - v[:, :, 0]); dn = v[:, :, 2] + u0 * (v[:, :, 3] - v[:, :, 2])
        w = up + u1 * (dn - up)
        new = ok & (got == 0)
        z = np.where(new[:, None, :], w, z); end = np.where(new[:, None, :], pos, end); got = np.where(new, h, got)
        step = np.take_along_axis(fw[q][:, 2 * way:2 * way + 2][gi], cell[:, None, :], 2)
    return z, got, end
def reference(x, eps, fl, cor, ms):
    xs = x.astype(np.float32).reshape(N, 8, 16, W); ep = eps.astype(np.float32).reshape(N, 8, 16, 1)
    fw = np.ascontiguousarray(fl.astype(np.int64).reshape(N, 4, 8, W).transpose(0, 2, 1, 3))
    taps = np.stack([gentries(a) for a in cor]).astype(np.int64).reshape(N, 8, 4, W); mis = np.stack([gentries(a) for a in ms]).astype(np.int64)
    kn = np.ones((N, 8, W), bool); np.put_along_axis(kn, mis, False, 2)
    mx = mis % GW; my = mis // GW; home = np.stack([4 * mx, 4 * my], axis=2)
    done = np.zeros((N, 8, M), bool); val = np.zeros((N, 8, 16, M), np.float32); ex = np.zeros((N, 8, 16, M), np.float64)
    for rnd in range(RO):
        ends = [(chase(a, 0, xs, kn, fw, taps, mis, home), chase(a, 1, xs, kn, fw, taps, mis, home)) for a in range(N)]
        nb = ((my + (0, 1, 0)[rnd]) % GH) * GW + (mx + (1, 0, GW - 1)[rnd]) % GW
        for a in range(N):
            (zf, gf, pf), (zb, gb, pb) = ends[a]
            both = (gf > 0) & (gb > 0); open_ = ~done[a]; dif = zf - zb; gap = np.abs(dif)
            agree = np.add.reduce((gap <= ep[a]).astype(np.int64), axis=1)
            won = both & open_ & (agree >= 9)
            ex[a] = np.where(open_[:, None, :], np.where(both[:, None, :], np.exp(-gap.astype(np.float64)), 0.0), ex[a])
            val[a] = np.where(won[:, None, :], zb + np.float32(0.5) * dif, val[a])
            cur = np.take_along_axis(fw[a], mis[a][:, None, :], 2); near = np.take_along_axis(fw[a], nb[a][:, None, :], 2)
            own = np.concatenate([(pf - home[a]) >> np.maximum(gf - 1, 0)[:, None, :], (pb - home[a]) >> np.maximum(gb - 1, 0)[:, None, :]], axis=1)
            new = np.where(won[:, None, :], own, np.where(open_[:, None, :], near, cur))
            done[a] = done[a] | won
            np.put_along_axis(fw[a], np.broadcast_to(mis[a][:, None, :], (8, 4, M)), new, 2)
            np.put_along_axis(kn[a], mis[a], done[a], 1)
            np.put_along_axis(xs[a], np.broadcast_to(mis[a][:, None, :], (8, 16, M)), val[a], 2)
    last = np.stack([np.take_along_axis(fw[a], mis[a][:, None, :], 2) for a in range(N)])
    yf = np.concatenate([last.transpose(0, 2, 1, 3).reshape(N, 32, M), done.astype(np.int64)], axis=1)
    return {"y": val.reshape(N, 128, M), "ye": ex.reshape(N, 128, M).astype(np.float32), "yf": yf.astype(np.float32)}

def check_inputs(d):
    bad = list(check_ranges(d))
    if not bad:
        for name, y in reference(**d).items():
            for q in range(N):
                v = np.abs(np.asarray(y[q], np.float64)); s = np.sqrt(np.mean(v * v))
                if v.max() > 8 * s or s < 2.0 ** -3: bad.append('%s of rank %d is uneven or too small' % (name, q))
    return bad

@@ -1,0 +1,741 @@
+from concourse.bass import DstId, RemoteDMATransfer
+from concourse.mybir import AluOpType as ALU, ActivationFunctionType as ACT
+
+W, M, TW = 2048, 512, 2560
+BIG = float(2.0 ** 96)
+TINY = float(2.0 ** -46)
+MAGIC = float(3 * 2 ** 22)
+
+F32, BF, I32, U16 = "float32", "bfloat16", "int32", "uint16"
+
+
+def _sb(n, dt):
+    return ("sbuf", [128, n], dt)
+
+
+SCRATCH = {
+    "msi": _sb(32, I32), "cori": _sb(512, I32), "epsc": _sb(4, F32), "fli": _sb(W, I32), "xo": _sb(W, BF),
+    "ms16": _sb(32, U16), "cor16": _sb(512, U16), "mw": _sb(TW, BF), "gg": _sb(8192, BF),
+    "tbo": _sb(TW, BF), "tbn": _sb(2 * TW, BF), "lt": _sb(W, BF), "t2": _sb(2 * W, BF),
+    "xl": _sb(3 * W, BF), "xf": _sb(4 * TW, F32), "lv": _sb(M, F32),
+    "ip": _sb(4, I32), "ia": _sb(160, I32), "ir": _sb(64, F32), "ig": _sb(128, F32), "lj": _sb(32, F32),
+    "ci": _sb(8, I32), "cf": _sb(32, F32), "mk": _sb(16, F32), "hc": _sb(48, BF), "sm": _sb(8, F32),
+    "dd": _sb(160, BF), "sel": _sb(5 * 128, BF), "fx": _sb(4 * 160, BF), "g14": _sb(160, BF), "bo": _sb(128, BF),
+    "boi": _sb(16 * 128, BF), "di": _sb(16 * 160, BF), "cm": _sb(8 * 128, BF), "ti": _sb(128, I32), "tj": _sb(128, I32),
+    "home": _sb(128, F32), "hom4": _sb(128, F32), "nbi": _sb(96, I32), "nb16": _sb(96, U16), "nbm": _sb(64, F32),
+    "nr16": _sb(32, U16), "gr": _sb(1024, BF), "gn": _sb(1024, BF), "tt": _sb(1024, BF), "tu": _sb(1024, BF),
+    "pf": _sb(128, F32), "p10": _sb(128, I32), "p11": _sb(128, I32), "p2": _sb(128, I32),
+    "cc": _sb(128, I32), "pl": _sb(64, I32), "pm": _sb(64, I32), "pl16": _sb(64, U16), "pn16": _sb(128, U16),
+    "mp16": _sb(64, U16), "t1f": _sb(256, F32), "t116": _sb(256, U16), "t2f": _sb(256, F32), "tsf": _sb(256, F32),
+    "ts16": _sb(256, U16), "ok": _sb(64, F32), "fh": _sb(64, F32), "q1": _sb(128, F32), "q2": _sb(128, F32),
+    "pe": _sb(128, I32), "pa": _sb(128, I32), "uv": _sb(128, BF), "own": _sb(128, BF), "nt": _sb(64, F32),
+    "br": _sb(M, BF), "dif": _sb(M, F32), "gap": _sb(M, F32), "cmpb": _sb(M, BF), "half": _sb(M, F32),
+    "won": _sb(M, F32), "tw": _sb(M, F32), "pen": _sb(M, F32), "val": _sb(M, F32), "ex": _sb(M, F32),
+    "yea": _sb(M, F32), "old0": _sb(M, F32), "newf": _sb(M, F32), "yo": _sb(M, F32),
+    "aa": _sb(4 * M, F32), "da": _sb(4 * M, F32), "sa": _sb(2 * M, F32), "ea": _sb(2 * M, F32), "zf": _sb(M, F32),
+}
+for _b in range(8):
+    SCRATCH["b%d" % _b] = ("psum", [128, 512], F32)
+
+SEMAPHORES = (["v", "s", "p", "gp"] + ["d%d" % i for i in range(24)] + ["l%d" % i for i in range(36)]
+              + ["tb%d_%d" % (a, c) for a in range(3) for c in range(5)]
+              + ["x%d_%d" % (a, c) for a in range(3) for c in range(2)]
+              + ["st%d_%d" % (r, a) for r in range(2) for a in range(2)]
+              + ["vl%d_%d_%d" % (r, a, h) for r in range(2) for a in range(3) for h in range(2)]
+              + ["cr%d_%d" % (r, a) for r in range(2) for a in range(3)])
+
+
+def rank_program(g, core, T, topo):
+    rank = T.rank_of(core)
+    if rank is None:
+        return
+    N = len(T.cores)
+    cores = list(T.cores)
+    up, dn, op = (rank + 1) % N, (rank - 1) % N, (rank + 2) % N
+
+    def same_chip(a, b):
+        return cores[b] in topo.cores_of(cores[a])
+
+    def slot(src, dst):
+        return {1: 0, N - 1: 1, 2: 2}[(src - dst) % N]
+
+    near = up if same_chip(rank, up) else dn
+    far = dn if near == up else up
+    off_eng = topo.engines(core, cores[far])
+    on_eng = [e for e in topo.engines(core, cores[near]) if e not in off_eng]
+    off_mask = sum(1 << e for e in off_eng)
+    on_mask = sum(1 << e for e in on_eng)
+    NE = len(off_eng)
+
+    def mask_to(d):
+        return on_mask if same_chip(rank, d) else off_mask
+
+    def dst_id(d):
+        rid, pid = topo.addr(cores[d], core)
+        return DstId(rid=rid, pnc=pid)
+
+    Q = {"v": g.vector, "s": g.scalar, "p": g.tensor, "g": g, "y": g.sync}
+    cnt = {"v": 0, "s": 0, "p": 0, "gp": 0}
+    waited = {q: {} for q in Q}
+    recs = {}
+    owed = {}
+    pend = []
+    nxt = {"d": 0, "l": 0}
+
+    def S(name, lo=None, hi=None, step=None, rows=None):
+        t = T[name]
+        lo = 0 if lo is None else lo
+        hi = t.shape[1] if hi is None else hi
+        r = slice(None) if rows is None else rows
+        ap = t[r, lo:hi] if step is None else t[r, lo:hi:step]
+        return (ap, [(name, lo, hi)])
+
+    def L(name, lo, n):
+        return S(name, lo, lo + n)
+
+    def IND(win, off):
+        return (win[0].indirect(off[0]), win[1], off[1])
+
+    def wait(q, tok):
+        sem, val = tok[0], tok[1]
+        if waited[q].get(sem, 0) < val:
+            Q[q].wait_ge(T.sem[sem], val)
+            waited[q][sem] = val
+
+    def deps(q, eng, reads, writes):
+        need = {}
+        for keys, isw in ((reads, False), (writes, True)):
+            for (n, lo, hi) in keys:
+                ps = SCRATCH[n][0] == "psum"
+                for (a, b, w, tok) in recs.get(n, []):
+                    same = eng is not None and tok[2] == eng
+                    if same and eng == "p":
+                        continue
+                    if (ps and not same) or (a < hi and lo < b and (w or isw)):
+                        need[tok[0]] = max(need.get(tok[0], 0), tok[1])
+        for sem, val in need.items():
+            wait(q, (sem, val))
+
+    def note(reads, writes, tok):
+        for (n, lo, hi) in writes:
+            recs[n] = [x for x in recs.get(n, []) if not (lo <= x[0] and x[1] <= hi)] + [(lo, hi, True, tok)]
+        for (n, lo, hi) in reads:
+            keep = [x for x in recs.get(n, []) if not (not x[2] and x[3][0] == tok[0] and lo <= x[0] and x[1] <= hi)]
+            recs[n] = keep + [(lo, hi, False, tok)]
+
+    def keys_of(ins):
+        r = []
+        for a in ins:
+            if isinstance(a, tuple):
+                r += a[1]
+                if len(a) == 3:
+                    r += a[2]
+        return r
+
+    def ap(a):
+        return a[0] if isinstance(a, tuple) else a
+
+    def comp(q, sem, fn, out, ins):
+        reads = keys_of(ins) + (out[2] if len(out) == 3 else [])
+        writes = out[1]
+        deps(q, sem, reads, writes)
+        cnt[sem] += 1
+        fn().then_inc(T.sem[sem], 1)
+        note(reads, writes, (sem, cnt[sem], sem))
+
+    V = g.vector
+
+    def cp(out, a):
+        comp("v", "v", lambda: V.tensor_copy(out[0], a[0]), out, [a])
+
+    def tt(out, a, b, o):
+        comp("v", "v", lambda: V.tensor_tensor(out[0], a[0], b[0], o), out, [a, b])
+
+    def ts(out, a, s1, o1, s2=None, o2=None):
+        if o2 is None:
+            comp("v", "v", lambda: V.tensor_scalar(out[0], a[0], ap(s1), None, o1), out, [a, s1])
+        else:
+            comp("v", "v", lambda: V.tensor_scalar(out[0], a[0], ap(s1), ap(s2), o1, o2), out, [a, s1, s2])
+
+    def ms(out, c):
+        comp("v", "v", lambda: V.memset(out[0], c), out, [])
+
+    def tr(out, a):
+        comp("v", "v", lambda: V.transpose(out[0], a[0]), out, [a])
+
+    def act(out, a, f, scale=None, bias=None):
+        kw = {}
+        if scale is not None:
+            kw["scale"] = ap(scale)
+        if bias is not None:
+            kw["bias"] = ap(bias)
+        comp("s", "s", lambda: g.scalar.activation(out[0], a[0], f, **kw), out, [a, scale, bias])
+
+    def mv(out, a, on_s):
+        if on_s:
+            act(out, a, ACT.Copy)
+        else:
+            cp(out, a)
+
+    def iota(out, pat, base, cmul, small=False):
+        kw = {"allow_small_or_imprecise_dtypes": True} if small else {}
+        comp("g", "gp", lambda: g.iota(out[0], pat, base, cmul, **kw), out, [])
+
+    def mm(out, l, r, start, stop, inc=False):
+        reads, writes = l[1] + r[1], out[1]
+        deps("p", "p", reads, writes)
+        ins = g.tensor.matmul(out[0], l[0], r[0], start, stop)
+        pend.append((reads, writes))
+        if inc:
+            cnt["p"] += 1
+            ins.then_inc(T.sem["p"], 1)
+            for a, b in pend:
+                note(a, b, ("p", cnt["p"], "p"))
+            del pend[:]
+
+    def dma(q, pairs):
+        sem = "d%d" % nxt["d"]
+        nxt["d"] += 1
+        rd, wr = [], []
+        for o, i in pairs:
+            rd += i[1]
+            wr += o[1]
+        deps(q, None, rd, wr)
+        for o, i in pairs:
+            Q[q].dma_start(o[0], i[0]).then_inc(T.sem[sem], 16)
+        owed[sem] = 16 * len(pairs)
+        note(rd, wr, (sem, 16 * len(pairs), None))
+
+    def send(src, items, before=()):
+        sem = "l%d" % nxt["l"]
+        nxt["l"] += 1
+        deps("g", None, src[1], [])
+        for t in before:
+            wait("g", t)
+        trs = [RemoteDMATransfer(dst_ids=[dst_id(d)], dma_engine_mask=mask_to(d), remote_sem=T.sem[rs],
+                                 src=src[0], dst=land[0]) for d, land, rs in items]
+        g.remote_dma_fused(trs, local_sem=T.sem[sem])
+        owed[sem] = NE * len(items)
+        note(src[1], [], (sem, NE * len(items), None))
+
+    def landed(where, sem):
+        owed[sem] = NE
+        note([], where[1], (sem, NE, None))
+
+    def credit(keys, dests, r):
+        deps("g", None, [], keys)
+        for d in dests:
+            sem = "l%d" % nxt["l"]
+            nxt["l"] += 1
+            rid, pid = topo.addr(cores[d], core)
+            e = (on_eng if same_chip(rank, d) else off_eng)[0]
+            g.remote_sem_update(T.sem["cr%d_%d" % (r, slot(rank, d))], T.sem[sem], pid, rid, 1 << e)
+            owed[sem] = 1
+
+    def cr(r, src):
+        sem = "cr%d_%d" % (r, slot(src, rank))
+        owed[sem] = 1
+        return (sem, 1)
+
+    def B(i, lo=0, hi=512, step=None):
+        return S("b%d" % i, lo, hi, step)
+
+    def col(name, j):
+        return S(name, j, j + 1)
+
+    def CM(k):
+        return L("cm", 128 * k, 128)
+
+    add, sub, mul, mx, mn = ALU.add, ALU.subtract, ALU.mult, ALU.max, ALU.min
+    band, shr = ALU.bitwise_and, ALU.arith_shift_right
+    EYE = S("dd", 16, 144)
+    LAN = S("tbo", W, TW)
+    XA = [0, 2 * TW, TW, 3 * TW]
+    kn, kf = slot(near, rank), slot(far, rank)
+
+    dma("y", [(S("msi"), (T.ms[:], []))])
+    dma("s", [(S("xo", 0, 1024), (T.x[:, 0:1024], []))])
+    dma("y", [(S("cori"), (T.cor[:], []))])
+    dma("s", [(S("xo", 1024, 2048), (T.x[:, 1024:2048], []))])
+    iota(col("ip", 0), [[0, 1]], 0, 1)
+    iota(S("ir"), [[1, 64]], 0, 0, True)
+    iota(S("ia"), [[1, 160]], 0, -1)
+    iota(S("ig"), [[1, 8], [0, 16]], 0, 0, True)
+
+    def load_flows(c):
+        iota(L("fli", 1024 * c, 1024), [[0, 1024]], 0, 0)
+        dma("y", [(S("fli", 1024 * c, 1024 * c + 1024, rows=slice(10 + q, 128, 16)),
+                   (T.fl[8 * q:8 * q + 8, 1024 * c:1024 * c + 1024], [])) for q in range(4)])
+
+    load_flows(0)
+    dma("y", [(col("epsc", 0), (T.eps[:], []))])
+    for j in range(8):
+        act(L("val", 64 * j, 64), S("ir"), ACT.Identity, scale=0.0, bias=-BIG)
+    act(S("pen"), S("val"), ACT.Abs)
+
+    def send_x(c, dests):
+        send(L("xo", 1024 * c, 1024),
+             [(d, L("xl", slot(rank, d) * W + 1024 * c, 1024), "x%d_%d" % (slot(rank, d), c)) for d in dests])
+
+    send_x(0, (far, near))
+    send_x(1, (near,))
+    load_flows(1)
+    dma("y", [(L("xf", XA[k] + W, M), S("pen" if k % 2 else "val")) for k in range(4)])
+    iota(S("lj"), [[16, 32]], W, 0, True)
+
+    ts(col("ci", 0), col("ip", 0), 15, band)
+    ts(col("ci", 1), col("ip", 0), 4, shr)
+    cp(S("cf", 0, 2), S("ci", 0, 2))
+    ts(col("ci", 2), col("ip", 0), 16, band)
+    ts(col("cf", 2), col("cf", 0), 5.0, ALU.is_lt)
+    ts(col("cf", 10), col("cf", 0), 10.0, ALU.is_lt)
+    ts(S("mk"), S("ir", 0, 16), col("cf", 0), ALU.is_equal)
+    tt(col("cf", 3), col("cf", 10), col("cf", 2), sub)
+    ts(S("hc", 0, 48), S("ir", 0, 48), col("cf", 2), mul)
+    ts(col("cf", 11), col("mk", 15), 8192.0, mul)
+    ts(S("mw", 0, 64), S("ir"), col("cf", 3), mul)
+    tt(col("hc", 33), col("hc", 32), col("cf", 11), add)
+    ts(S("bo"), S("ig"), col("cf", 1), ALU.is_equal)
+    ts(S("dd"), S("ia"), 16.0, ALU.is_equal)
+    for i in range(16):
+        act(L("boi", 128 * i, 128), S("bo"), ACT.Copy, scale=col("mk", i))
+    n = 64
+    while n < W:
+        ts(S("mw", n, 2 * n), S("mw", 0, n), col("hc", n // 64), add)
+        if n == 64:
+            tt(S("sm", 0, 5), S("mk", 0, 5), S("mk", 5, 10), add)
+        if n == 128:
+            ts(S("sm", 0, 4), S("sm", 0, 4), col("mk", 15), add)
+        if n == 256:
+            ts(S("mw", W, TW), S("mw", 0, M), col("hc", 33), add)
+        n *= 2
+    ts(col("cf", 4), col("ci", 2), 0.0, ALU.is_equal)
+    ts(col("cf", 5), col("ci", 2), 0.0, ALU.is_gt)
+    cp(S("ms16"), S("msi"))
+    for h in range(2):
+        ts(L("fx", 320 * h + 160, 160), S("dd"), col("cf", 4 + h), mul, 64.0, mul)
+    for i in range(5):
+        act(L("sel", 128 * i, 128), EYE, ACT.Copy, scale=col("sm", i))
+    for h in range(2):
+        act(L("fx", 320 * h, 160), S("dd"), ACT.Copy, scale=col("cf", 4 + h))
+    for i in range(DI_EARLY):
+        act(L("di", 160 * i, 160), S("dd"), ACT.Copy, scale=col("mk", i))
+    cp(IND(S("mw", 0, W), S("ms16")), S("mw", W, TW))
+    cp(S("cor16", 0, 128), S("cori", 0, 128))
+    cp(S("cor16", 128, 512), S("cori", 128, 512))
+
+    def relay_x(c):
+        a = L("xl", kf * W + 1024 * c, 1024)
+        landed(a, "x%d_%d" % (kf, c))
+        send(a, [(near, L("xl", 2 * W + 1024 * c, 1024), "x2_%d" % c)])
+
+    def relay_tb(c):
+        a, n = BLOCKS[c]
+        landed(L("tbn", kf * TW + a, n), "tb%d_%d" % (kf, c))
+        send(L("tbn", kf * TW + a, n), [(near, L("lt", a, n), "tb2_%d" % c)])
+
+    def unit(c, i, on_s):
+        a, n = BLOCKS[c]
+        mv(L("gg", W * i + a, n), IND(S("mw", 0, W), L("cor16", 128 * i + a // 16, n // 16)), on_s)
+
+    def finish_block(c):
+        a, n = BLOCKS[c]
+        tt(L("tbo", a, n), B(c, 0, n), L("fli", a, n), add)
+        send(L("tbo", a, n),
+             [(d, L("tbn", slot(rank, d) * TW + a, n), "tb%d_%d" % (slot(rank, d), c)) for d in (far, near)])
+
+    for c, (a, n) in enumerate(BLOCKS):
+        unit(c, 0, True)
+        unit(c, 3, False)
+        unit(c, 1, True)
+        if c > 0:
+            finish_block(c - 1)
+        unit(c, 2, c >= 3)
+        mm(B(c, 0, n), L("sel", 512, 128), L("mw", a, n), True, False)
+        for k, i in enumerate((0, 3, 1, 2)):
+            mm(B(c, 0, n), L("sel", 128 * i, 128), L("gg", W * i + a, n), False, k == 3, k == 3)
+        if c == 2:
+            relay_x(0)
+        if c == 4:
+            relay_tb(0)
+    finish_block(4)
+    send_x(1, (far,))
+    for c in range(1, 5):
+        relay_tb(c)
+    relay_x(1)
+    iota(LAN, [[0, M]], 1, 0, True)
+    for c, (a, n) in enumerate(BLOCKS):
+        landed(L("tbn", kn * TW + a, n), "tb%d_%d" % (kn, c))
+        landed(L("lt", a, n), "tb2_%d" % c)
+    for c in range(2):
+        landed(L("xl", kn * W + 1024 * c, 1024), "x%d_%d" % (kn, c))
+        landed(L("xl", 2 * W + 1024 * c, 1024), "x2_%d" % c)
+
+    def fix(bank, base, terms, lo, hi, inc, src="tt"):
+        n = (hi - lo) // 16
+        for h in range(2):
+            k = 0
+            for e in range(2):
+                for q, w in terms:
+                    end = k == 2 * len(terms) - 1
+                    mm(B(bank, base + h, base + n, 2), L("fx", 320 * h + 160 * w + 16 - 16 * (e - h), 128),
+                       S(src, lo + 16 * e + q, hi, 32), k == 0, end, inc and end and h == 1)
+                    k += 1
+
+    def fix_flows(bank, lo_f, lo_b, src="tt"):
+        fix(bank, 0, [(10, 0)], lo_f, lo_f + 512, False, src)
+        fix(bank, 32, [(12, 0)], lo_b, lo_b + 512, False, src)
+        fix(bank, 64, [(11, 0)], lo_f, lo_f + 512, False, src)
+        fix(bank, 96, [(13, 0)], lo_b, lo_b + 512, True, src)
+
+    def fix_taps(bank, base, inc=True, src="tt"):
+        for i in range(4):
+            fix(bank, base + 64 * i, [(i, 1), (5 + i, 0)], 0, 1024, inc and i == 3, src)
+
+    def position(bank, start, p, lst):
+        tt(S("pf"), B(bank, 0, 128), S(start), add)
+        ts(S(p, 64, 128), S("pf", 64, 128), 0.0, mx, 127.0, mn)
+        ts(S(p, 0, 64), S("pf", 0, 64), 0.0, mx, 255.0, mn)
+        ts(S("cc", 64, 128), S(p, 64, 128), 2, shr)
+        ts(S("cc", 0, 64), S(p, 0, 64), 2, shr)
+        ts(B(bank, 128, 192), S("cc", 64, 128), 64.0, mul)
+        tt(S("pl"), B(bank, 128, 192), S("cc", 0, 64), add)
+        cp(lst, S("pl"))
+
+    def cast(k, c, on_s):
+        mv(L("xf", XA[k] + 1024 * c, 1024), L("xl", k * W + 1024 * c, 1024), on_s)
+
+    rot = [0]
+
+    def shifted(k, src, dst, on_s, banks=(0, 7)):
+        b = banks[rot[0] % 2]
+        rot[0] += 1
+        mm(B(b), CM(5 + k), src, True, True, True)
+        mv(dst, B(b), on_s)
+
+    def shift_x(c, k, on_s=True, banks=(0, 7)):
+        shifted(k, L("xl", 2 * W + M * c, M), L("xf", XA[2 + k] + M * c, M), on_s, banks)
+
+    def shift_t(c, k, on_s=True):
+        shifted(k, L("lt", M * c, M), L("t2", W * k + M * c, M), on_s)
+
+    def gather_near(r):
+        act(S("br"), IND(S("tbo", 0, W if r == 0 else TW), S("nb16", 0, 32) if r == 0 else S("nr16")), ACT.Identity,
+            scale=col("cf", 6), bias=col("cf", 8) if r == 2 else col("mk", 14))
+
+    def P1(r):
+        return "p1%d" % (r % 2)
+
+    def PN(r, k=None):
+        return L("pn16", 64 * (r % 2), 64) if k is None else L("pn16", 64 * (r % 2) + 32 * k, 32)
+
+    act(S("gr", 0, 512), IND(S("tbo", 0, W), S("ms16")), ACT.Copy)
+    ts(S("tj", 32, 64), S("msi"), 63, band)
+    ts(S("tj", 64, 96), S("msi"), 6, shr)
+    for j in range(4):
+        ts(L("home", 32 * j, 32), L("tj", 32 + 32 * (j // 2), 32), 4.0, mul)
+    tr(S("tt", 0, 512), S("gr", 0, 512))
+    fix_flows(2, 0, 0)
+    cast(kn, 0, True)
+    cast(kn, 1, True)
+    for k in range(2):
+        ts(S("pa"), S("ia", 0, 128), (16.0, 112.0)[k], add)
+        ts(S("pe"), S("pa"), 127, band)
+        ts(CM(5 + k), S("pe"), 0.0, ALU.is_equal)
+    position(2, "home", P1(0), PN(0))
+    ms(col("cf", 15), float(TW))
+    ts(S("ti", 0, 32), S("msi"), 1.0, add)
+    ts(S("ti", 96, 128), S("msi"), W - 64, band)
+    ts(S("tj", 0, 32), S("ti", 0, 32), 63, band)
+    ts(col("cf", 12), col("cf", 0), 14.0, ALU.is_lt)
+    tt(S("nbi", 0, 32), S("tj", 0, 32), S("ti", 96, 128), add)
+    tt(col("cf", 6), col("cf", 12), col("cf", 10), sub)
+
+    def rolled(dst, src, k, n=M):
+        (dn_, d0), (sn, s0) = dst, src
+        cuts = ((0, 112, 16), (112, 128, 0)) if k == 0 else ((16, 128, 0), (0, 16, 112))
+        return [(S(dn_, d0, d0 + n, rows=slice(a, b)), S(sn, s0, s0 + n, rows=slice(c, c + b - a))) for a, b, c in cuts]
+
+    for c in range(3):
+        dma("y", rolled(("t2", M * c), ("lt", M * c), 0) + rolled(("t2", W + M * c), ("lt", M * c), 1))
+    ts(S("ti", 32, 64), S("msi"), 64.0, add)
+    ts(S("ti", 64, 96), S("msi"), 63.0, add)
+    ts(S("nbi", 32, 64), S("ti", 32, 64), W - 1, band)
+    ts(S("tj", 64, 96), S("ti", 64, 96), 63, band)
+    ts(col("cf", 8), col("mk", 14), -1.0, mul)
+    tt(S("nbi", 64, 96), S("tj", 64, 96), S("ti", 96, 128), add)
+    ts(S("lj"), S("lj"), col("cf", 0), add)
+    cp(S("nb16"), S("nbi"))
+    for i in range(DI_EARLY, DI_EARLY + 5):
+        ts(L("di", 160 * i, 160), S("dd"), col("mk", i), mul)
+
+    def late_constants(part):
+        if part == 0:
+            ts(S("hom4"), S("home"), 0.4, add)
+            for i in range(DI_EARLY + 5, 16):
+                ts(L("di", 160 * i, 160), S("dd"), col("mk", i), mul)
+            return
+        tt(col("cf", 9), col("cf", 6), col("cf", 8), add)
+        ms(col("cf", 14), 24.5)
+        ts(S("g14"), S("dd"), col("mk", 14), mul, 8192.0, mul)
+        ts(col("cf", 13), col("cf", 14), 4.0 * BIG, mul)
+        ts(CM(0), S("bo"), col("mk", 14), mul, 16.0, mul)
+        ts(CM(1), EYE, col("cf", 6), mul)
+        ts(CM(2), EYE, col("mk", 14), mul)
+        ts(CM(3), EYE, col("cf", 9), mul)
+        ts(CM(4), EYE, col("cf", 8), mul)
+        ts(CM(7), EYE, -1.0, mul)
+
+    def flag_unit(i, k, on_s, to=None):
+        to = i if to is None else to
+        mv(L("gg", 1024 * to + M * k, M), IND(L("tbn", k * TW, TW), L("t116", 64 * i + 32 * k, 32)), on_s)
+
+    def flag_sum(i, k, plus, to):
+        tt(L("gg", 1024 * to + M * k, M), IND(L("tbn", k * TW, TW), L("t116", 64 * i + 32 * k, 32)),
+           L("gg", 1024 * plus + M * k, M), add)
+
+    def flags(i, turn):
+        for j in range(16):
+            mm(B(6, 0, 64), S("g14", 30 - j, 158 - j), S("gg", 1024 * i + j, 1024 * i + 1024, 16),
+               turn == 0 and j == 0, turn == 3 and j == 15, j == 15)
+
+    def tap(k, i):
+        return IND(L("xf", 2 * TW * k, 2 * TW), L("ts16", 64 * i + 32 * k, 32))
+
+    def AA(k, j):
+        return L("aa", M * (2 * k + j), M)
+
+    def DA(k, j):
+        return L("da", M * (2 * k + j), M)
+
+    SA = [L("sa", 0, M), L("sa", M, M)]
+    EA = [L("ea", 0, M), L("ea", M, M)]
+
+    for r in range(3):
+        last = r == 2
+        p1 = P1(r)
+        if r == 0:
+            shift_x(0, 0)
+            shift_x(1, 0)
+            for k in (kn, kf):
+                mv(L("gr", M * k, M), IND(L("tbn", TW * k, W), PN(0, k)), k == kn)
+            cast(kf, 0, True)
+            tr(S("tt"), S("gr"))
+            fix_flows(3, 0, 512)
+            gather_near(0)
+            act(S("gn"), IND(S("tbo", 0, W), S("nb16", 32, 96)), ACT.Copy)
+            late_constants(0)
+            position(3, p1, "p2", S("pl16"))
+            tr(S("tu", 0, 512), S("br"))
+            shift_t(3, 0)
+            shift_t(3, 1, False)
+            fix_taps(4, 64, False)
+            fix(6, 0, [(15, 0)], 0, 1024, True)
+            fix_flows(1, 0, 0, "tu")
+            for k in range(2):
+                mv(L("gr", M * k, M), IND(L("t2", W * k, W), L("pl16", 32 * k, 32)), k == 0)
+            cast(kf, 1, True)
+            tr(S("tt"), S("gr"))
+            fix_taps(5, 0)
+            tr(S("tu"), S("gn"))
+            fix(3, 0, [(4, 1), (9, 0)], 0, 1024, True, "tu")
+            cp(S("t1f"), B(4, 64, 320))
+            tt(S("q2"), S(p1), S("p2"), sub)
+        else:
+            for k in range(2):
+                landed(L("tbn", k * TW + W, M), "st%d_%d" % (r - 1, k))
+            for k in (kn, kf):
+                mv(L("gr", M * k, M), IND(L("tbn", k * TW, TW), L("mp16", 32 * k, 32)), k == kn)
+                if k == kn:
+                    flag_unit(1, kf, True)
+                    flag_unit(0, kn, True)
+            for k in (kn, kf):
+                tr(L("tt", M * k, M), L("gr", M * k, M))
+                fix(3, 32 * k, [(10 + 2 * k, 0)], M * k, M * k + M, False)
+                fix(3, 64 + 32 * k, [(11 + 2 * k, 0)], M * k, M * k + M, True)
+            flag_unit(0, kf, True)
+            if r == 1:
+                position(1, "home", P1(2), PN(2))
+            else:
+                flag_sum(2, kf, 1, 2)
+            flag_unit(1, kn, True, 1 if r == 1 else 2)
+            flags(0, 0)
+            position(3, p1, "p2", S("pl16"))
+            flags(1 if r == 1 else 2, 1)
+            for k in range(2):
+                mv(L("gr", M * k, M), IND(L("t2", W * k, W), L("pl16", 32 * k, 32)), k == 0)
+            flag_unit(2, kn, True, 4)
+            tr(S("tt"), S("gr"))
+            fix_taps(5, 0)
+            tt(S("q2"), S(p1), S("p2"), sub)
+            if r == 1:
+                flag_unit(2, kf, True, 4)
+            else:
+                flag_unit(3, kf, True)
+            flag_sum(3, kn, 4, 3)
+            if r == 1:
+                flag_sum(3, kf, 4, 3)
+            flags(3, 3)
+            if r == 2:
+                tt(S("yea"), B(2), S("yea"), add)
+            for k in (kn, kf):
+                for h in range(2):
+                    landed(L("xf", XA[k] + W + h * M // 2, M // 2), "vl%d_%d_%d" % (r - 1, k, h))
+        act(S("t2f"), B(5, 0, 256), ACT.Identity, bias=col("cf", 15))
+        for i in range(4):
+            tt(B(6, 64 + 64 * i, 128 + 64 * i), B(6, 0, 64), L("t1f", 64 * i, 64), add)
+        ts(S("ok"), B(6, 0, 64), 0.0, ALU.is_equal)
+        tt(S("tsf"), B(6, 64, 320), S("t2f"), mn)
+        tt(B(6, 320, 384), S("q2", 0, 64), S("ok"), mul)
+        cp(S("ts16"), S("tsf"))
+        if r == 0:
+            shift_x(2, 0, True, (0, 7))
+            shift_x(3, 0, True, (0, 7))
+        for j in range(2):
+            act(AA(0, j), tap(0, 2 * j), ACT.Copy)
+        tt(B(6, 384, 448), S("q2", 64, 128), S("ok"), mul)
+        ts(S("fh"), S("ok"), 0.5, mul, 0.5, add)
+        tt(S("pe"), B(6, 320, 448), S("p2"), add)
+        ts(S("pa"), S("pe"), 3, band)
+        tt(B(6, 64, 192), S("pe"), S("hom4"), sub)
+        ts(S("uv"), S("pa"), 0.25, mul, TINY, mx)
+        if r == 0:
+            position(1, "home", P1(1), PN(1))
+            tt(S("nbm", 0, 32), B(3, 0, 32), S("lj"), sub)
+            tt(S("nbm", 32, 64), B(3, 32, 64), S("lj"), sub)
+            late_constants(1)
+        for b, a in ((0, 0), (1, 64), (2, 32), (3, 96)):
+            for i in range(16):
+                mm(B(b, i, 512, 16), L("boi", 128 * i, 128), L("uv", a, 32), True, True, i == 15)
+            if r == 0 and b == 1:
+                for c in range(4):
+                    shift_x(c, 1, True, (5, 7))
+        if r > 0:
+            for k in (1, 3):
+                act(L("xf", XA[k] + W, M), L("xf", XA[k] + W, M), ACT.Abs)
+        act(AA(1, 0), tap(1, 0), ACT.Copy)
+        act(DA(1, 0), tap(1, 1), ACT.Copy)
+        act(B(7), DA(1, 0), ACT.Copy)
+        act(AA(1, 1), tap(1, 2), ACT.Copy)
+        act(DA(1, 1), tap(1, 3), ACT.Copy)
+        tt(DA(0, 0), tap(0, 1), AA(0, 0), sub)
+        tt(S("q1", 0, 64), B(6, 64, 128), S("fh"), mul)
+        tt(S("q1", 64, 128), B(6, 128, 192), S("fh"), mul)
+        tt(DA(0, 1), tap(0, 3), AA(0, 1), sub)
+        ts(S("own"), S("q1"), MAGIC, add, -MAGIC, add)
+        mm(B(5), CM(7), S("br"), True, False)
+        for i in range(16):
+            for j, q in enumerate((10, 12, 11, 13)):
+                end = i == 15 and j == 3
+                mm(B(5, i, 512, 16), L("di", 160 * i + 16 - (q - i), 128), L("own", 32 * j, 32), False, end, end)
+        tt(B(4), B(0), DA(0, 0), mul)
+        tt(B(0), B(0), DA(0, 1), mul)
+        tt(SA[0], B(4), AA(0, 0), add)
+        act(B(4), DA(1, 1), ACT.Copy)
+        if not last:
+            keys = S("xf")[1] + S("lv")[1] + ([("tbn", W, TW), ("tbn", TW + W, 2 * TW)] if r else [])
+            credit(keys, [near] if r == 0 else [near, far, op], r)
+        tt(B(0), B(0), AA(0, 1), add)
+        tt(EA[0], B(0), SA[0], sub)
+        mm(B(6), CM(3 if last else 1), S("br"), True, False)
+        mm(B(6), CM(4 if last else 2), LAN, False, True, True)
+        if last:
+            act(S("old0"), S("val"), ACT.Relu)
+        else:
+            for k in range(2):
+                act(L("gn", M * k, M), IND(L("tbn", TW * k, W), PN(r + 1, k)), ACT.Copy)
+        tt(DA(1, 0), B(7), AA(1, 0), sub)
+        tt(B(1), B(1), EA[0], mul)
+        tt(B(0), B(2), DA(1, 0), mul)
+        tt(S("zf"), B(1), SA[0], add)
+        tt(DA(1, 1), B(4), AA(1, 1), sub)
+        tt(SA[1], B(0), AA(1, 0), add)
+        tt(B(2), B(2), DA(1, 1), mul)
+        if last:
+            mm(B(4), L("boi", 128 * 14, 128), LAN, True, True, True)
+        H = M // 2
+        for a in (0, H):
+            tt(B(2, a, a + H), B(2, a, a + H), L("aa", 3 * M + a, H), add)
+        for a in (0, H):
+            tt(L("ea", M + a, H), B(2, a, a + H), L("sa", M + a, H), sub)
+        for a in (0, H):
+            tt(B(3, a, a + H), B(3, a, a + H), L("ea", M + a, H), mul)
+        for a in (0, H):
+            tt(B(3, a, a + H), B(3, a, a + H), L("sa", M + a, H), add)
+        for a in (0, H):
+            tt(L("dif", a, H), L("zf", a, H), B(3, a, a + H), sub)
+            act(L("gap", a, H), L("dif", a, H), ACT.Abs)
+        act(S("half"), S("dif"), ACT.Copy, scale=0.5)
+        act(S("ex") if last else B(2), S("gap"), ACT.Exp, scale=-1.0)
+        CB = {0: B(7, 0, H), H: B(1, 0, H)}
+        for a in (0, H):
+            mm(CB[a], CM(0), L("tbo", W + a, H), True, False)
+        for a in (0, H):
+            ts(L("cmpb", a, H), L("gap", a, H), col("epsc", 0), ALU.is_le)
+            mm(CB[a], S("bo"), L("cmpb", a, H), False, True, True)
+        for a in (0, H):
+            ts(L("won", a, H), CB[a], 25.0, ALU.is_ge)
+        if last:
+            tt(B(0), B(3), S("half"), add)
+            tt(B(4), B(4), S("ex"), mul)
+            tt(B(0), B(0), S("won"), mul)
+            tt(S("yea"), B(4), S("yea"), add)
+            dma("s", [((T.ye[:], []), S("yea"))])
+            tt(S("yo"), B(0), S("old0"), add)
+            dma("y", [((T.y[:], []), S("yo"))])
+            for a in (0, H):
+                tt(L("tw", a, H), B(5, a, a + H), L("won", a, H), mul)
+            for a in (0, H):
+                tt(L("newf", a, H), B(6, a, a + H), L("tw", a, H), add)
+            for q, rows in (("s", (0, 1, 2)), ("y", (3, 4))):
+                dma(q, [((T.yf[8 * j:8 * j + 8, :], []), S("newf", rows=slice(10 + j, 128, 16))) for j in rows])
+            break
+        for a in (0, H):
+            act(L("pen", a, H), CB[a], ACT.Relu, scale=-4.0 * BIG, bias=col("cf", 13))
+        for a in (0, H):
+            tt(L("tw", a, H), B(5, a, a + H), L("won", a, H), mul)
+        for a in (0, H):
+            tt(L("tbo", W + a, H), B(6, a, a + H), L("tw", a, H), add)
+        send(LAN, [(d, L("tbn", slot(rank, d) * TW + W, M), "st%d_%d" % (r, slot(rank, d))) for d in (far, near)],
+             [cr(r, near), cr(r, far)] if r else [])
+        tr(S("tt", 0, 512), LAN)
+        fix(5, 0, [(14, 0)], 0, 512, True)
+        tr(S("tu"), S("gn"))
+        fix(4, 0, [(4, 1), (9, 0)], 0, 1024, False, "tu")
+        fix_taps(4, 64, True, "tu")
+        tt(S("nt", 0, 32), B(5, 0, 32), L("nbm", 32 * r, 32), mul)
+        tt(B(0, 0, H), B(3, 0, H), L("half", 0, H), add)
+        tt(S("nt", 32, 64), S("nt", 0, 32), S("lj"), add)
+        tt(B(0, H, M), B(3, H, M), L("half", H, H), add)
+        cp(S("nr16"), S("nt", 32, 64))
+        gather_near(r + 1)
+        tt(B(0, 0, H), B(0, 0, H), L("pen", 0, H), sub)
+        tt(B(0, H, M), B(0, H, M), L("pen", H, H), sub)
+        cp(S("mp16"), B(4, 0, 64))
+        cp(S("t116"), B(4, 64, 320))
+        for h, a in enumerate((0, H)):
+            tt(L("val", a, H), B(0, a, a + H), L("val", a, H), mx)
+            send(L("val", a, H),
+                 [(op, L("lv", a, H), "vl%d_2_%d" % (r, h)),
+                  (near, L("xf", XA[slot(rank, near)] + W + a, H), "vl%d_%d_%d" % (r, slot(rank, near), h))],
+                 [cr(r, near), cr(r, op)] if r else [cr(r, near)])
+        for h, a in enumerate((0, H)):
+            landed(L("lv", a, H), "vl%d_2_%d" % (r, h))
+            send(L("lv", a, H), [(near, L("xf", XA[slot(op, near)] + W + a, H), "vl%d_%d_%d" % (r, slot(op, near), h))])
+            dma("y", rolled(("xf", XA[2] + W + a), ("lv", a), 0, H) + rolled(("xf", XA[3] + W + a), ("lv", a), 1, H))
+        cp(S("t1f"), B(4, 64, 320))
+        if r == 0:
+            tr(S("tu", 0, 512), S("br"))
+            fix_flows(1, 0, 0, "tu")
+            tt(S("yea"), B(2), S("won"), mul)
+        else:
+            tt(B(2), B(2), S("won"), mul)
+
+    for sem in ("v", "s", "p", "gp"):
+        wait("g", (sem, cnt[sem]))
+    for sem, val in owed.items():
+        wait("g", (sem, val))
+
+
+DI_EARLY = 5
+BLOCKS = [(0, 512), (512, 512), (1024, 512), (1536, 256), (1792, 256)]

@@ -17,7 +17,7 @@ SCRATCH = {
     "msi": _sb(32, I32), "cori": _sb(512, I32), "epsc": _sb(4, F32), "fli": _sb(W, I32), "xo": _sb(W, BF),
     "ms16": _sb(32, U16), "cor16": _sb(512, U16), "mw": _sb(TW, BF), "gg": _sb(8192, BF),
     "tbo": _sb(TW, BF), "tbn": _sb(2 * TW, BF), "lt": _sb(W, BF), "t2": _sb(2 * W, BF),
-    "xl": _sb(3 * W, BF), "xf": _sb(4 * TW, F32), "lv": _sb(M, F32),
+    "xl": _sb(3 * W, BF), "xf": _sb(4 * TW + 8, F32), "dn": _sb(32, F32), "eyef": _sb(128, F32), "lv": _sb(M, F32),
     "ip": _sb(4, I32), "ia": _sb(160, I32), "ir": _sb(64, F32), "ig": _sb(128, F32), "lj": _sb(32, F32),
     "ci": _sb(8, I32), "cf": _sb(32, F32), "mk": _sb(16, F32), "hc": _sb(48, BF), "sm": _sb(8, F32),
     "dd": _sb(160, BF), "sel": _sb(5 * 128, BF), "fx": _sb(4 * 160, BF), "g14": _sb(160, BF), "bo": _sb(128, BF),
@@ -27,7 +27,7 @@ SCRATCH = {
     "pf": _sb(128, F32), "p10": _sb(128, I32), "p11": _sb(128, I32), "p2": _sb(128, I32),
     "cc": _sb(128, I32), "pl": _sb(64, I32), "pm": _sb(64, I32), "pl16": _sb(64, U16), "pn16": _sb(128, U16),
     "mp16": _sb(64, U16), "t1f": _sb(256, F32), "t116": _sb(256, U16), "t2f": _sb(256, F32), "tsf": _sb(256, F32),
-    "ts16": _sb(256, U16), "ok": _sb(64, F32), "fh": _sb(64, F32), "q1": _sb(128, F32), "q2": _sb(128, F32),
+    "ts16": _sb(256, U16), "ok": _sb(64, F32), "fh": _sb(64, F32), "fi": _sb(64, F32), "q1": _sb(128, F32), "q2": _sb(128, F32),
     "pe": _sb(128, I32), "pa": _sb(128, I32), "uv": _sb(128, BF), "own": _sb(128, BF), "nt": _sb(64, F32),
     "br": _sb(M, BF), "dif": _sb(M, F32), "gap": _sb(M, F32), "cmpb": _sb(M, BF), "half": _sb(M, F32),
     "won": _sb(M, F32), "tw": _sb(M, F32), "pen": _sb(M, F32), "val": _sb(M, F32), "ex": _sb(M, F32),
@@ -37,9 +37,9 @@ SCRATCH = {
 for _b in range(8):
     SCRATCH["b%d" % _b] = ("psum", [128, 512], F32)
 
-SEMAPHORES = (["v", "s", "p", "gp"] + ["d%d" % i for i in range(24)] + ["l%d" % i for i in range(36)]
+SEMAPHORES = (["v", "s", "p", "gp"] + ["d%d" % i for i in range(24)] + ["l%d" % i for i in range(40)]
               + ["tb%d_%d" % (a, c) for a in range(3) for c in range(5)]
-              + ["x%d_%d" % (a, c) for a in range(3) for c in range(2)]
+              + ["x%d_%d" % (a, c) for a in range(3) for c in range(3)]
               + ["st%d_%d" % (r, a) for r in range(2) for a in range(2)]
               + ["vl%d_%d_%d" % (r, a, h) for r in range(2) for a in range(3) for h in range(2)]
               + ["cr%d_%d" % (r, a) for r in range(2) for a in range(3)])
@@ -106,7 +106,7 @@ def rank_program(g, core, T, topo):
         need = {}
         for keys, isw in ((reads, False), (writes, True)):
             for (n, lo, hi) in keys:
-                ps = SCRATCH[n][0] == "psum"
+                ps = n in SCRATCH and SCRATCH[n][0] == "psum"
                 for (a, b, w, tok) in recs.get(n, []):
                     same = eng is not None and tok[2] == eng
                     if same and eng == "p":
@@ -193,7 +193,7 @@ def rank_program(g, core, T, topo):
                 note(a, b, ("p", cnt["p"], "p"))
             del pend[:]
 
-    def dma(q, pairs):
+    def dma(q, pairs, **kw):
         sem = "d%d" % nxt["d"]
         nxt["d"] += 1
         rd, wr = [], []
@@ -202,7 +202,7 @@ def rank_program(g, core, T, topo):
             wr += o[1]
         deps(q, None, rd, wr)
         for o, i in pairs:
-            Q[q].dma_start(o[0], i[0]).then_inc(T.sem[sem], 16)
+            Q[q].dma_start(o[0], i[0], **kw).then_inc(T.sem[sem], 16)
         owed[sem] = 16 * len(pairs)
         note(rd, wr, (sem, 16 * len(pairs), None))
 
@@ -250,7 +250,8 @@ def rank_program(g, core, T, topo):
     band, shr = ALU.bitwise_and, ALU.arith_shift_right
     EYE = S("dd", 16, 144)
     LAN = S("tbo", W, TW)
-    XA = [0, 2 * TW, TW, 3 * TW]
+    FW = 2 * TW + 8
+    XA = [0, FW, TW, FW + TW]
     kn, kf = slot(near, rank), slot(far, rank)
 
     dma("y", [(S("msi"), (T.ms[:], []))])
@@ -271,16 +272,16 @@ def rank_program(g, core, T, topo):
     dma("y", [(col("epsc", 0), (T.eps[:], []))])
     for j in range(8):
         act(L("val", 64 * j, 64), S("ir"), ACT.Identity, scale=0.0, bias=-BIG)
-    act(S("pen"), S("val"), ACT.Abs)
+    act(L("xf", 2 * TW, 8), L("val", 0, 8), ACT.Copy)
 
-    def send_x(c, dests):
-        send(L("xo", 1024 * c, 1024),
-             [(d, L("xl", slot(rank, d) * W + 1024 * c, 1024), "x%d_%d" % (slot(rank, d), c)) for d in dests])
+    def send_x(c, dests, n=None):
+        a, n = XB[c][0], n or XB[c][1]
+        send(L("xo", a, n), [(d, L("xl", slot(rank, d) * W + a, n), "x%d_%d" % (slot(rank, d), c)) for d in dests])
 
     send_x(0, (far, near))
-    send_x(1, (near,))
+    send_x(1, (near,), 1024)
     load_flows(1)
-    dma("y", [(L("xf", XA[k] + W, M), S("pen" if k % 2 else "val")) for k in range(4)])
+    dma("y", [(L("xf", XA[k] + W, M), S("val")) for k in range(4)])
     iota(S("lj"), [[16, 32]], W, 0, True)
 
     ts(col("ci", 0), col("ip", 0), 15, band)
@@ -325,9 +326,9 @@ def rank_program(g, core, T, topo):
     cp(S("cor16", 128, 512), S("cori", 128, 512))
 
     def relay_x(c):
-        a = L("xl", kf * W + 1024 * c, 1024)
-        landed(a, "x%d_%d" % (kf, c))
-        send(a, [(near, L("xl", 2 * W + 1024 * c, 1024), "x2_%d" % c)])
+        a, n = XB[c]
+        landed(L("xl", kf * W + a, n), "x%d_%d" % (kf, c))
+        send(L("xl", kf * W + a, n), [(near, L("xl", 2 * W + a, n), "x2_%d" % c)])
 
     def relay_tb(c):
         a, n = BLOCKS[c]
@@ -356,20 +357,23 @@ def rank_program(g, core, T, topo):
             mm(B(c, 0, n), L("sel", 128 * i, 128), L("gg", W * i + a, n), False, k == 3, k == 3)
         if c == 2:
             relay_x(0)
-        if c == 4:
-            relay_tb(0)
     finish_block(4)
+    relay_tb(0)
+    relay_tb(1)
     send_x(1, (far,))
-    for c in range(1, 5):
+    send_x(2, (far,))
+    for c in range(2, 5):
         relay_tb(c)
     relay_x(1)
+    relay_x(2)
     iota(LAN, [[0, M]], 1, 0, True)
     for c, (a, n) in enumerate(BLOCKS):
         landed(L("tbn", kn * TW + a, n), "tb%d_%d" % (kn, c))
         landed(L("lt", a, n), "tb2_%d" % c)
     for c in range(2):
         landed(L("xl", kn * W + 1024 * c, 1024), "x%d_%d" % (kn, c))
-        landed(L("xl", 2 * W + 1024 * c, 1024), "x2_%d" % c)
+    for c, (a, n) in enumerate(XB):
+        landed(L("xl", 2 * W + a, n), "x2_%d" % c)
 
     def fix(bank, base, terms, lo, hi, inc, src="tt"):
         n = (hi - lo) // 16
@@ -385,8 +389,8 @@ def rank_program(g, core, T, topo):
     def fix_flows(bank, lo_f, lo_b, src="tt"):
         fix(bank, 0, [(10, 0)], lo_f, lo_f + 512, False, src)
         fix(bank, 32, [(12, 0)], lo_b, lo_b + 512, False, src)
-        fix(bank, 64, [(11, 0)], lo_f, lo_f + 512, False, src)
-        fix(bank, 96, [(13, 0)], lo_b, lo_b + 512, True, src)
+        fix(bank, 64, [(11, 1)], lo_f, lo_f + 512, False, src)
+        fix(bank, 96, [(13, 1)], lo_b, lo_b + 512, True, src)
 
     def fix_taps(bank, base, inc=True, src="tt"):
         for i in range(4):
@@ -394,12 +398,11 @@ def rank_program(g, core, T, topo):
 
     def position(bank, start, p, lst):
         tt(S("pf"), B(bank, 0, 128), S(start), add)
-        ts(S(p, 64, 128), S("pf", 64, 128), 0.0, mx, 127.0, mn)
+        ts(S(p, 64, 128), S("pf", 64, 128), 0.0, mx, 127.0 * 64, mn)
         ts(S(p, 0, 64), S("pf", 0, 64), 0.0, mx, 255.0, mn)
-        ts(S("cc", 64, 128), S(p, 64, 128), 2, shr)
+        ts(S("cc", 64, 128), S(p, 64, 128), 2, shr, W - 64, band)
         ts(S("cc", 0, 64), S(p, 0, 64), 2, shr)
-        ts(B(bank, 128, 192), S("cc", 64, 128), 64.0, mul)
-        tt(S("pl"), B(bank, 128, 192), S("cc", 0, 64), add)
+        tt(S("pl"), S("cc", 64, 128), S("cc", 0, 64), add)
         cp(lst, S("pl"))
 
     def cast(k, c, on_s):
@@ -430,10 +433,18 @@ def rank_program(g, core, T, topo):
         return L("pn16", 64 * (r % 2), 64) if k is None else L("pn16", 64 * (r % 2) + 32 * k, 32)
 
     act(S("gr", 0, 512), IND(S("tbo", 0, W), S("ms16")), ACT.Copy)
+    ts(S("ti", 0, 32), S("msi"), 1.0, add)
+    ts(S("ti", 96, 128), S("msi"), W - 64, band)
+    ts(S("tj", 0, 32), S("ti", 0, 32), 63, band)
+    ts(col("cf", 12), col("cf", 0), 14.0, ALU.is_lt)
+    tt(S("nbi", 0, 32), S("tj", 0, 32), S("ti", 96, 128), add)
+    tt(col("cf", 6), col("cf", 12), col("cf", 10), sub)
+    cp(S("nb16", 0, 32), S("nbi", 0, 32))
+    gather_near(0)
     ts(S("tj", 32, 64), S("msi"), 63, band)
     ts(S("tj", 64, 96), S("msi"), 6, shr)
     for j in range(4):
-        ts(L("home", 32 * j, 32), L("tj", 32 + 32 * (j // 2), 32), 4.0, mul)
+        ts(L("home", 32 * j, 32), L("tj", 32 + 32 * (j // 2), 32), (4.0, 256.0)[j // 2], mul)
     tr(S("tt", 0, 512), S("gr", 0, 512))
     fix_flows(2, 0, 0)
     cast(kn, 0, True)
@@ -442,14 +453,10 @@ def rank_program(g, core, T, topo):
         ts(S("pa"), S("ia", 0, 128), (16.0, 112.0)[k], add)
         ts(S("pe"), S("pa"), 127, band)
         ts(CM(5 + k), S("pe"), 0.0, ALU.is_equal)
+    tr(S("tu", 0, 512), S("br"))
+    fix_flows(1, 0, 0, "tu")
     position(2, "home", P1(0), PN(0))
     ms(col("cf", 15), float(TW))
-    ts(S("ti", 0, 32), S("msi"), 1.0, add)
-    ts(S("ti", 96, 128), S("msi"), W - 64, band)
-    ts(S("tj", 0, 32), S("ti", 0, 32), 63, band)
-    ts(col("cf", 12), col("cf", 0), 14.0, ALU.is_lt)
-    tt(S("nbi", 0, 32), S("tj", 0, 32), S("ti", 96, 128), add)
-    tt(col("cf", 6), col("cf", 12), col("cf", 10), sub)
 
     def rolled(dst, src, k, n=M):
         (dn_, d0), (sn, s0) = dst, src
@@ -465,13 +472,15 @@ def rank_program(g, core, T, topo):
     ts(col("cf", 8), col("mk", 14), -1.0, mul)
     tt(S("nbi", 64, 96), S("tj", 64, 96), S("ti", 96, 128), add)
     ts(S("lj"), S("lj"), col("cf", 0), add)
-    cp(S("nb16"), S("nbi"))
+    cp(S("nb16", 32, 96), S("nbi", 32, 96))
+    position(1, "home", P1(1), PN(1))
     for i in range(DI_EARLY, DI_EARLY + 5):
         ts(L("di", 160 * i, 160), S("dd"), col("mk", i), mul)
 
     def late_constants(part):
         if part == 0:
-            ts(S("hom4"), S("home"), 0.4, add)
+            ts(S("hom4", 0, 64), S("home", 0, 64), 0.375, add)
+            ts(S("hom4", 64, 128), S("home", 64, 128), 24.0, add)
             for i in range(DI_EARLY + 5, 16):
                 ts(L("di", 160 * i, 160), S("dd"), col("mk", i), mul)
             return
@@ -499,8 +508,14 @@ def rank_program(g, core, T, topo):
             mm(B(6, 0, 64), S("g14", 30 - j, 158 - j), S("gg", 1024 * i + j, 1024 * i + 1024, 16),
                turn == 0 and j == 0, turn == 3 and j == 15, j == 15)
 
+    def own_rows(b):
+        for i in range(16):
+            for j, q in enumerate((10, 12, 11, 13)):
+                end = i == 15 and j == 3
+                mm(B(b, i, 512, 16), L("di", 160 * i + 16 - (q - i), 128), L("own", 32 * j, 32), False, end, end)
+
     def tap(k, i):
-        return IND(L("xf", 2 * TW * k, 2 * TW), L("ts16", 64 * i + 32 * k, 32))
+        return IND(L("xf", FW * k, FW - 8 * k), L("ts16", 64 * i + 32 * k, 32))
 
     def AA(k, j):
         return L("aa", M * (2 * k + j), M)
@@ -508,6 +523,7 @@ def rank_program(g, core, T, topo):
     def DA(k, j):
         return L("da", M * (2 * k + j), M)
 
+    H = M // 2
     SA = [L("sa", 0, M), L("sa", M, M)]
     EA = [L("ea", 0, M), L("ea", M, M)]
 
@@ -516,24 +532,24 @@ def rank_program(g, core, T, topo):
         p1 = P1(r)
         if r == 0:
             shift_x(0, 0)
-            shift_x(1, 0)
             for k in (kn, kf):
                 mv(L("gr", M * k, M), IND(L("tbn", TW * k, W), PN(0, k)), k == kn)
-            cast(kf, 0, True)
+            shift_x(1, 0)
+            act(S("gn"), IND(S("tbo", 0, W), S("nb16", 32, 96)), ACT.Copy)
             tr(S("tt"), S("gr"))
             fix_flows(3, 0, 512)
-            gather_near(0)
-            act(S("gn"), IND(S("tbo", 0, W), S("nb16", 32, 96)), ACT.Copy)
             late_constants(0)
             position(3, p1, "p2", S("pl16"))
-            tr(S("tu", 0, 512), S("br"))
+            late_constants(1)
             shift_t(3, 0)
             shift_t(3, 1, False)
+            cast(kf, 0, True)
             fix_taps(4, 64, False)
             fix(6, 0, [(15, 0)], 0, 1024, True)
-            fix_flows(1, 0, 0, "tu")
             for k in range(2):
                 mv(L("gr", M * k, M), IND(L("t2", W * k, W), L("pl16", 32 * k, 32)), k == 0)
+            shift_x(2, 0, True, (0, 7))
+            shift_x(0, 1, True, (0, 7))
             cast(kf, 1, True)
             tr(S("tt"), S("gr"))
             fix_taps(5, 0)
@@ -552,31 +568,25 @@ def rank_program(g, core, T, topo):
             for k in (kn, kf):
                 tr(L("tt", M * k, M), L("gr", M * k, M))
                 fix(3, 32 * k, [(10 + 2 * k, 0)], M * k, M * k + M, False)
-                fix(3, 64 + 32 * k, [(11 + 2 * k, 0)], M * k, M * k + M, True)
+                fix(3, 64 + 32 * k, [(11 + 2 * k, 1)], M * k, M * k + M, True)
             flag_unit(0, kf, True)
-            if r == 1:
-                position(1, "home", P1(2), PN(2))
-            else:
-                flag_sum(2, kf, 1, 2)
-            flag_unit(1, kn, True, 1 if r == 1 else 2)
+            flag_sum(2, kf, 1, 2)
+            flag_unit(1, kn, True, 2)
             flags(0, 0)
             position(3, p1, "p2", S("pl16"))
-            flags(1 if r == 1 else 2, 1)
+            flags(2, 1)
             for k in range(2):
                 mv(L("gr", M * k, M), IND(L("t2", W * k, W), L("pl16", 32 * k, 32)), k == 0)
             flag_unit(2, kn, True, 4)
             tr(S("tt"), S("gr"))
             fix_taps(5, 0)
             tt(S("q2"), S(p1), S("p2"), sub)
-            if r == 1:
-                flag_unit(2, kf, True, 4)
-            else:
-                flag_unit(3, kf, True)
+            flag_unit(3, kf, True)
             flag_sum(3, kn, 4, 3)
-            if r == 1:
-                flag_sum(3, kf, 4, 3)
             flags(3, 3)
-            if r == 2:
+            if r == 1:
+                position(1, "home", P1(2), PN(2))
+            else:
                 tt(S("yea"), B(2), S("yea"), add)
             for k in (kn, kf):
                 for h in range(2):
@@ -587,132 +597,161 @@ def rank_program(g, core, T, topo):
         ts(S("ok"), B(6, 0, 64), 0.0, ALU.is_equal)
         tt(S("tsf"), B(6, 64, 320), S("t2f"), mn)
         tt(B(6, 320, 384), S("q2", 0, 64), S("ok"), mul)
+        if last:
+            tt(S("tsf", 0, 32), S("tsf", 0, 32), S("dn"), mx)
         cp(S("ts16"), S("tsf"))
         if r == 0:
-            shift_x(2, 0, True, (0, 7))
             shift_x(3, 0, True, (0, 7))
         for j in range(2):
             act(AA(0, j), tap(0, 2 * j), ACT.Copy)
+        if r == 0:
+            for c in (1, 2):
+                shift_x(c, 1, True, (5, 7))
         tt(B(6, 384, 448), S("q2", 64, 128), S("ok"), mul)
         ts(S("fh"), S("ok"), 0.5, mul, 0.5, add)
         tt(S("pe"), B(6, 320, 448), S("p2"), add)
-        ts(S("pa"), S("pe"), 3, band)
+        ts(S("fi"), S("ok"), 0.5 / 64, mul, 0.5 / 64, add)
+        ts(S("pa", 0, 64), S("pe", 0, 64), 3, band)
+        ts(S("pa", 64, 128), S("pe", 64, 128), 6, shr, 3, band)
+        ts(S("uv", 0, 64), S("pa", 0, 64), 0.25, mul, TINY, mx)
+        ts(S("uv", 64, 128), S("pa", 64, 128), 0.25, mul, TINY, mx)
         tt(B(6, 64, 192), S("pe"), S("hom4"), sub)
-        ts(S("uv"), S("pa"), 0.25, mul, TINY, mx)
         if r == 0:
-            position(1, "home", P1(1), PN(1))
             tt(S("nbm", 0, 32), B(3, 0, 32), S("lj"), sub)
             tt(S("nbm", 32, 64), B(3, 32, 64), S("lj"), sub)
-            late_constants(1)
         for b, a in ((0, 0), (1, 64), (2, 32), (3, 96)):
             for i in range(16):
                 mm(B(b, i, 512, 16), L("boi", 128 * i, 128), L("uv", a, 32), True, True, i == 15)
             if r == 0 and b == 1:
-                for c in range(4):
-                    shift_x(c, 1, True, (5, 7))
-        if r > 0:
-            for k in (1, 3):
-                act(L("xf", XA[k] + W, M), L("xf", XA[k] + W, M), ACT.Abs)
-        act(AA(1, 0), tap(1, 0), ACT.Copy)
-        act(DA(1, 0), tap(1, 1), ACT.Copy)
-        act(B(7), DA(1, 0), ACT.Copy)
-        act(AA(1, 1), tap(1, 2), ACT.Copy)
-        act(DA(1, 1), tap(1, 3), ACT.Copy)
+                shift_x(3, 1, True, (5, 7))
+        act(AA(1, 0), tap(1, 0), ACT.Abs)
+        act(DA(1, 0), tap(1, 1), ACT.Abs)
         tt(DA(0, 0), tap(0, 1), AA(0, 0), sub)
         tt(S("q1", 0, 64), B(6, 64, 128), S("fh"), mul)
-        tt(S("q1", 64, 128), B(6, 128, 192), S("fh"), mul)
+        tt(S("q1", 64, 128), B(6, 128, 192), S("fi"), mul)
         tt(DA(0, 1), tap(0, 3), AA(0, 1), sub)
-        ts(S("own"), S("q1"), MAGIC, add, -MAGIC, add)
-        mm(B(5), CM(7), S("br"), True, False)
-        for i in range(16):
-            for j, q in enumerate((10, 12, 11, 13)):
-                end = i == 15 and j == 3
-                mm(B(5, i, 512, 16), L("di", 160 * i + 16 - (q - i), 128), L("own", 32 * j, 32), False, end, end)
         tt(B(4), B(0), DA(0, 0), mul)
-        tt(B(0), B(0), DA(0, 1), mul)
+        ts(S("own"), S("q1"), MAGIC, add, -MAGIC, add)
+        act(B(7), DA(1, 0), ACT.Copy)
         tt(SA[0], B(4), AA(0, 0), add)
+        act(AA(1, 1), tap(1, 2), ACT.Abs)
+        act(DA(1, 1), tap(1, 3), ACT.Abs)
+        mm(B(5), CM(7), S("br"), True, False)
+        own_rows(5)
+        for a in (0, H):
+            tt(B(0, a, a + H), B(0, a, a + H), L("da", M + a, H), mul)
         act(B(4), DA(1, 1), ACT.Copy)
         if not last:
             keys = S("xf")[1] + S("lv")[1] + ([("tbn", W, TW), ("tbn", TW + W, 2 * TW)] if r else [])
             credit(keys, [near] if r == 0 else [near, far, op], r)
-        tt(B(0), B(0), AA(0, 1), add)
-        tt(EA[0], B(0), SA[0], sub)
+        for a in (0, H):
+            tt(B(0, a, a + H), B(0, a, a + H), L("aa", M + a, H), add)
+        for a in (0, H):
+            tt(L("ea", a, H), B(0, a, a + H), L("sa", a, H), sub)
         mm(B(6), CM(3 if last else 1), S("br"), True, False)
         mm(B(6), CM(4 if last else 2), LAN, False, True, True)
         if last:
             act(S("old0"), S("val"), ACT.Relu)
+            act(S("eyef"), EYE, ACT.Copy)
         else:
             for k in range(2):
                 act(L("gn", M * k, M), IND(L("tbn", TW * k, W), PN(r + 1, k)), ACT.Copy)
+        tt(B(1, 0, H), B(1, 0, H), L("ea", 0, H), mul)
         tt(DA(1, 0), B(7), AA(1, 0), sub)
-        tt(B(1), B(1), EA[0], mul)
-        tt(B(0), B(2), DA(1, 0), mul)
-        tt(S("zf"), B(1), SA[0], add)
-        tt(DA(1, 1), B(4), AA(1, 1), sub)
-        tt(SA[1], B(0), AA(1, 0), add)
-        tt(B(2), B(2), DA(1, 1), mul)
+        tt(B(1, H, M), B(1, H, M), L("ea", H, H), mul)
+        for a in (0, H):
+            tt(B(0, a, a + H), B(2, a, a + H), L("da", 2 * M + a, H), mul)
+        CB = {0: B(7, 0, H), H: B(4, 0, H)}
+
+        def PB(b, a):
+            return B(b, a, a + H)
+
+        def step(name, a):
+            if name == "zf":
+                tt(L("zf", a, H), PB(1, a), L("sa", a, H), add)
+            elif name == "s":
+                tt(L("sa", M + a, H), PB(0, a), L("aa", 2 * M + a, H), add)
+            elif name == "d":
+                tt(L("da", 3 * M + a, H), PB(4, a), L("aa", 3 * M + a, H), sub)
+                if a:
+                    for c in (0, H):
+                        mm(CB[c], CM(0), L("tbo", W + c, H), True, False)
+                    if last:
+                        mm(B(1), S("eyef"), S("yea"), True, False)
+            elif name == "m":
+                tt(PB(2, a), PB(2, a), L("da", 3 * M + a, H), mul)
+            elif name == "t":
+                tt(PB(2, a), PB(2, a), L("aa", 3 * M + a, H), add)
+            elif name == "e":
+                tt(L("ea", M + a, H), PB(2, a), L("sa", M + a, H), sub)
+            elif name == "mz":
+                tt(PB(3, a), PB(3, a), L("ea", M + a, H), mul)
+            elif name == "z":
+                tt(PB(3, a), PB(3, a), L("sa", M + a, H), add)
+            elif name == "dif":
+                tt(L("dif", a, H), L("zf", a, H), PB(3, a), sub)
+                act(L("gap", a, H), L("dif", a, H), ACT.Abs)
+            elif name == "cmp":
+                ts(L("cmpb", a, H), L("gap", a, H), col("epsc", 0), ALU.is_le)
+                mm(CB[a], S("bo"), L("cmpb", a, H), False, True, True)
+            elif name == "won":
+                ts(L("won", a, H), CB[a], 25.0, ALU.is_ge)
+            elif name == "hf":
+                act(L("half", a, H), L("dif", a, H), ACT.Copy, scale=0.5)
+            elif name == "tg":
+                tr(L("tu", 2 * a, M), L("gn", 2 * a, M))
+            elif name == "ex":
+                act(L("ex", a, H), L("gap", a, H), ACT.Exp, scale=-1.0)
+                mm(PB(1, a), S("eyef"), L("ex", a, H), False, a > 0, True)
+            elif name == "hv":
+                tt(PB(0, a), PB(3, a), L("half", a, H), add)
+            elif name == "tw":
+                tt(L("tw", a, H), PB(5, a), L("won", a, H), mul)
+            elif name == "new" and last:
+                tt(L("newf", a, H), PB(6, a), L("tw", a, H), add)
+            elif name == "new":
+                tt(L("tbo", W + a, H), PB(6, a), L("tw", a, H), add)
+                if a:
+                    send(LAN, [(d, L("tbn", slot(rank, d) * TW + W, M), "st%d_%d" % (r, slot(rank, d)))
+                               for d in (far, near)], [cr(r, near), cr(r, far)] if r else [])
+            elif name == "yw":
+                tt(PB(0, a), PB(0, a), L("won", a, H), mul)
+            elif name == "y":
+                tt(L("yo", a, H), PB(0, a), L("old0", a, H), add)
+                dma("y", [((T.y[:, a:a + H], []), L("yo", a, H))])
+            elif name == "ye":
+                act(S("pen"), B(1), ACT.Copy)
+                dma("s", [((T.ye[:], []), S("pen"))])
+
+        order = "s0 s1 zf0 zf1 d0 d1 m0 m1 t0 t1 e0 e1 mz0 mz1 z0 z1 dif0 dif1 cmp0 cmp1 "
         if last:
-            mm(B(4), L("boi", 128 * 14, 128), LAN, True, True, True)
-        H = M // 2
-        for a in (0, H):
-            tt(B(2, a, a + H), B(2, a, a + H), L("aa", 3 * M + a, H), add)
-        for a in (0, H):
-            tt(L("ea", M + a, H), B(2, a, a + H), L("sa", M + a, H), sub)
-        for a in (0, H):
-            tt(B(3, a, a + H), B(3, a, a + H), L("ea", M + a, H), mul)
-        for a in (0, H):
-            tt(B(3, a, a + H), B(3, a, a + H), L("sa", M + a, H), add)
-        for a in (0, H):
-            tt(L("dif", a, H), L("zf", a, H), B(3, a, a + H), sub)
-            act(L("gap", a, H), L("dif", a, H), ACT.Abs)
-        act(S("half"), S("dif"), ACT.Copy, scale=0.5)
-        act(S("ex") if last else B(2), S("gap"), ACT.Exp, scale=-1.0)
-        CB = {0: B(7, 0, H), H: B(1, 0, H)}
-        for a in (0, H):
-            mm(CB[a], CM(0), L("tbo", W + a, H), True, False)
-        for a in (0, H):
-            ts(L("cmpb", a, H), L("gap", a, H), col("epsc", 0), ALU.is_le)
-            mm(CB[a], S("bo"), L("cmpb", a, H), False, True, True)
-        for a in (0, H):
-            ts(L("won", a, H), CB[a], 25.0, ALU.is_ge)
+            order += "hf0 hf1 won0 won1 hv0 hv1 ex0 ex1 yw0 yw1 y0 y1 ye0 tw0 tw1 new0 new1"
+        else:
+            order += "hf0 hf1 won0 won1 tw0 tw1 new0 new1 tg0 tg1 hv0"
+        for w in order.split():
+            step(w[:-1], H * int(w[-1]))
         if last:
-            tt(B(0), B(3), S("half"), add)
-            tt(B(4), B(4), S("ex"), mul)
-            tt(B(0), B(0), S("won"), mul)
-            tt(S("yea"), B(4), S("yea"), add)
-            dma("s", [((T.ye[:], []), S("yea"))])
-            tt(S("yo"), B(0), S("old0"), add)
-            dma("y", [((T.y[:], []), S("yo"))])
-            for a in (0, H):
-                tt(L("tw", a, H), B(5, a, a + H), L("won", a, H), mul)
-            for a in (0, H):
-                tt(L("newf", a, H), B(6, a, a + H), L("tw", a, H), add)
             for q, rows in (("s", (0, 1, 2)), ("y", (3, 4))):
                 dma(q, [((T.yf[8 * j:8 * j + 8, :], []), S("newf", rows=slice(10 + j, 128, 16))) for j in rows])
             break
         for a in (0, H):
             act(L("pen", a, H), CB[a], ACT.Relu, scale=-4.0 * BIG, bias=col("cf", 13))
-        for a in (0, H):
-            tt(L("tw", a, H), B(5, a, a + H), L("won", a, H), mul)
-        for a in (0, H):
-            tt(L("tbo", W + a, H), B(6, a, a + H), L("tw", a, H), add)
-        send(LAN, [(d, L("tbn", slot(rank, d) * TW + W, M), "st%d_%d" % (r, slot(rank, d))) for d in (far, near)],
-             [cr(r, near), cr(r, far)] if r else [])
-        tr(S("tt", 0, 512), LAN)
+        tr(S("tt", 0, M), LAN)
+        fix(1, 0, [(4, 1), (9, 0)], 0, 1024, False, "tu")
         fix(5, 0, [(14, 0)], 0, 512, True)
-        tr(S("tu"), S("gn"))
-        fix(4, 0, [(4, 1), (9, 0)], 0, 1024, False, "tu")
-        fix_taps(4, 64, True, "tu")
+        fix_taps(1, 64, True, "tu")
+        step("hv", H)
         tt(S("nt", 0, 32), B(5, 0, 32), L("nbm", 32 * r, 32), mul)
-        tt(B(0, 0, H), B(3, 0, H), L("half", 0, H), add)
-        tt(S("nt", 32, 64), S("nt", 0, 32), S("lj"), add)
-        tt(B(0, H, M), B(3, H, M), L("half", H, H), add)
-        cp(S("nr16"), S("nt", 32, 64))
-        gather_near(r + 1)
         tt(B(0, 0, H), B(0, 0, H), L("pen", 0, H), sub)
+        tt(S("nt", 32, 64), S("nt", 0, 32), S("lj"), add)
+        if r == 1:
+            ts(S("dn"), B(5, 0, 32), -2.0 * TW, mul, 2.0 * TW, add)
+        cp(S("nr16"), S("nt", 32, 64))
+        act(B(2), S("gap"), ACT.Exp, scale=-1.0)
+        gather_near(r + 1)
         tt(B(0, H, M), B(0, H, M), L("pen", H, H), sub)
-        cp(S("mp16"), B(4, 0, 64))
-        cp(S("t116"), B(4, 64, 320))
+        cp(S("mp16"), B(1, 0, 64))
+        cp(S("t116"), B(1, 64, 320))
         for h, a in enumerate((0, H)):
             tt(L("val", a, H), B(0, a, a + H), L("val", a, H), mx)
             send(L("val", a, H),
@@ -723,7 +762,7 @@ def rank_program(g, core, T, topo):
             landed(L("lv", a, H), "vl%d_2_%d" % (r, h))
             send(L("lv", a, H), [(near, L("xf", XA[slot(op, near)] + W + a, H), "vl%d_%d_%d" % (r, slot(op, near), h))])
             dma("y", rolled(("xf", XA[2] + W + a), ("lv", a), 0, H) + rolled(("xf", XA[3] + W + a), ("lv", a), 1, H))
-        cp(S("t1f"), B(4, 64, 320))
+        cp(S("t1f"), B(1, 64, 320))
         if r == 0:
             tr(S("tu", 0, 512), S("br"))
             fix_flows(1, 0, 0, "tu")
@@ -738,4 +777,5 @@ def rank_program(g, core, T, topo):
 
 
 DI_EARLY = 5
+XB = [(0, 1024), (1024, 512), (1536, 512)]
 BLOCKS = [(0, 512), (512, 512), (1024, 512), (1536, 256), (1792, 256)]

@@ -5,8 +5,20 @@ W, M, TW = 2048, 512, 2560
 BIG = float(2.0 ** 96)
 TINY = float(2.0 ** -46)
 MAGIC = float(3 * 2 ** 22)
+FAR = 8192.0
+FW = 2 * TW + 8
+BW = 2 * W + 16
+XN = 1024
+BLOCKS = [(0, 512), (512, 512), (1024, 512), (1536, 256), (1792, 256)]
+
+CYCLE, PE_CYCLE, GATHER, SCATTER, WAKE = 0.83, 0.45, 1.56, 3.8, 100.0
+ISSUE, DMA_START, LOCAL_RATE, REMOTE_RATE = 300.0, 1700.0, 300.0, 160.0
+FIRST_EXP, SPARE, PASSES = 1300.0, 1.0, 6
 
 F32, BF, I32, U16 = "float32", "bfloat16", "int32", "uint16"
+SIZE = {F32: 4, BF: 2, I32: 4, U16: 2}
+COLS = ("row grp b16 fv fq fb b1 b2 p hi tap lo flag even low keep up down ma tapc mb own t1 fto h0 h1 "
+        "flow fin base0 cto lt14 lt10 way0 way1").split()
 
 
 def _sb(n, dt):
@@ -14,44 +26,130 @@ def _sb(n, dt):
 
 
 SCRATCH = {
-    "msi": _sb(32, I32), "cori": _sb(512, I32), "epsc": _sb(4, F32), "fli": _sb(W, I32), "xo": _sb(W, BF),
-    "ms16": _sb(32, U16), "cor16": _sb(512, U16), "mw": _sb(TW, BF), "gg": _sb(8192, BF),
-    "tbo": _sb(TW, BF), "tbn": _sb(2 * TW, BF), "lt": _sb(W, BF), "t2": _sb(2 * W, BF),
-    "xl": _sb(3 * W, BF), "xf": _sb(4 * TW + 8, F32), "dn": _sb(32, F32), "eyef": _sb(128, F32), "lv": _sb(M, F32),
-    "ip": _sb(4, I32), "ia": _sb(160, I32), "ir": _sb(64, F32), "ig": _sb(128, F32), "lj": _sb(32, F32),
-    "ci": _sb(8, I32), "cf": _sb(32, F32), "mk": _sb(16, F32), "hc": _sb(48, BF), "sm": _sb(8, F32),
-    "dd": _sb(160, BF), "sel": _sb(5 * 128, BF), "fx": _sb(4 * 160, BF), "g14": _sb(160, BF), "bo": _sb(128, BF),
-    "boi": _sb(16 * 128, BF), "di": _sb(16 * 160, BF), "cm": _sb(8 * 128, BF), "ti": _sb(128, I32), "tj": _sb(128, I32),
-    "home": _sb(128, F32), "hom4": _sb(128, F32), "nbi": _sb(96, I32), "nb16": _sb(96, U16), "nbm": _sb(64, F32),
-    "nr16": _sb(32, U16), "gr": _sb(1024, BF), "gn": _sb(1024, BF), "tt": _sb(1024, BF), "tu": _sb(1024, BF),
-    "pf": _sb(128, F32), "p10": _sb(128, I32), "p11": _sb(128, I32), "p2": _sb(128, I32),
-    "cc": _sb(128, I32), "pl": _sb(64, I32), "pm": _sb(64, I32), "pl16": _sb(64, U16), "pn16": _sb(128, U16),
-    "mp16": _sb(64, U16), "t1f": _sb(256, F32), "t116": _sb(256, U16), "t2f": _sb(256, F32), "tsf": _sb(256, F32),
-    "ts16": _sb(256, U16), "ok": _sb(64, F32), "fh": _sb(64, F32), "fi": _sb(64, F32), "q1": _sb(128, F32), "q2": _sb(128, F32),
-    "pe": _sb(128, I32), "pa": _sb(128, I32), "uv": _sb(128, BF), "own": _sb(128, BF), "nt": _sb(64, F32),
-    "br": _sb(M, BF), "dif": _sb(M, F32), "gap": _sb(M, F32), "cmpb": _sb(M, BF), "half": _sb(M, F32),
-    "won": _sb(M, F32), "tw": _sb(M, F32), "pen": _sb(M, F32), "val": _sb(M, F32), "ex": _sb(M, F32),
-    "yea": _sb(M, F32), "old0": _sb(M, F32), "newf": _sb(M, F32), "yo": _sb(M, F32),
-    "aa": _sb(4 * M, F32), "da": _sb(4 * M, F32), "sa": _sb(2 * M, F32), "ea": _sb(2 * M, F32), "zf": _sb(M, F32),
+    "msi": _sb(32, I32), "cori": _sb(512, I32), "epsc": _sb(4, F32), "fli": _sb(M, I32), "flb": _sb(M, BF),
+    "xo": _sb(W, BF), "ms16": _sb(32, U16), "cor16": _sb(512, U16), "mw": _sb(TW, BF), "gg": _sb(8192, BF),
+    "tbo": _sb(TW, BF), "tbn": _sb(2 * TW, BF), "lt": _sb(W, BF), "t2": _sb(W, BF),
+    "xb": _sb(2 * BW, BF), "xf": _sb(2 * FW, F32), "eyef": _sb(128, F32), "turn": _sb(128, F32), "rv": _sb(M, F32),
+    "ia": _sb(160, I32), "iam": _sb(160, I32), "ir": _sb(64, F32),
+    "ci": _sb(12, I32), "cf": _sb(40, F32), "mk": _sb(32, F32), "hc": _sb(48, BF), "m4": _sb(4, F32),
+    "dd": _sb(160, BF), "sel": _sb(3 * 128, BF), "fx": _sb(4 * 160, BF), "e64": _sb(128, BF),
+    "sf": _sb(5 * 128, BF), "zz": _sb(256, BF), "zc": _sb(144, BF), "cb": _sb(704, BF), "dm": _sb(8 * 144, BF),
+    "wq": _sb(20, F32),
+    "boi": _sb(16 * 128, BF), "di": _sb(2304, BF), "one": _sb(2304, BF), "ti": _sb(160, I32), "tj": _sb(96, I32),
+    "homb": _sb(128, BF), "homu": _sb(64, BF), "em": _sb(128, BF), "nbi": _sb(96, I32), "nb16": _sb(96, U16), "nr16": _sb(64, U16),
+    "gr": _sb(1024, BF), "g2": _sb(1024, BF), "gn": _sb(1024, BF), "go": _sb(1536, BF),
+    "tt": _sb(1024, BF), "tv": _sb(1024, BF), "tu": _sb(1024, BF), "tw": _sb(2048, BF),
+    "pb": _sb(512, BF), "cc": _sb(384, I32), "pn16": _sb(256, U16),
+    "t1f": _sb(256, F32), "t116": _sb(640, U16), "c2": _sb(384, F32), "sl": _sb(384, I32), "ts16": _sb(256, U16),
+    "okb": _sb(64, BF), "fh": _sb(128, F32), "ee": _sb(128, I32), "pa": _sb(128, I32), "uv": _sb(128, BF),
+    "q0": _sb(128, F32), "q1": _sb(128, F32), "own": _sb(128, BF), "base": _sb(32, F32), "idx": _sb(32, U16),
+    "ixi": _sb(64, I32), "ixf": _sb(32, F32), "dnb": _sb(32, BF), "ixg": _sb(32, U16),
+    "sw": _sb(6 * M, BF), "vw": _sb(6 * M, F32), "gw": _sb(3 * M + 16, F32),
+    "dif": _sb(M, F32), "cmpb": _sb(M, BF), "half": _sb(M, F32), "val": _sb(M, F32), "yea": _sb(M, F32),
+    "yeo": _sb(M, F32), "newf": _sb(M, F32),
+    "aa": _sb(4 * M, F32), "da": _sb(4 * M, F32), "sa": _sb(2 * M, F32), "ea": _sb(2 * M, F32), "z1": _sb(M, F32),
 }
 for _b in range(8):
     SCRATCH["b%d" % _b] = ("psum", [128, 512], F32)
+for _c in range(W // XN):
+    SCRATCH["hx%d" % _c] = ("dram", [160, XN], BF)
 
-SEMAPHORES = (["v", "s", "p", "gp"] + ["d%d" % i for i in range(24)] + ["l%d" % i for i in range(40)]
-              + ["tb%d_%d" % (a, c) for a in range(3) for c in range(5)]
-              + ["x%d_%d" % (a, c) for a in range(3) for c in range(3)]
+SEMAPHORES = (["v", "s", "p", "gp"] + ["d%d" % i for i in range(24)] + ["l%d" % i for i in range(36)]
+              + ["e%d" % i for i in range(5)]
+              + ["tb%d_%d" % (a, c) for a in range(2) for c in range(5)] + ["tc%d" % c for c in range(5)]
+              + ["x%d_%d" % (a, c) for a in range(4) for c in range(2)] + ["hx0", "hx1"]
               + ["st%d_%d" % (r, a) for r in range(2) for a in range(2)]
-              + ["vl%d_%d_%d" % (r, a, h) for r in range(2) for a in range(3) for h in range(2)]
-              + ["cr%d_%d" % (r, a) for r in range(2) for a in range(3)])
+              + ["v%s%d_%d" % (a, r, h) for a in "no" for r in range(2) for h in range(2)] + ["vf0", "vf1"]
+              + ["cr%d" % a for a in range(3)])
+
+
+def in_psum(name):
+    return name in SCRATCH and SCRATCH[name][0] == "psum"
+
+
+def put_in_order(calls):
+    n = len(calls)
+    before = [dict() for _ in calls]
+    seen, last_pe = {}, {}
+    for j, c in enumerate(calls):
+        for i, extra in c["after"]:
+            before[j][i] = extra
+        for keys, isw in ((c["reads"], False), (c["writes"], True)):
+            for name, lo, hi in keys:
+                for a, b, w, i in seen.get(name, []):
+                    if a < hi and lo < b and (w or isw):
+                        before[j][i] = max(before[j].get(i, 0.0), 0.0)
+                if in_psum(name) and "p" in c["cost"]:
+                    if name in last_pe and last_pe[name] != j:
+                        before[j].setdefault(last_pe[name], 0.0)
+                    last_pe[name] = j
+        for name, lo, hi in c["writes"]:
+            seen[name] = [x for x in seen.get(name, []) if not (lo <= x[0] and x[1] <= hi)] + [(lo, hi, True, j)]
+        for name, lo, hi in c["reads"]:
+            seen.setdefault(name, []).append((lo, hi, False, j))
+        before[j].pop(j, None)
+    for j in range(n):
+        for i in before[j]:
+            before[j][i] += calls[i]["lat"] + WAKE
+    for q in "gy":
+        js = [j for j, c in enumerate(calls) if q in c["cost"]]
+        for i, j in zip(js, js[1:]):
+            before[j].setdefault(i, 0.0)
+    banks = [sorted({k[0] for k in c["reads"] + c["writes"] if in_psum(k[0])}) for c in calls]
+
+    def place(turns):
+        busy, end, on = {}, [0.0] * n, [None] * n
+        for j in turns:
+            ready = max([0.0] + [end[i] + gap for i, gap in before[j].items()])
+            best = None
+            for q in calls[j]["cost"]:
+                d, t, moved = calls[j]["cost"][q], ready, q != "n"
+                while moved:
+                    moved = False
+                    for k in [q] + banks[j]:
+                        spans = busy.get(k, [])
+                        for a, b, who in spans[first_after(spans, t - WAKE):]:
+                            pad = 0.0 if who == q else WAKE
+                            if a - pad >= t + d:
+                                break
+                            if t < b + pad:
+                                t, moved = b + pad, True
+                score = t + d * (1 + SPARE if q == "v" else 1)
+                if best is None or score < best[0]:
+                    best = (score, t, d, q)
+            _, t, d, q = best
+            for k in [q] + banks[j]:
+                spans = busy.setdefault(k, [])
+                spans.insert(first_after(spans, t), (t, t + d, q))
+            end[j], on[j] = t + d, q
+        return end, on
+
+    def first_after(spans, t):
+        lo, hi = 0, len(spans)
+        while lo < hi:
+            mid = (lo + hi) // 2
+            lo, hi = (mid + 1, hi) if spans[mid][1] <= t else (lo, mid)
+        return lo
+
+    turns, taken = [], set()
+
+    def take(j):
+        if j not in taken:
+            taken.add(j)
+            for i in sorted(before[j]):
+                take(i)
+            turns.append(j)
+        assert j in turns
+
+    for j in [j for j in range(n) if not calls[j]["aside"]] + list(range(n)):
+        take(j)
+    end, on = place(turns)
+    return [(j, on[j]) for j in sorted(range(n), key=lambda j: (end[j] - calls[j]["cost"][on[j]], j))]
 
 
 def rank_program(g, core, T, topo):
-    rank = T.rank_of(core)
-    if rank is None:
-        return
     N = len(T.cores)
     cores = list(T.cores)
-    up, dn, op = (rank + 1) % N, (rank - 1) % N, (rank + 2) % N
 
     def same_chip(a, b):
         return cores[b] in topo.cores_of(cores[a])
@@ -59,28 +157,50 @@ def rank_program(g, core, T, topo):
     def slot(src, dst):
         return {1: 0, N - 1: 1, 2: 2}[(src - dst) % N]
 
-    near = up if same_chip(rank, up) else dn
-    far = dn if near == up else up
-    off_eng = topo.engines(core, cores[far])
-    on_eng = [e for e in topo.engines(core, cores[near]) if e not in off_eng]
-    off_mask = sum(1 << e for e in off_eng)
-    on_mask = sum(1 << e for e in on_eng)
-    NE = len(off_eng)
+    def ring(r):
+        up, dn = (r + 1) % N, (r - 1) % N
+        return (up, dn, (r + 2) % N) if same_chip(r, up) else (dn, up, (r + 2) % N)
 
-    def mask_to(d):
-        return on_mask if same_chip(rank, d) else off_mask
+    def helper(r):
+        return [c for c in topo.cores_of(cores[ring(r)[1]]) if c not in cores and topo.die(c) == topo.die(cores[r])][0]
 
-    def dst_id(d):
-        rid, pid = topo.addr(cores[d], core)
+    def bits(engines):
+        return sum(1 << e for e in engines)
+
+    def to_core(c):
+        rid, pid = topo.addr(c, core)
         return DstId(rid=rid, pnc=pid)
 
+    def xb_at(k, second, c):
+        a = BW * k + W * second + XN * c
+        return T.xb[:, a:a + XN]
+
+    rank = T.rank_of(core)
+    if rank is None:
+        for r in range(N):
+            if helper(r) == core:
+                hand_on_x(g, core, T, topo, cores[ring(r)[1]], cores[ring(r)[2]], slot(r, ring(r)[1]), bits, to_core, xb_at)
+        return
+    near, far, op = ring(rank)
+    off_eng = topo.engines(core, cores[far])
+    on_eng = [e for e in topo.engines(core, cores[near]) if e not in off_eng]
+    NE = len(off_eng)
+    ka, kb = slot(near, rank), slot(far, rank)
+
+    def mask_to(c):
+        return bits(on_eng if c in topo.cores_of(core) else off_eng)
+
     Q = {"v": g.vector, "s": g.scalar, "p": g.tensor, "g": g, "y": g.sync}
+    SEM = {"v": "v", "s": "s", "p": "p", "g": "gp"}
     cnt = {"v": 0, "s": 0, "p": 0, "gp": 0}
     waited = {q: {} for q in Q}
     recs = {}
     owed = {}
+    nxt = {"d": 0, "l": 0, "e": 0}
+    calls = []
     pend = []
-    nxt = {"d": 0, "l": 0}
+    now = [0, ""]
+    aside = [False]
 
     def S(name, lo=None, hi=None, step=None, rows=None):
         t = T[name]
@@ -88,13 +208,16 @@ def rank_program(g, core, T, topo):
         hi = t.shape[1] if hi is None else hi
         r = slice(None) if rows is None else rows
         ap = t[r, lo:hi] if step is None else t[r, lo:hi:step]
-        return (ap, [(name, lo, hi)])
+        return (ap, [(name, lo, hi)], [], len(range(lo, hi, step or 1)), name)
 
     def L(name, lo, n):
         return S(name, lo, lo + n)
 
+    def HBM(ap):
+        return (ap, [], [], 0, None)
+
     def IND(win, off):
-        return (win[0].indirect(off[0]), win[1], off[1])
+        return (win[0].indirect(off[0]), win[1], off[1], 16 * off[3], win[4])
 
     def wait(q, tok):
         sem, val = tok[0], tok[1]
@@ -106,7 +229,7 @@ def rank_program(g, core, T, topo):
         need = {}
         for keys, isw in ((reads, False), (writes, True)):
             for (n, lo, hi) in keys:
-                ps = n in SCRATCH and SCRATCH[n][0] == "psum"
+                ps = in_psum(n)
                 for (a, b, w, tok) in recs.get(n, []):
                     same = eng is not None and tok[2] == eng
                     if same and eng == "p":
@@ -123,117 +246,164 @@ def rank_program(g, core, T, topo):
             keep = [x for x in recs.get(n, []) if not (not x[2] and x[3][0] == tok[0] and lo <= x[0] and x[1] <= hi)]
             recs[n] = keep + [(lo, hi, False, tok)]
 
-    def keys_of(ins):
-        r = []
-        for a in ins:
-            if isinstance(a, tuple):
-                r += a[1]
-                if len(a) == 3:
-                    r += a[2]
-        return r
+    def record(cost, emit, reads, writes, lat=0.0, after=()):
+        calls.append(dict(cost=cost, emit=emit, reads=reads, writes=writes, lat=lat, after=list(after), aside=aside[0],
+                          step=tuple(now)))
+        return len(calls) - 1
+
+    def step(name, k=None):
+        now[1] = name if k is None else name + "ab"[k != ka]
 
     def ap(a):
         return a[0] if isinstance(a, tuple) else a
 
-    def comp(q, sem, fn, out, ins):
-        reads = keys_of(ins) + (out[2] if len(out) == 3 else [])
-        writes = out[1]
-        deps(q, sem, reads, writes)
-        cnt[sem] += 1
-        fn().then_inc(T.sem[sem], 1)
-        note(reads, writes, (sem, cnt[sem], sem))
+    def comp(forms, out, ins, twice=False):
+        ops = [a for a in ins if isinstance(a, tuple)]
+        reads = [k for a in ops for k in a[1] + a[2]] + out[2]
+        short = all(SIZE[SCRATCH[a[4]][2]] == 2 for a in [out] + ops[:1])
+        cost = {}
+        for q in forms:
+            if out[2] or (ops and ops[0][2]):
+                cost[q] = 60 + out[3] * CYCLE * (SCATTER if out[2] else GATHER)
+            elif q == "g":
+                cost[q] = 130 + 2 * out[3] * CYCLE
+            else:
+                cost[q] = out[3] * (2 if twice else 0.5 if short and q == "v" else 1) * CYCLE + 60
+
+        def emit(q):
+            sem = SEM[q]
+            deps(q, sem, reads, out[1])
+            cnt[sem] += 1
+            forms[q]().then_inc(T.sem[sem], 1)
+            note(reads, out[1], (sem, cnt[sem], sem))
+        record(cost, emit, reads, out[1])
 
     V = g.vector
 
     def cp(out, a):
-        comp("v", "v", lambda: V.tensor_copy(out[0], a[0]), out, [a])
+        comp({"v": lambda: V.tensor_copy(out[0], a[0])}, out, [a])
 
     def tt(out, a, b, o):
-        comp("v", "v", lambda: V.tensor_tensor(out[0], a[0], b[0], o), out, [a, b])
+        comp({"v": lambda: V.tensor_tensor(out[0], a[0], b[0], o)}, out, [a, b], not (in_psum(a[4]) or in_psum(b[4])))
+
+    def ts_call(out, a, s1, o1, s2=None, o2=None):
+        if o2 is None:
+            return lambda: V.tensor_scalar(out[0], a[0], ap(s1), None, o1)
+        return lambda: V.tensor_scalar(out[0], a[0], ap(s1), ap(s2), o1, o2)
 
     def ts(out, a, s1, o1, s2=None, o2=None):
-        if o2 is None:
-            comp("v", "v", lambda: V.tensor_scalar(out[0], a[0], ap(s1), None, o1), out, [a, s1])
-        else:
-            comp("v", "v", lambda: V.tensor_scalar(out[0], a[0], ap(s1), ap(s2), o1, o2), out, [a, s1, s2])
+        comp({"v": ts_call(out, a, s1, o1, s2, o2)}, out, [a, s1, s2])
 
     def ms(out, c):
-        comp("v", "v", lambda: V.memset(out[0], c), out, [])
+        comp({"v": lambda: V.memset(out[0], c)}, out, [])
 
     def tr(out, a):
-        comp("v", "v", lambda: V.transpose(out[0], a[0]), out, [a])
+        comp({"v": lambda: V.transpose(out[0], a[0])}, out, [a])
 
-    def act(out, a, f, scale=None, bias=None):
+    def act_call(out, a, f, scale=None, bias=None):
         kw = {}
         if scale is not None:
             kw["scale"] = ap(scale)
         if bias is not None:
             kw["bias"] = ap(bias)
-        comp("s", "s", lambda: g.scalar.activation(out[0], a[0], f, **kw), out, [a, scale, bias])
+        return lambda: g.scalar.activation(out[0], a[0], f, **kw)
 
-    def mv(out, a, on_s):
-        if on_s:
-            act(out, a, ACT.Copy)
+    def act(out, a, f, scale=None, bias=None):
+        comp({"s": act_call(out, a, f, scale, bias)}, out, [a, scale, bias])
+
+    def lin(out, a, scale=None, bias=None, on="sv"):
+        forms = {"s": act_call(out, a, ACT.Copy if bias is None else ACT.Identity, scale, bias)}
+        if scale is None and bias is None:
+            forms["v"] = lambda: V.tensor_copy(out[0], a[0])
+        elif bias is None:
+            forms["v"] = ts_call(out, a, scale, ALU.mult)
+        elif scale is None:
+            forms["v"] = ts_call(out, a, bias, ALU.add)
         else:
-            cp(out, a)
+            forms["v"] = ts_call(out, a, scale, ALU.mult, bias, ALU.add)
+        comp({q: forms[q] for q in on}, out, [a, scale, bias])
 
     def iota(out, pat, base, cmul, small=False):
         kw = {"allow_small_or_imprecise_dtypes": True} if small else {}
-        comp("g", "gp", lambda: g.iota(out[0], pat, base, cmul, **kw), out, [])
+        comp({"g": lambda: g.iota(out[0], pat, base, cmul, **kw)}, out, [])
+
+    def select(out, a, *how):
+        comp({"g": lambda: g.affine_select(out[0], a[0], *how)}, out, [a])
 
     def mm(out, l, r, start, stop, inc=False):
-        reads, writes = l[1] + r[1], out[1]
-        deps("p", "p", reads, writes)
-        ins = g.tensor.matmul(out[0], l[0], r[0], start, stop)
-        pend.append((reads, writes))
-        if inc:
+        pend.append((out, l, r, start, stop))
+        if not inc:
+            return
+        group = list(pend)
+        del pend[:]
+        reads = list({k for _, l, r, _, _ in group for k in l[1] + r[1]})
+        writes = list({k for o in group for k in o[0][1]})
+
+        def emit(q):
+            ins = None
+            for o, l, r, st, sp in group:
+                deps("p", "p", l[1] + r[1], o[1])
+                ins = g.tensor.matmul(o[0], l[0], r[0], st, sp)
             cnt["p"] += 1
             ins.then_inc(T.sem["p"], 1)
-            for a, b in pend:
-                note(a, b, ("p", cnt["p"], "p"))
-            del pend[:]
+            note(reads, writes, ("p", cnt["p"], "p"))
+        cost = sum(max(64, r[3]) * (4 if SCRATCH[l[4]][2] == F32 else 1) for _, l, r, _, _ in group) * PE_CYCLE
+        record({"p": cost}, emit, reads, writes, 60.0)
 
-    def dma(q, pairs, **kw):
-        sem = "d%d" % nxt["d"]
-        nxt["d"] += 1
-        rd, wr = [], []
-        for o, i in pairs:
-            rd += i[1]
-            wr += o[1]
-        deps(q, None, rd, wr)
-        for o, i in pairs:
-            Q[q].dma_start(o[0], i[0], **kw).then_inc(T.sem[sem], 16)
-        owed[sem] = 16 * len(pairs)
-        note(rd, wr, (sem, 16 * len(pairs), None))
+    def dma(q, pairs, size, **kw):
+        kind = "e" if q == "g" else "d"
+        sem = "%s%d" % (kind, nxt[kind])
+        nxt[kind] += 1
+        rd = [k for _, i in pairs for k in i[1]]
+        wr = [k for o, _ in pairs for k in o[1]]
 
-    def send(src, items, before=()):
+        def emit(q):
+            deps(q, None, rd, wr)
+            for o, i in pairs:
+                Q[q].dma_start(o[0], i[0], **kw).then_inc(T.sem[sem], 16)
+            owed[sem] = 16 * len(pairs)
+            note(rd, wr, (sem, 16 * len(pairs), None))
+        record({q: (2 * ISSUE if q == "g" else 60.0) * len(pairs)}, emit, rd, wr, DMA_START + size / LOCAL_RATE)
+
+    def send(items, before=(), wide=False):
         sem = "l%d" % nxt["l"]
         nxt["l"] += 1
-        deps("g", None, src[1], [])
-        for t in before:
-            wait("g", t)
-        trs = [RemoteDMATransfer(dst_ids=[dst_id(d)], dma_engine_mask=mask_to(d), remote_sem=T.sem[rs],
-                                 src=src[0], dst=land[0]) for d, land, rs in items]
-        g.remote_dma_fused(trs, local_sem=T.sem[sem])
-        owed[sem] = NE * len(items)
-        note(src[1], [], (sem, NE * len(items), None))
+        rd = [k for it in items for k in it[0][1]]
+        n = len(on_eng + off_eng) if wide else NE * len(items)
 
-    def landed(where, sem):
-        owed[sem] = NE
-        note([], where[1], (sem, NE, None))
+        def emit(q):
+            deps("g", None, rd, [])
+            for t in before:
+                wait("g", t)
+            trs = [RemoteDMATransfer(dst_ids=[to_core(d)], dma_engine_mask=bits(on_eng + off_eng) if wide else mask_to(d),
+                                     remote_sem=T.sem[rs], src=src[0], dst=land) for src, d, land, rs in items]
+            g.remote_dma_fused(trs, local_sem=T.sem[sem])
+            owed[sem] = n
+            note(rd, [], (sem, n, None))
+        src = items[0][0]
+        return record({"g": ISSUE}, emit, rd, [], DMA_START + 128 * src[3] * SIZE[SCRATCH[src[4]][2]] / REMOTE_RATE)
 
-    def credit(keys, dests, r):
-        deps("g", None, [], keys)
+    def landed(where, sem, like, extra=0.0, n=NE):
+        def emit(q):
+            owed[sem] = n
+            note([], where[1], (sem, n, None))
+        record({"n": 0.0}, emit, [], where[1], 0.0, [(like, extra)])
+
+    def credit(keys, dests):
         for d in dests:
             sem = "l%d" % nxt["l"]
             nxt["l"] += 1
-            rid, pid = topo.addr(cores[d], core)
-            e = (on_eng if same_chip(rank, d) else off_eng)[0]
-            g.remote_sem_update(T.sem["cr%d_%d" % (r, slot(rank, d))], T.sem[sem], pid, rid, 1 << e)
-            owed[sem] = 1
 
-    def cr(r, src):
-        sem = "cr%d_%d" % (r, slot(src, rank))
+            def emit(q, d=d, sem=sem):
+                deps("g", None, [], keys)
+                rid, pid = topo.addr(cores[d], core)
+                e = (on_eng if same_chip(rank, d) else off_eng)[0]
+                g.remote_sem_update(T.sem["cr%d" % slot(rank, d)], T.sem[sem], pid, rid, 1 << e)
+                owed[sem] = 1
+            record({"g": ISSUE}, emit, [], keys)
+
+    def cr(src):
+        sem = "cr%d" % slot(src, rank)
         owed[sem] = 1
         return (sem, 1)
 
@@ -243,539 +413,613 @@ def rank_program(g, core, T, topo):
     def col(name, j):
         return S(name, j, j + 1)
 
-    def CM(k):
-        return L("cm", 128 * k, 128)
+    def C(name):
+        return col("cf", COLS.index(name))
 
     add, sub, mul, mx, mn = ALU.add, ALU.subtract, ALU.mult, ALU.max, ALU.min
-    band, shr = ALU.bitwise_and, ALU.arith_shift_right
+    band, shr, eq = ALU.bitwise_and, ALU.arith_shift_right, ALU.is_equal
     EYE = S("dd", 16, 144)
     LAN = S("tbo", W, TW)
-    FW = 2 * TW + 8
     XA = [0, FW, TW, FW + TW]
-    kn, kf = slot(near, rank), slot(far, rank)
+    H = M // 2
 
-    dma("y", [(S("msi"), (T.ms[:], []))])
-    dma("s", [(S("xo", 0, 1024), (T.x[:, 0:1024], []))])
-    dma("y", [(S("cori"), (T.cor[:], []))])
-    dma("s", [(S("xo", 1024, 2048), (T.x[:, 1024:2048], []))])
-    iota(col("ip", 0), [[0, 1]], 0, 1)
+    dma("y", [(S("msi"), HBM(T.ms[:]))], 0)
+    dma("s", [(S("xo", 0, XN), HBM(T.x[:, 0:XN]))], 256 * XN)
+    dma("y", [(S("cori"), HBM(T.cor[:]))], 512 * M)
+    dma("s", [(S("xo", XN, W), HBM(T.x[:, XN:W]))], 512 * XN)
+    dma("y", [(S("fli"), HBM(T.fl[:]))], 1024 * M)
+    dma("y", [(col("epsc", 0), HBM(T.eps[:]))], 0)
+    IP = col("ci", 8)
+    iota(IP, [[0, 1]], 0, 1)
     iota(S("ir"), [[1, 64]], 0, 0, True)
     iota(S("ia"), [[1, 160]], 0, -1)
-    iota(S("ig"), [[1, 8], [0, 16]], 0, 0, True)
+    iota(S("ixf"), [[32, 32]], 0, 0, True)
+    for c in range(W // XN):
+        x = L("xo", XN * c, XN)
+        sent = send([(x, helper(rank), T["hx%d" % c][16:144, :], "hx%d" % c),
+                     (x, cores[near], xb_at(slot(rank, near), 0, c), "x%d_%d" % (slot(rank, near), c))])
+        landed(L("xb", BW * ka + XN * c, XN), "x%d_%d" % (ka, c), sent)
+        landed(L("xb", BW * kb + XN * c, XN), "x%d_%d" % (kb, c), sent, 2 * DMA_START)
+        for k in range(2):
+            landed(L("xb", BW * k + W + XN * c, XN), "x%d_%d" % (2 + k, c), sent, 3 * DMA_START)
+    iota(S("one"), [[0, 2304]], 1, 0, True)
 
-    def load_flows(c):
-        iota(L("fli", 1024 * c, 1024), [[0, 1024]], 0, 0)
-        dma("y", [(S("fli", 1024 * c, 1024 * c + 1024, rows=slice(10 + q, 128, 16)),
-                   (T.fl[8 * q:8 * q + 8, 1024 * c:1024 * c + 1024], [])) for q in range(4)])
-
-    load_flows(0)
-    dma("y", [(col("epsc", 0), (T.eps[:], []))])
-    for j in range(8):
-        act(L("val", 64 * j, 64), S("ir"), ACT.Identity, scale=0.0, bias=-BIG)
-    act(L("xf", 2 * TW, 8), L("val", 0, 8), ACT.Copy)
-
-    def send_x(c, dests, n=None):
-        a, n = XB[c][0], n or XB[c][1]
-        send(L("xo", a, n), [(d, L("xl", slot(rank, d) * W + a, n), "x%d_%d" % (slot(rank, d), c)) for d in dests])
-
-    send_x(0, (far, near))
-    send_x(1, (near,), 1024)
-    load_flows(1)
-    dma("y", [(L("xf", XA[k] + W, M), S("val")) for k in range(4)])
-    iota(S("lj"), [[16, 32]], W, 0, True)
-
-    ts(col("ci", 0), col("ip", 0), 15, band)
-    ts(col("ci", 1), col("ip", 0), 4, shr)
+    aside[0] = True
+    step("cb")
+    a = 0
+    for n, value in ((64, M - FAR), (128, 0), (64, M - FAR), (64, M), (128, W), (64, M), (128, TW), (64, M)):
+        lin(L("cb", a, n), L("one", 0, n), float(value))
+        a += n
+    step("")
+    ts(col("ci", 0), IP, 15, band)
+    ts(col("ci", 1), IP, 4, shr)
     cp(S("cf", 0, 2), S("ci", 0, 2))
-    ts(col("ci", 2), col("ip", 0), 16, band)
-    ts(col("cf", 2), col("cf", 0), 5.0, ALU.is_lt)
-    ts(col("cf", 10), col("cf", 0), 10.0, ALU.is_lt)
-    ts(S("mk"), S("ir", 0, 16), col("cf", 0), ALU.is_equal)
-    tt(col("cf", 3), col("cf", 10), col("cf", 2), sub)
-    ts(S("hc", 0, 48), S("ir", 0, 48), col("cf", 2), mul)
-    ts(col("cf", 11), col("mk", 15), 8192.0, mul)
-    ts(S("mw", 0, 64), S("ir"), col("cf", 3), mul)
-    tt(col("hc", 33), col("hc", 32), col("cf", 11), add)
-    ts(S("bo"), S("ig"), col("cf", 1), ALU.is_equal)
-    ts(S("dd"), S("ia"), 16.0, ALU.is_equal)
-    for i in range(16):
-        act(L("boi", 128 * i, 128), S("bo"), ACT.Copy, scale=col("mk", i))
+    ts(col("ci", 2), IP, 16, band)
+    ts(col("ci", 3), IP, 2, shr, 7, band)
+    ts(col("ci", 4), IP, 5, shr)
+    ts(col("ci", 5), IP, 3, band)
+    ts(col("ci", 6), IP, 1, band)
+    ts(col("ci", 7), IP, 2, band)
+    cp(S("cf", 2, 9), S("ci", 2, 9))
+    ts(S("mk", 0, 16), S("ir", 0, 16), C("row"), eq)
+    ts(S("m4"), S("ir", 0, 4), C("fb"), eq)
+    for name, bound in (("hi", 4.0), ("tap", 8.0), ("lt10", 10.0), ("lt14", 14.0)):
+        ts(C(name), C("row"), bound, ALU.is_lt)
+    ts(C("even"), C("b1"), 0.0, eq, C("tap"), mul)
+    ts(C("low"), C("b2"), 0.0, eq, C("tap"), mul)
+    step("half")
+    ts(C("h0"), C("b16"), 0.0, eq)
+    ts(C("h1"), C("b16"), 0.0, ALU.is_gt)
+    step("")
+    for name, a, scale, bias in (
+            ("lo", C("hi"), -1.0, C("tap")), ("flag", col("mk", 15), FAR, None),
+            ("down", C("even"), -128.0, None),
+            ("ma", C("low"), None, col("mk", 15)), ("tapc", C("tap"), None, col("mk", 15)), ("mb", C("low"), -1.0, C("tapc")),
+            ("own", col("mk", 3), None, col("mk", 4)), ("t1", C("fv"), 16.0, C("fq")), ("fto", C("p"), -1.0, C("t1")),
+            ("flow", C("lt10"), -1.0, C("lt14")),
+            ("base0", C("row"), 2.0, -1.0 / 32), ("cto", C("row"), -1.0, 15.0), ("fin", col("mk", 14), -1.0, C("flow")),
+            ("way0", col("mk", 10), None, col("mk", 11)), ("way1", col("mk", 12), None, col("mk", 13))):
+        lin(C(name), a, scale, bias, "v" if name == "lo" else "s")
+
+    lin(S("hc", 0, 48), S("ir", 0, 48), C("hi"), on="s")
+    lin(S("mw", 0, 64), S("ir"), C("lo"), on="v")
+    lin(col("hc", 33), col("hc", 32), bias=C("flag"), on="s")
     n = 64
     while n < W:
-        ts(S("mw", n, 2 * n), S("mw", 0, n), col("hc", n // 64), add)
-        if n == 64:
-            tt(S("sm", 0, 5), S("mk", 0, 5), S("mk", 5, 10), add)
-        if n == 128:
-            ts(S("sm", 0, 4), S("sm", 0, 4), col("mk", 15), add)
-        if n == 256:
-            ts(S("mw", W, TW), S("mw", 0, M), col("hc", 33), add)
+        lin(S("mw", n, 2 * n), S("mw", 0, n), bias=col("hc", n // 64), on="v")
         n *= 2
-    ts(col("cf", 4), col("ci", 2), 0.0, ALU.is_equal)
-    ts(col("cf", 5), col("ci", 2), 0.0, ALU.is_gt)
+    lin(S("mw", W, TW), S("mw", 0, M), bias=col("hc", 33), on="s")
+    for j in range(len(calls) - 6, len(calls)):
+        calls[j]["aside"] = False
+    aside[0] = False
+    ts(S("dd"), S("ia"), 16.0, eq)
     cp(S("ms16"), S("msi"))
-    for h in range(2):
-        ts(L("fx", 320 * h + 160, 160), S("dd"), col("cf", 4 + h), mul, 64.0, mul)
-    for i in range(5):
-        act(L("sel", 128 * i, 128), EYE, ACT.Copy, scale=col("sm", i))
-    for h in range(2):
-        act(L("fx", 320 * h, 160), S("dd"), ACT.Copy, scale=col("cf", 4 + h))
-    for i in range(DI_EARLY):
-        act(L("di", 160 * i, 160), S("dd"), ACT.Copy, scale=col("mk", i))
+    ts(L("sf", 512, 128), S("ia", 0, 128), -10.0, add, C("fto"), eq)
+    lin(C("keep"), C("even"), bias=col("mk", 15), on="s")
+    lin(C("up"), C("even"), 128.0, on="s")
+    lin(L("sel", 0, 128), EYE, C("ma"), on="s")
+    lin(L("sel", 128, 128), EYE, C("mb"), on="s")
+    lin(L("sel", 256, 128), S("dd", 11, 139), C("own"), on="s")
+    for b in range(4):
+        lin(L("sf", 128 * b, 128), L("sf", 512, 128), col("m4", b), on="s")
     cp(IND(S("mw", 0, W), S("ms16")), S("mw", W, TW))
     cp(S("cor16", 0, 128), S("cori", 0, 128))
     cp(S("cor16", 128, 512), S("cori", 128, 512))
+    cp(S("flb"), S("fli"))
+    aside[0] = True
+    step("zz")
+    ts(S("iam"), S("ia"), 127, band)
+    for j, by in enumerate((112.0, 24.0)):
+        ts(L("zz", 128 * j, 128), S("iam", 0, 128), by, eq, C("tap"), mul)
+    step("fx")
+    for h in range(2):
+        lin(L("fx", 320 * h, 160), S("dd"), C("h%d" % h), on="s")
+        lin(L("fx", 320 * h + 160, 160), L("fx", 320 * h, 160), 64.0, on="s")
+    step("")
+    lin(S("eyef"), EYE, on="s")
+    step("zc")
+    ts(S("zc"), S("ia", 0, 144), C("cto"), eq, 1.0 / 16, mul)
+    ts(S("turn"), S("iam", 0, 128), (112.0, 16.0)[ka], eq)
+    step("")
+    lin(S("e64"), EYE, 1.0 / 64, on="s")
+    lin(S("em"), EYE, -1.0, on="s")
+    lin(S("mk", 16, 32), S("mk", 0, 16), 16.0, on="s")
+    for q, (a, w, b) in enumerate(((0, 64.0, 4), (1, 64.0, 5), (2, 64.0, 6), (3, 64.0, 7), (8, 64.0, 9), (10, 1.0, 12), (11, 1.0, 13))):
+        lin(col("wq", q), col("mk", 16 + a), w, col("mk", 16 + b), "s")
+    lin(col("wq", 8), col("wq", 6), 64.0, on="s")
+    lin(col("wq", 7), col("mk", 30), FAR, on="s")
+    for q in range(8):
+        step("dm%d" % (q // 4))
+        lin(L("dm", 144 * q, 144), S("zc"), col("wq", 8 if q == 6 else q))
+    step("")
+    lin(S("base"), S("ixf"), bias=C("base0"), on="s")
 
-    def relay_x(c):
-        a, n = XB[c]
-        landed(L("xl", kf * W + a, n), "x%d_%d" % (kf, c))
-        send(L("xl", kf * W + a, n), [(near, L("xl", 2 * W + a, n), "x2_%d" % c)])
+    aside[0] = False
 
-    def relay_tb(c):
+    def block_out(c):
         a, n = BLOCKS[c]
-        landed(L("tbn", kf * TW + a, n), "tb%d_%d" % (kf, c))
-        send(L("tbn", kf * TW + a, n), [(near, L("lt", a, n), "tb2_%d" % c)])
-
-    def unit(c, i, on_s):
-        a, n = BLOCKS[c]
-        mv(L("gg", W * i + a, n), IND(S("mw", 0, W), L("cor16", 128 * i + a // 16, n // 16)), on_s)
-
-    def finish_block(c):
-        a, n = BLOCKS[c]
-        tt(L("tbo", a, n), B(c, 0, n), L("fli", a, n), add)
-        send(L("tbo", a, n),
-             [(d, L("tbn", slot(rank, d) * TW + a, n), "tb%d_%d" % (slot(rank, d), c)) for d in (far, near)])
+        step("out%d" % c)
+        lin(L("tbo", a, n), B(c, 0, n), bias=C("down"))
+        sent = send([(L("tbo", a, n), cores[d], L("tbn", slot(rank, d) * TW + a, n)[0], "tb%d_%d" % (slot(rank, d), c))
+                     for d in (far, near)])
+        for k in range(2):
+            landed(L("tbn", k * TW + a, n), "tb%d_%d" % (k, c), sent)
 
     for c, (a, n) in enumerate(BLOCKS):
-        unit(c, 0, True)
-        unit(c, 3, False)
-        unit(c, 1, True)
-        if c > 0:
-            finish_block(c - 1)
-        unit(c, 2, c >= 3)
-        mm(B(c, 0, n), L("sel", 512, 128), L("mw", a, n), True, False)
-        for k, i in enumerate((0, 3, 1, 2)):
-            mm(B(c, 0, n), L("sel", 128 * i, 128), L("gg", W * i + a, n), False, k == 3, k == 3)
-        if c == 2:
-            relay_x(0)
-    finish_block(4)
-    relay_tb(0)
-    relay_tb(1)
-    send_x(1, (far,))
-    send_x(2, (far,))
-    for c in range(2, 5):
-        relay_tb(c)
-    relay_x(1)
-    relay_x(2)
-    iota(LAN, [[0, M]], 1, 0, True)
-    for c, (a, n) in enumerate(BLOCKS):
-        landed(L("tbn", kn * TW + a, n), "tb%d_%d" % (kn, c))
-        landed(L("lt", a, n), "tb2_%d" % c)
-    for c in range(2):
-        landed(L("xl", kn * W + 1024 * c, 1024), "x%d_%d" % (kn, c))
-    for c, (a, n) in enumerate(XB):
-        landed(L("xl", 2 * W + a, n), "x2_%d" % c)
+        for j in range(2):
+            step("tap%d%d" % (c, j))
+            lin(L("gg", W * (2 + j) + a, n), IND(S("mw", 0, W), L("cor16", 256 * j + a // 16, n // 16)), C("keep"), C("up"), "s")
+            tt(L("gg", W * j + a, n), IND(S("mw", 0, W), L("cor16", 256 * j + 128 + a // 16, n // 16)),
+               L("gg", W * (2 + j) + a, n), mx)
+        mm(B(c, 0, n), L("sel", 256, 128), L("mw", a, n), True, False)
+        mm(B(c, 0, n), L("sf", 128 * (a // M), 128), L("flb", a % M, n), False, False, True)
+        for j in range(2):
+            mm(B(c, 0, n), L("sel", 128 * j, 128), L("gg", W * j + a, n), False, j == 1, True)
+        if c:
+            block_out(c - 1)
+    block_out(len(BLOCKS) - 1)
 
-    def fix(bank, base, terms, lo, hi, inc, src="tt"):
+    def second_table():
+        for c, (a, n) in enumerate(BLOCKS):
+            sent = send([(L("tbn", kb * TW + a, n), cores[near], L("lt", a, n)[0], "tc%d" % c)], wide=True)
+            landed(L("lt", a, n), "tc%d" % c, sent, n=len(on_eng + off_eng))
+            b = (4, 7, 6, 4, 7)[c]
+            step("u%d" % c)
+            for j in range(2):
+                mm(B(b, 0, n), L("zz", 128 * j, 128), L("lt", a, n), j == 0, j == 1, j == 1)
+            lin(L("t2", a, n), B(b, 0, n))
+        select(S("boi"), L("one", 0, 2048), [[16, 8], [0, 16], [1, 16]], eq, 0.0, 0, -1)
+        for k in (ka, kb):
+            for second in range(2):
+                dma("g", [(L("xf", XA[k + 2 * second], W), L("xb", BW * k + W * second, W))], 1024 * W)
+        select(S("di"), S("one"), [[16, 9], [1000, 16], [1, 16]], eq, 0.0, -13000, -1)
+
+    def fix(bank, base, terms, lo, hi, src, step=1, opened=False, close=True, inc=False):
         n = (hi - lo) // 16
         for h in range(2):
             k = 0
             for e in range(2):
                 for q, w in terms:
                     end = k == 2 * len(terms) - 1
-                    mm(B(bank, base + h, base + n, 2), L("fx", 320 * h + 160 * w + 16 - 16 * (e - h), 128),
-                       S(src, lo + 16 * e + q, hi, 32), k == 0, end, inc and end and h == 1)
+                    fin = end and h == 1
+                    mm(B(bank, base + step * h, base + step * (n - 1) + 1, 2 * step),
+                       L("fx", 320 * h + 160 * w + 16 - 16 * (e - h), 128), S(src, lo + 16 * e + q, hi, 32),
+                       k == 0 and not opened, (fin and close) if opened else end, inc and fin)
                     k += 1
 
-    def fix_flows(bank, lo_f, lo_b, src="tt"):
-        fix(bank, 0, [(10, 0)], lo_f, lo_f + 512, False, src)
-        fix(bank, 32, [(12, 0)], lo_b, lo_b + 512, False, src)
-        fix(bank, 64, [(11, 1)], lo_f, lo_f + 512, False, src)
-        fix(bank, 96, [(13, 1)], lo_b, lo_b + 512, True, src)
+    def PN(r, k):
+        return L("pn16", 64 * r + 32 * k, 32)
 
-    def fix_taps(bank, base, inc=True, src="tt"):
-        for i in range(4):
-            fix(bank, base + 64 * i, [(i, 1), (5 + i, 0)], 0, 1024, inc and i == 3, src)
+    def PB(r):
+        return L("pb", 128 * r, 128)
 
-    def position(bank, start, p, lst):
-        tt(S("pf"), B(bank, 0, 128), S(start), add)
-        ts(S(p, 64, 128), S("pf", 64, 128), 0.0, mx, 127.0 * 64, mn)
-        ts(S(p, 0, 64), S("pf", 0, 64), 0.0, mx, 255.0, mn)
-        ts(S("cc", 64, 128), S(p, 64, 128), 2, shr, W - 64, band)
-        ts(S("cc", 0, 64), S(p, 0, 64), 2, shr)
-        tt(S("pl"), S("cc", 64, 128), S("cc", 0, 64), add)
-        cp(lst, S("pl"))
+    def spread(bank, base, q, src, lo, n, start, stop):
+        for i in range(16):
+            mm(B(bank, base, base + n), L("dm", 144 * q + 15 - i, 128), S(src, lo + i, lo + 16 * n, 16),
+               start and i == 0, stop and i == 15, i == 15)
 
-    def cast(k, c, on_s):
-        mv(L("xf", XA[k] + 1024 * c, 1024), L("xl", k * W + 1024 * c, 1024), on_s)
+    def place(bank, r, xbank):
+        c = 192 * (r // 3)
+        ts(L("cc", c, 64), B(bank, 64, 128), 0.0, mx, 127.0 * 64, mn)
+        if xbank == bank:
+            ts(L("pb", 128 * r, 64), B(xbank, 0, 64), 0.0, mx, 255.0, mn)
+        else:
+            ts(L("pb", 128 * r + 64, 64), B(bank, 64, 128), 0.0, mx, 127.0 * 64, mn)
+        ts(L("cc", c + 64, 64), L("cc", c, 64), W * 4 - 256, band)
+        if xbank == bank:
+            ts(L("pb", 128 * r + 64, 64), B(bank, 64, 128), 0.0, mx, 127.0 * 64, mn)
+        else:
+            ts(L("pb", 128 * r, 64), B(xbank, 0, 64), 0.0, mx, 255.0, mn)
+        tt(L("cc", c + 128, 64), L("cc", c + 64, 64), L("pb", 128 * r, 64), add)
+        ts(L("pn16", 64 * r, 64), L("cc", c + 128, 64), -1.5, add, 0.25, mul)
 
-    rot = [0]
+    def first_place(bank, r, rows, lo):
+        step("turn%d" % r)
+        tr(L("tw", lo, M), rows)
+        mm(B(bank, 0, 128), EYE, S("homb"), True, False)
+        for j, (q, w) in enumerate(((10, 0), (12, 0), (11, 1), (13, 1))):
+            fix(bank, 32 * j, [(q, w)], lo, lo + M, "tw", 1, True, j == 3, j == 3)
+        step("first%d" % r)
+        place(bank, r, bank)
 
-    def shifted(k, src, dst, on_s, banks=(0, 7)):
-        b = banks[rot[0] % 2]
-        rot[0] += 1
-        mm(B(b), CM(5 + k), src, True, True, True)
-        mv(dst, B(b), on_s)
-
-    def shift_x(c, k, on_s=True, banks=(0, 7)):
-        shifted(k, L("xl", 2 * W + M * c, M), L("xf", XA[2 + k] + M * c, M), on_s, banks)
-
-    def shift_t(c, k, on_s=True):
-        shifted(k, L("lt", M * c, M), L("t2", W * k + M * c, M), on_s)
+    def pair(name, r, odd, a=0, n=M):
+        return S(name, 2 * M * r + 2 * a + odd, 2 * M * r + 2 * a + 2 * n, 2)
 
     def gather_near(r):
-        act(S("br"), IND(S("tbo", 0, W if r == 0 else TW), S("nb16", 0, 32) if r == 0 else S("nr16")), ACT.Identity,
-            scale=col("cf", 6), bias=col("cf", 8) if r == 2 else col("mk", 14))
+        lin(pair("sw", r, 0), IND(S("tbo", 0, W if r == 0 else TW), S("nb16", 0, 32) if r == 0 else L("nr16", 32 * r - 32, 32)),
+            C("flow"), col("mk", 14), "s")
 
-    def P1(r):
-        return "p1%d" % (r % 2)
+    def rolled(dst, src, n, by):
+        s = 16 * (by % 8)
+        return [(S("xf", dst, dst + n, rows=slice(a, b)), S("xf", src, src + n, rows=slice(c, c + b - a)))
+                for a, b, c in ((0, 128 - s, s), (128 - s, 128, 0))]
 
-    def PN(r, k=None):
-        return L("pn16", 64 * (r % 2), 64) if k is None else L("pn16", 64 * (r % 2) + 32 * k, 32)
+    def fill(out, value):
+        comp({"s": act_call(out, S("mw", 0, out[3]), ACT.Identity, 0.0, value), "v": lambda: V.memset(out[0], value)},
+             out, [S("mw", 0, out[3])])
 
-    act(S("gr", 0, 512), IND(S("tbo", 0, W), S("ms16")), ACT.Copy)
+    aside[0] = True
+    step("grid")
+    ts(S("tj", 32, 64), S("msi"), 63, band)
+    ts(S("tj", 64, 96), S("msi"), 6, shr)
+    ts(S("homu"), S("tj", 32, 96), 4.0, mul)
+    step("home")
+    for j in range(4):
+        lin(L("homb", 32 * j, 32), L("homu", 32 * (j // 2), 32), (1.0, 64.0)[j // 2], on="s")
+    step("right")
     ts(S("ti", 0, 32), S("msi"), 1.0, add)
     ts(S("ti", 96, 128), S("msi"), W - 64, band)
     ts(S("tj", 0, 32), S("ti", 0, 32), 63, band)
-    ts(col("cf", 12), col("cf", 0), 14.0, ALU.is_lt)
-    tt(S("nbi", 0, 32), S("tj", 0, 32), S("ti", 96, 128), add)
-    tt(col("cf", 6), col("cf", 12), col("cf", 10), sub)
-    cp(S("nb16", 0, 32), S("nbi", 0, 32))
-    gather_near(0)
-    ts(S("tj", 32, 64), S("msi"), 63, band)
-    ts(S("tj", 64, 96), S("msi"), 6, shr)
-    for j in range(4):
-        ts(L("home", 32 * j, 32), L("tj", 32 + 32 * (j // 2), 32), (4.0, 256.0)[j // 2], mul)
-    tr(S("tt", 0, 512), S("gr", 0, 512))
-    fix_flows(2, 0, 0)
-    cast(kn, 0, True)
-    cast(kn, 1, True)
-    for k in range(2):
-        ts(S("pa"), S("ia", 0, 128), (16.0, 112.0)[k], add)
-        ts(S("pe"), S("pa"), 127, band)
-        ts(CM(5 + k), S("pe"), 0.0, ALU.is_equal)
-    tr(S("tu", 0, 512), S("br"))
-    fix_flows(1, 0, 0, "tu")
-    position(2, "home", P1(0), PN(0))
-    ms(col("cf", 15), float(TW))
-
-    def rolled(dst, src, k, n=M):
-        (dn_, d0), (sn, s0) = dst, src
-        cuts = ((0, 112, 16), (112, 128, 0)) if k == 0 else ((16, 128, 0), (0, 16, 112))
-        return [(S(dn_, d0, d0 + n, rows=slice(a, b)), S(sn, s0, s0 + n, rows=slice(c, c + b - a))) for a, b, c in cuts]
-
-    for c in range(3):
-        dma("y", rolled(("t2", M * c), ("lt", M * c), 0) + rolled(("t2", W + M * c), ("lt", M * c), 1))
     ts(S("ti", 32, 64), S("msi"), 64.0, add)
+    tt(S("nbi", 0, 32), S("tj", 0, 32), S("ti", 96, 128), add)
     ts(S("ti", 64, 96), S("msi"), 63.0, add)
+    cp(S("nb16", 0, 32), S("nbi", 0, 32))
+    step("below")
+    ts(S("ti", 128, 160), S("ti", 64, 96), 63, band)
     ts(S("nbi", 32, 64), S("ti", 32, 64), W - 1, band)
-    ts(S("tj", 64, 96), S("ti", 64, 96), 63, band)
-    ts(col("cf", 8), col("mk", 14), -1.0, mul)
-    tt(S("nbi", 64, 96), S("tj", 64, 96), S("ti", 96, 128), add)
-    ts(S("lj"), S("lj"), col("cf", 0), add)
+    tt(S("nbi", 64, 96), S("ti", 128, 160), S("ti", 96, 128), add)
     cp(S("nb16", 32, 96), S("nbi", 32, 96))
-    position(1, "home", P1(1), PN(1))
-    for i in range(DI_EARLY, DI_EARLY + 5):
-        ts(L("di", 160 * i, 160), S("dd"), col("mk", i), mul)
+    step("")
+    for k in range(2):
+        fill(L("xb", BW * k + 2 * W, 16), -BIG)
+        fill(L("xf", FW * k + 2 * TW, 8), -BIG)
+    fill(L("gw", 2 * M, 16), BIG)
+    aside[0] = False
+    step("go")
+    lin(S("go", 0, M), IND(S("tbo", 0, W), S("ms16")))
+    first_place(1, 0, S("go", 0, M), 0)
+    step("near0")
+    gather_near(0)
+    first_place(5, 1, pair("sw", 0, 0), M)
+    second_table()
 
-    def late_constants(part):
-        if part == 0:
-            ts(S("hom4", 0, 64), S("home", 0, 64), 0.375, add)
-            ts(S("hom4", 64, 128), S("home", 64, 128), 24.0, add)
-            for i in range(DI_EARLY + 5, 16):
-                ts(L("di", 160 * i, 160), S("dd"), col("mk", i), mul)
-            return
-        tt(col("cf", 9), col("cf", 6), col("cf", 8), add)
-        ms(col("cf", 14), 24.5)
-        ts(S("g14"), S("dd"), col("mk", 14), mul, 8192.0, mul)
-        ts(col("cf", 13), col("cf", 14), 4.0 * BIG, mul)
-        ts(CM(0), S("bo"), col("mk", 14), mul, 16.0, mul)
-        ts(CM(1), EYE, col("cf", 6), mul)
-        ts(CM(2), EYE, col("mk", 14), mul)
-        ts(CM(3), EYE, col("cf", 9), mul)
-        ts(CM(4), EYE, col("cf", 8), mul)
-        ts(CM(7), EYE, -1.0, mul)
+    BK = {ka: dict(pos=0, flag=1, sec=4, fst=2, u=0, v=1), kb: dict(pos=6, flag=5, sec=7, fst=3, u=2, v=3)}
 
-    def flag_unit(i, k, on_s, to=None):
-        to = i if to is None else to
-        mv(L("gg", 1024 * to + M * k, M), IND(L("tbn", k * TW, TW), L("t116", 64 * i + 32 * k, 32)), on_s)
+    def G(j, k):
+        return L("gg", 2048 * k + M * j, M)
 
-    def flag_sum(i, k, plus, to):
-        tt(L("gg", 1024 * to + M * k, M), IND(L("tbn", k * TW, TW), L("t116", 64 * i + 32 * k, 32)),
-           L("gg", 1024 * plus + M * k, M), add)
+    def T1(r, i, k):
+        return L("t116", 320 * (r % 2) + 64 + 64 * i + 32 * k, 32)
 
-    def flags(i, turn):
-        for j in range(16):
-            mm(B(6, 0, 64), S("g14", 30 - j, 158 - j), S("gg", 1024 * i + j, 1024 * i + 1024, 16),
-               turn == 0 and j == 0, turn == 3 and j == 15, j == 15)
+    def second_places(r):
+        step("o0")
+        xbank = 6 if r else 0
+        if r:
+            mm(B(6, 0, 64), EYE, L("pb", 128 * r, 64), True, False)
+            mm(B(0, 64, 128), EYE, L("pb", 128 * r + 64, 64), True, False, True)
+        else:
+            mm(B(0, 0, 128), EYE, PB(r), True, False, True)
+        if r == 0:
+            for k in (ka, kb):
+                step("gr", k)
+                lin(L("gr", M * k, M), IND(L("tbn", TW * k, W), PN(0, k)))
+                step("tt", k)
+                tr(L("tt", M * k, M), L("gr", M * k, M))
+                fix(0, 64 + 32 * k, [(11 + 2 * k, 1)], M * k, M * k + M, "tt", 1, True, False)
+                fix(0, 32 * k, [(10 + 2 * k, 0)], M * k, M * k + M, "tt", 1, True, k == kb, True)
+        else:
+            for k in (ka, kb):
+                step("gr", k)
+                lin(L("gr", M * k, M), IND(L("tbn", TW * k, TW), T1(r, -1, k)), C("way%d" % k))
+            spread(0, 64, 6, "gr", 0, 64, False, True)
+            spread(6, 0, 5, "gr", 0, 64, False, True)
+        step("place")
+        place(0, 3, xbank)
 
-    def own_rows(b):
-        for i in range(16):
-            for j, q in enumerate((10, 12, 11, 13)):
-                end = i == 15 and j == 3
-                mm(B(b, i, 512, 16), L("di", 160 * i + 16 - (q - i), 128), L("own", 32 * j, 32), False, end, end)
+    def opening(b, r, k, offsets, p):
+        tp, ps = (0, 128) if k == ka else (64, 0)
+        mm(B(b, 0, 192), EYE, L("cb", offsets + 64 - tp, 192), True, False)
+        if r and k == ka and p < 3:
+            mm(B(b, 0, 32), EYE, S("dnb"), False, False)
+        mm(B(b, ps, ps + 64), S("em"), S("homu"), False, False)
+        mm(B(b, ps, ps + 32), EYE, L("pb", 128 * p + 32 * k, 32), False, False)
+        mm(B(b, ps + 32, ps + 64), S("e64"), L("pb", 128 * p + 64 + 32 * k, 32), False, False, True)
 
-    def tap(k, i):
-        return IND(L("xf", FW * k, FW - 8 * k), L("ts16", 64 * i + 32 * k, 32))
+    def second_visit(r, k):
+        bk, lo = BK[k], M * k
+        c, tp = (0, 0) if k == ka else (192, 64)
+        step("g2", k)
+        lin(L("g2", lo, M), IND(S("t2"), PN(3, k)))
+        step("tv", k)
+        tr(L("tv", lo, M), L("g2", lo, M))
+        b = bk["sec"]
+        step("o2", k)
+        opening(b, r, k, 448 if r else 256, 3)
+        if k == ka:
+            mm(B(6, 64, 96), EYE, L("cb", 512 if r else 320, 32), True, False, r == 0)
+            if r:
+                mm(B(6, 64, 96), EYE, S("dnb"), False, False, True)
+            step("x0", k)
+            fix(6, 64, [(8 * k, 1), (8 * k + 4, 0)], lo, lo + M, "tv", 1, True, True, True)
+        step("x2", k)
+        for i in range(k == ka, 4):
+            fix(b, tp + 32 * i, [(8 * k + i, 1), (8 * k + 4 + i, 0)], lo, lo + M, "tv", 1, True, i == 3, i == 3)
 
-    def AA(k, j):
-        return L("aa", M * (2 * k + j), M)
+    def missing(r, k):
+        b = BK[k]["flag"]
+        if r == 0:
+            step("f", k)
+            fix(b, 0, [(15, 0)], M * k, M * k + M, "tt", inc=True)
+        for i in range(4 if r else 0):
+            step("f%d" % i, k)
+            flags = IND(L("tbn", k * TW, TW), T1(r, i, k))
+            if i == SUMMED[k != ka] + 1:
+                tt(G(i, k), flags, G(i - 1, k), add)
+            else:
+                lin(G(i, k), flags)
+            if i != SUMMED[k != ka]:
+                spread(b, 0, 7, "gg", 2048 * k + M * i, 32, i == (SUMMED[k != ka] == 0), i == 3)
 
-    def DA(k, j):
-        return L("da", M * (2 * k + j), M)
+    def choose(r, k):
+        bk, lo = BK[k], M * k
+        c, tp, e = (0, 0, 0) if k == ka else (192, 64, 64)
+        step("ok", k)
+        lin(L("okb", 32 * k, 32), B(bk["flag"], 0, 32), 2.0)
+        b = bk["fst"]
+        step("o1", k)
+        opening(b, r, k, 0, r)
+        step("x1", k)
+        for i in range(4):
+            if r == 0:
+                fix(b, tp + 32 * i, [(i, 1), (4 + i, 0)], lo, lo + M, "tt", 1, True, False, i == 3)
+            else:
+                mm(B(b, tp + 32 * i, tp + 32 * i + 32), S("eyef"), L("t1f", 64 * i + 32 * k, 32), False, False, i == 3)
+        step("sp", k)
+        for i in range(6):
+            mm(B(b, 32 * i, 32 * i + 32), EYE, L("okb", 32 * k, 32), False, i == 5, i == 5)
+        step("c2", k)
+        lin(L("c2", c, 192), B(b, 0, 192))
+        a, end = 32 if k == ka else 0, float(2 * (TW if r else W))
+        if k == ka:
+            step("min0")
+            tt(L("sl", 0, 32), B(6, 64, 96), L("c2", 0, 32), mn)
+            step("ts0")
+            ts(L("ts16", 128 * k, 32), L("sl", 0, 32), end, mn)
+        step("min", k)
+        tt(L("sl", c + a, 192 - a), B(bk["sec"], a, 192), L("c2", c + a, 192 - a), mn)
+        step("ts", k)
+        ts(L("ts16", 128 * k + a, 128 - a), L("sl", c + tp + a, 128 - a), end, mn)
+        step("pa", k)
+        ts(L("pa", e, 64), L("sl", 128 + e, 64), 3, band)
+        step("uv", k)
+        ts(L("uv", e, 64), L("pa", e, 64), 0.25, mul, TINY, mx)
+        for b, a in ((bk["u"], e), (bk["v"], e + 32)):
+            for i in range(16):
+                mm(B(b, i, M, 16), S("boi", i, 2048, 16), L("uv", a, 32), True, True, i == 15)
 
-    H = M // 2
-    SA = [L("sa", 0, M), L("sa", M, M)]
-    EA = [L("ea", 0, M), L("ea", M, M)]
+    def tap(r, k, i):
+        win = L("xf", FW * k, FW) if r else L("xb", BW * k, BW)
+        return IND(win, L("ts16", 128 * k + 32 * i, 32))
+
+    def AA(k, j, a=0, n=M):
+        return L("aa", M * (2 * k + j) + a, n)
+
+    def DA(k, j, a=0, n=M):
+        return L("da", M * (2 * k + j) + a, n)
+
+    def P2(b, a):
+        return B(b, a, a + H)
+
+    def whole(**steps):
+        for name, operands in steps.items():
+            step(name)
+            tt(*operands)
+
+    ua, va, ub, vb = BK[ka]["u"], BK[ka]["v"], BK[kb]["u"], BK[kb]["v"]
 
     for r in range(3):
         last = r == 2
-        p1 = P1(r)
+        now[0] = r
+        second_places(r)
+        for k in (ka, kb):
+            missing(r, k)
+            second_visit(r, k)
+            choose(r, k)
         if r == 0:
-            shift_x(0, 0)
-            for k in (kn, kf):
-                mv(L("gr", M * k, M), IND(L("tbn", TW * k, W), PN(0, k)), k == kn)
-            shift_x(1, 0)
-            act(S("gn"), IND(S("tbo", 0, W), S("nb16", 32, 96)), ACT.Copy)
-            tr(S("tt"), S("gr"))
-            fix_flows(3, 0, 512)
-            late_constants(0)
-            position(3, p1, "p2", S("pl16"))
-            late_constants(1)
-            shift_t(3, 0)
-            shift_t(3, 1, False)
-            cast(kf, 0, True)
-            fix_taps(4, 64, False)
-            fix(6, 0, [(15, 0)], 0, 1024, True)
-            for k in range(2):
-                mv(L("gr", M * k, M), IND(L("t2", W * k, W), L("pl16", 32 * k, 32)), k == 0)
-            shift_x(2, 0, True, (0, 7))
-            shift_x(0, 1, True, (0, 7))
-            cast(kf, 1, True)
-            tr(S("tt"), S("gr"))
-            fix_taps(5, 0)
-            tr(S("tu"), S("gn"))
-            fix(3, 0, [(4, 1), (9, 0)], 0, 1024, True, "tu")
-            cp(S("t1f"), B(4, 64, 320))
-            tt(S("q2"), S(p1), S("p2"), sub)
+            step("nb")
+            lin(S("go", M, 3 * M), IND(S("tbo", 0, W), S("nb16", 32, 96)))
+            spread(6, 192, 4, "go", M, 64, True, True)
+            step("nr")
+            cp(S("nr16"), B(6, 192, 256))
+        if r == 0:
+            for k, name, f, d0, d1, at in ((ka, "A", ACT.Copy, 4, ua, 0), (kb, "B", ACT.Abs, 7, ub, M)):
+                a = [G(i, k) for i in range(4)]
+                u = L("g2", M * k, M)
+                step("u", k)
+                lin(u, B(d1))
+                for i in range(4):
+                    step(name + str(i))
+                    act(a[i], tap(r, k, i), f)
+                    if i % 2:
+                        mm(B((d0, d1)[i // 2]), EYE, a[i], True, False)
+                        mm(B((d0, d1)[i // 2]), S("em"), a[i - 1], False, True, True)
+                two = "2" * (k == kb)
+                whole(**{"m" + two: (B(d0), B(d0), u, mul), "s" + two: (L("sa", at, M), B(d0), a[0], add),
+                         "n" + two: (B(d1), B(d1), u, mul), "t" + two: (B(d1), B(d1), a[2], add)})
         else:
-            for k in range(2):
-                landed(L("tbn", k * TW + W, M), "st%d_%d" % (r - 1, k))
-            for k in (kn, kf):
-                mv(L("gr", M * k, M), IND(L("tbn", k * TW, TW), L("mp16", 32 * k, 32)), k == kn)
-                if k == kn:
-                    flag_unit(1, kf, True)
-                    flag_unit(0, kn, True)
-            for k in (kn, kf):
-                tr(L("tt", M * k, M), L("gr", M * k, M))
-                fix(3, 32 * k, [(10 + 2 * k, 0)], M * k, M * k + M, False)
-                fix(3, 64 + 32 * k, [(11 + 2 * k, 1)], M * k, M * k + M, True)
-            flag_unit(0, kf, True)
-            flag_sum(2, kf, 1, 2)
-            flag_unit(1, kn, True, 2)
-            flags(0, 0)
-            position(3, p1, "p2", S("pl16"))
-            flags(2, 1)
-            for k in range(2):
-                mv(L("gr", M * k, M), IND(L("t2", W * k, W), L("pl16", 32 * k, 32)), k == 0)
-            flag_unit(2, kn, True, 4)
-            tr(S("tt"), S("gr"))
-            fix_taps(5, 0)
-            tt(S("q2"), S(p1), S("p2"), sub)
-            flag_unit(3, kf, True)
-            flag_sum(3, kn, 4, 3)
-            flags(3, 3)
-            if r == 1:
-                position(1, "home", P1(2), PN(2))
-            else:
-                tt(S("yea"), B(2), S("yea"), add)
-            for k in (kn, kf):
-                for h in range(2):
-                    landed(L("xf", XA[k] + W + h * M // 2, M // 2), "vl%d_%d_%d" % (r - 1, k, h))
-        act(S("t2f"), B(5, 0, 256), ACT.Identity, bias=col("cf", 15))
-        for i in range(4):
-            tt(B(6, 64 + 64 * i, 128 + 64 * i), B(6, 0, 64), L("t1f", 64 * i, 64), add)
-        ts(S("ok"), B(6, 0, 64), 0.0, ALU.is_equal)
-        tt(S("tsf"), B(6, 64, 320), S("t2f"), mn)
-        tt(B(6, 320, 384), S("q2", 0, 64), S("ok"), mul)
-        if last:
-            tt(S("tsf", 0, 32), S("tsf", 0, 32), S("dn"), mx)
-        cp(S("ts16"), S("tsf"))
-        if r == 0:
-            shift_x(3, 0, True, (0, 7))
-        for j in range(2):
-            act(AA(0, j), tap(0, 2 * j), ACT.Copy)
-        if r == 0:
-            for c in (1, 2):
-                shift_x(c, 1, True, (5, 7))
-        tt(B(6, 384, 448), S("q2", 64, 128), S("ok"), mul)
-        ts(S("fh"), S("ok"), 0.5, mul, 0.5, add)
-        tt(S("pe"), B(6, 320, 448), S("p2"), add)
-        ts(S("fi"), S("ok"), 0.5 / 64, mul, 0.5 / 64, add)
-        ts(S("pa", 0, 64), S("pe", 0, 64), 3, band)
-        ts(S("pa", 64, 128), S("pe", 64, 128), 6, shr, 3, band)
-        ts(S("uv", 0, 64), S("pa", 0, 64), 0.25, mul, TINY, mx)
-        ts(S("uv", 64, 128), S("pa", 64, 128), 0.25, mul, TINY, mx)
-        tt(B(6, 64, 192), S("pe"), S("hom4"), sub)
-        if r == 0:
-            tt(S("nbm", 0, 32), B(3, 0, 32), S("lj"), sub)
-            tt(S("nbm", 32, 64), B(3, 32, 64), S("lj"), sub)
-        for b, a in ((0, 0), (1, 64), (2, 32), (3, 96)):
-            for i in range(16):
-                mm(B(b, i, 512, 16), L("boi", 128 * i, 128), L("uv", a, 32), True, True, i == 15)
-            if r == 0 and b == 1:
-                shift_x(3, 1, True, (5, 7))
-        act(AA(1, 0), tap(1, 0), ACT.Abs)
-        act(DA(1, 0), tap(1, 1), ACT.Abs)
-        tt(DA(0, 0), tap(0, 1), AA(0, 0), sub)
-        tt(S("q1", 0, 64), B(6, 64, 128), S("fh"), mul)
-        tt(S("q1", 64, 128), B(6, 128, 192), S("fi"), mul)
-        tt(DA(0, 1), tap(0, 3), AA(0, 1), sub)
-        tt(B(4), B(0), DA(0, 0), mul)
+            for j in range(2):
+                step("A%d" % (2 * j))
+                lin(AA(0, j), tap(r, ka, 2 * j))
+                step("D%d" % j)
+                tt(DA(0, j), tap(r, ka, 2 * j + 1), AA(0, j), sub)
+            whole(m=(B(4), B(ua), DA(0, 0), mul), n=(B(ua), B(ua), DA(0, 1), mul),
+                  s=(L("sa", 0, M), B(4), AA(0, 0), add), t=(B(ua), B(ua), AA(0, 1), add))
+            for j, b in enumerate((7, 4)):
+                step("B%d" % (2 * j + 1))
+                act(DA(1, j), tap(r, kb, 2 * j + 1), ACT.Abs)
+                step("B%d" % (2 * j))
+                act(AA(1, j), tap(r, kb, 2 * j), ACT.Abs)
+                mm(B(b), S("eyef"), DA(1, j), True, True, True)
+            whole(d0=(DA(1, 0), B(7), AA(1, 0), sub), m2=(B(7), B(ub), DA(1, 0), mul), s2=(L("sa", M, M), B(7), AA(1, 0), add),
+                  d1=(DA(1, 1), B(4), AA(1, 1), sub), n2=(B(ub), B(ub), DA(1, 1), mul), t2=(B(ub), B(ub), AA(1, 1), add))
+        whole(e=(L("ea", 0, M), B(ua), L("sa", 0, M), sub), w=(B(va), B(va), L("ea", 0, M), mul),
+              z=(S("z1"), B(va), L("sa", 0, M), add))
+        step("ee")
+        ts(S("ee"), S("sl", 128, 256), 2 * M - 1, band)
+        step("fh")
+        ts(S("fh"), S("sl", 128, 256), 0.0, ALU.is_lt, 0.5, mx)
+        step("q0")
+        ts(B(5, 0, 128), S("ee"), -M - 0.375, add)
+        step("q1")
+        tt(S("q1"), B(5, 0, 128), S("fh"), mul)
+        step("own")
         ts(S("own"), S("q1"), MAGIC, add, -MAGIC, add)
-        act(B(7), DA(1, 0), ACT.Copy)
-        tt(SA[0], B(4), AA(0, 0), add)
-        act(AA(1, 1), tap(1, 2), ACT.Abs)
-        act(DA(1, 1), tap(1, 3), ACT.Abs)
-        mm(B(5), CM(7), S("br"), True, False)
-        own_rows(5)
-        for a in (0, H):
-            tt(B(0, a, a + H), B(0, a, a + H), L("da", M + a, H), mul)
-        act(B(4), DA(1, 1), ACT.Copy)
-        if not last:
-            keys = S("xf")[1] + S("lv")[1] + ([("tbn", W, TW), ("tbn", TW + W, 2 * TW)] if r else [])
-            credit(keys, [near] if r == 0 else [near, far, op], r)
-        for a in (0, H):
-            tt(B(0, a, a + H), B(0, a, a + H), L("aa", M + a, H), add)
-        for a in (0, H):
-            tt(L("ea", a, H), B(0, a, a + H), L("sa", a, H), sub)
-        mm(B(6), CM(3 if last else 1), S("br"), True, False)
-        mm(B(6), CM(4 if last else 2), LAN, False, True, True)
-        if last:
-            act(S("old0"), S("val"), ACT.Relu)
-            act(S("eyef"), EYE, ACT.Copy)
-        else:
-            for k in range(2):
-                act(L("gn", M * k, M), IND(L("tbn", TW * k, W), PN(r + 1, k)), ACT.Copy)
-        tt(B(1, 0, H), B(1, 0, H), L("ea", 0, H), mul)
-        tt(DA(1, 0), B(7), AA(1, 0), sub)
-        tt(B(1, H, M), B(1, H, M), L("ea", H, H), mul)
-        for a in (0, H):
-            tt(B(0, a, a + H), B(2, a, a + H), L("da", 2 * M + a, H), mul)
-        CB = {0: B(7, 0, H), H: B(4, 0, H)}
-
-        def PB(b, a):
-            return B(b, a, a + H)
-
-        def step(name, a):
-            if name == "zf":
-                tt(L("zf", a, H), PB(1, a), L("sa", a, H), add)
-            elif name == "s":
-                tt(L("sa", M + a, H), PB(0, a), L("aa", 2 * M + a, H), add)
-            elif name == "d":
-                tt(L("da", 3 * M + a, H), PB(4, a), L("aa", 3 * M + a, H), sub)
-                if a:
-                    for c in (0, H):
-                        mm(CB[c], CM(0), L("tbo", W + c, H), True, False)
-                    if last:
-                        mm(B(1), S("eyef"), S("yea"), True, False)
-            elif name == "m":
-                tt(PB(2, a), PB(2, a), L("da", 3 * M + a, H), mul)
-            elif name == "t":
-                tt(PB(2, a), PB(2, a), L("aa", 3 * M + a, H), add)
-            elif name == "e":
-                tt(L("ea", M + a, H), PB(2, a), L("sa", M + a, H), sub)
-            elif name == "mz":
-                tt(PB(3, a), PB(3, a), L("ea", M + a, H), mul)
-            elif name == "z":
-                tt(PB(3, a), PB(3, a), L("sa", M + a, H), add)
-            elif name == "dif":
-                tt(L("dif", a, H), L("zf", a, H), PB(3, a), sub)
-                act(L("gap", a, H), L("dif", a, H), ACT.Abs)
-            elif name == "cmp":
-                ts(L("cmpb", a, H), L("gap", a, H), col("epsc", 0), ALU.is_le)
-                mm(CB[a], S("bo"), L("cmpb", a, H), False, True, True)
-            elif name == "won":
-                ts(L("won", a, H), CB[a], 25.0, ALU.is_ge)
-            elif name == "hf":
-                act(L("half", a, H), L("dif", a, H), ACT.Copy, scale=0.5)
-            elif name == "tg":
-                tr(L("tu", 2 * a, M), L("gn", 2 * a, M))
-            elif name == "ex":
-                act(L("ex", a, H), L("gap", a, H), ACT.Exp, scale=-1.0)
-                mm(PB(1, a), S("eyef"), L("ex", a, H), False, a > 0, True)
-            elif name == "hv":
-                tt(PB(0, a), PB(3, a), L("half", a, H), add)
-            elif name == "tw":
-                tt(L("tw", a, H), PB(5, a), L("won", a, H), mul)
-            elif name == "new" and last:
-                tt(L("newf", a, H), PB(6, a), L("tw", a, H), add)
-            elif name == "new":
-                tt(L("tbo", W + a, H), PB(6, a), L("tw", a, H), add)
-                if a:
-                    send(LAN, [(d, L("tbn", slot(rank, d) * TW + W, M), "st%d_%d" % (r, slot(rank, d)))
-                               for d in (far, near)], [cr(r, near), cr(r, far)] if r else [])
-            elif name == "yw":
-                tt(PB(0, a), PB(0, a), L("won", a, H), mul)
-            elif name == "y":
-                tt(L("yo", a, H), PB(0, a), L("old0", a, H), add)
-                dma("y", [((T.y[:, a:a + H], []), L("yo", a, H))])
-            elif name == "ye":
-                act(S("pen"), B(1), ACT.Copy)
-                dma("s", [((T.ye[:], []), S("pen"))])
-
-        order = "s0 s1 zf0 zf1 d0 d1 m0 m1 t0 t1 e0 e1 mz0 mz1 z0 z1 dif0 dif1 cmp0 cmp1 "
-        if last:
-            order += "hf0 hf1 won0 won1 hv0 hv1 ex0 ex1 yw0 yw1 y0 y1 ye0 tw0 tw1 new0 new1"
-        else:
-            order += "hf0 hf1 won0 won1 tw0 tw1 new0 new1 tg0 tg1 hv0"
-        for w in order.split():
-            step(w[:-1], H * int(w[-1]))
-        if last:
-            for q, rows in (("s", (0, 1, 2)), ("y", (3, 4))):
-                dma(q, [((T.yf[8 * j:8 * j + 8, :], []), S("newf", rows=slice(10 + j, 128, 16))) for j in rows])
-            break
-        for a in (0, H):
-            act(L("pen", a, H), CB[a], ACT.Relu, scale=-4.0 * BIG, bias=col("cf", 13))
-        tr(S("tt", 0, M), LAN)
-        fix(1, 0, [(4, 1), (9, 0)], 0, 1024, False, "tu")
-        fix(5, 0, [(14, 0)], 0, 512, True)
-        fix_taps(1, 64, True, "tu")
-        step("hv", H)
-        tt(S("nt", 0, 32), B(5, 0, 32), L("nbm", 32 * r, 32), mul)
-        tt(B(0, 0, H), B(0, 0, H), L("pen", 0, H), sub)
-        tt(S("nt", 32, 64), S("nt", 0, 32), S("lj"), add)
+        for i in range(16):
+            for j, q in enumerate((10 + 2 * ka, 11 + 2 * ka, 10 + 2 * kb, 11 + 2 * kb)):
+                mm(B(5, i, M, 16), S("di", i + 16 * (13 - q), i + 16 * (141 - q), 16), L("own", 32 * j, 32), j == 0, j == 3,
+                   i % 4 == 3 and j == 3)
         if r == 1:
-            ts(S("dn"), B(5, 0, 32), -2.0 * TW, mul, 2.0 * TW, add)
-        cp(S("nr16"), S("nt", 32, 64))
-        act(B(2), S("gap"), ACT.Exp, scale=-1.0)
-        gather_near(r + 1)
-        tt(B(0, H, M), B(0, H, M), L("pen", H, H), sub)
-        cp(S("mp16"), B(1, 0, 64))
-        cp(S("t116"), B(1, 64, 320))
-        for h, a in enumerate((0, H)):
-            tt(L("val", a, H), B(0, a, a + H), L("val", a, H), mx)
-            send(L("val", a, H),
-                 [(op, L("lv", a, H), "vl%d_2_%d" % (r, h)),
-                  (near, L("xf", XA[slot(rank, near)] + W + a, H), "vl%d_%d_%d" % (r, slot(rank, near), h))],
-                 [cr(r, near), cr(r, op)] if r else [cr(r, near)])
-        for h, a in enumerate((0, H)):
-            landed(L("lv", a, H), "vl%d_2_%d" % (r, h))
-            send(L("lv", a, H), [(near, L("xf", XA[slot(op, near)] + W + a, H), "vl%d_%d_%d" % (r, slot(op, near), h))])
-            dma("y", rolled(("xf", XA[2] + W + a), ("lv", a), 0, H) + rolled(("xf", XA[3] + W + a), ("lv", a), 1, H))
-        cp(S("t1f"), B(1, 64, 320))
+            credit(S("xf")[1] + [("tbn", W, TW), ("tbn", TW + W, 2 * TW)], [near, far, op])
+        step("rows")
+        lin(pair("sw", r, 1), B(5))
         if r == 0:
-            tr(S("tu", 0, 512), S("br"))
-            fix_flows(1, 0, 0, "tu")
-            tt(S("yea"), B(2), S("won"), mul)
+            select(S("vw", 0, 6 * M, 2), L("xf", XA[ka], 3 * M), [[0, 3 * M]], ALU.is_gt, -BIG, 0, 0)
+        if last:
+            step("yea")
+            act(S("yea"), IND(S("gw", 0, 2 * M + 16), S("ixg")), ACT.Exp, scale=-1.0)
+            calls[-1]["cost"]["s"] += FIRST_EXP
+            YE = (T.ye[:], [("ye", 0, M)], [], 0, None)
+            dma("y", [(YE, S("yea"))], 512 * M)
         else:
-            tt(B(2), B(2), S("won"), mul)
+            step("gn")
+            for k in range(2):
+                lin(L("gn", M * k, M), IND(L("tbn", TW * k, W), PN(r + 1, k)))
+            for i in range(5):
+                spread(6, 192 + 64 * ((i + 1) % 5), i, "gn", 0, 64, True, True)
+            step("t1f")
+            lin(S("t1f"), B(6, 256, 512))
+            step("t116")
+            cp(L("t116", 320 * ((r + 1) % 2), 320), B(6, 192, 512))
+        step("o3")
+        mm(B(6, 0, 32), S("eyef"), S("base"), True, False, True)
+        gap0 = M * r + (16 if last else 0)
+        for h, a in enumerate((0, H)):
+            zb, half = (P2(vb, a), L("half", a, H)) if ka == 0 else (L("z1", a, H), P2(va, a))
+            whole(**{"e2%d" % h: (L("ea", M + a, H), P2(ub, a), L("sa", M + a, H), sub),
+                     "w2%d" % h: (P2(vb, a), P2(vb, a), L("ea", M + a, H), mul),
+                     "z2%d" % h: (P2(vb, a), P2(vb, a), L("sa", M + a, H), add),
+                     "dif%d" % h: (L("dif", a, H), L("z1", a, H) if ka == 0 else P2(vb, a), zb, sub)})
+            step("gap%d" % h)
+            act(L("gw", gap0 + a, H), L("dif", a, H), ACT.Abs)
+            step("cmp%d" % h)
+            ts(L("cmpb", a, H), L("gw", gap0 + a, H), col("epsc", 0), ALU.is_le)
+            step("hf%d" % h)
+            lin(half, L("dif", a, H), 0.5)
+            step("hv%d" % h)
+            tt(pair("vw", r, 1, a, H), zb, half, add)
+            if last:
+                step("ex%d" % h)
+                act(L("yeo", a, H), L("gw", gap0 + a, H), ACT.Exp, scale=-1.0)
+        step("count")
+        for i in range(16):
+            mm(B(6, 0, 32), L("zc", 15 - i, 128), S("cmpb", i, M, 16), False, i == 15, i == 15)
+        step("idx")
+        ts(S("idx"), B(6, 0, 32), MAGIC, add, -MAGIC, add)
+        if last:
+            dma("g", [(YE, S("yeo"))], 1024 * M, accum_op=add)
+            step("y")
+            ts(S("val"), IND(S("vw"), S("idx")), 0.0, mx)
+            dma("y", [(HBM(T.y[:]), S("val"))], 512 * M)
+            step("yf")
+            lin(S("newf"), IND(S("sw"), S("idx")), C("fin"), col("mk", 14))
+            for q, rows in (("s", (0, 1, 2)), ("y", (3, 4))):
+                dma(q, [(HBM(T.yf[8 * j:8 * j + 8, :]), S("newf", rows=slice(10 + j, 128, 16))) for j in rows], 0)
+            break
+        for h in range(2):
+            step("state%d" % h)
+            lin(L("tbo", W + H * h, H), IND(S("sw", 0, 2 * M * (r + 1)), L("idx", 16 * h, 16)))
+        sent = send([(LAN, cores[d], L("tbn", slot(rank, d) * TW + W, M)[0], "st%d_%d" % (r, slot(rank, d))) for d in (far, near)],
+                    [cr(near), cr(far), cr(op)] if r else [])
+        for k in (ka, kb):
+            landed(L("tbn", k * TW + W, M), "st%d_%d" % (r, k), sent)
+        for h in range(2):
+            a = H * h
+            step("val%d" % h)
+            lin(L("val", a, H), IND(S("vw", 0, 2 * M * (r + 1)), L("idx", 16 * h, 16)))
+            mm(B(4 + 3 * h, 0, H), S("turn"), L("val", a, H), True, True, True)
+            step("rv%d" % h)
+            lin(L("rv", a, H), B(4 + 3 * h, 0, H))
+            sent = send([(L("rv", a, H), cores[op], L("xf", XA[2 + ka] + W + a, H)[0], "vo%d_%d" % (r, h)),
+                         (L("val", a, H), cores[near], L("xf", XA[slot(rank, near)] + W + a, H)[0], "vn%d_%d" % (r, h))])
+            landed(L("xf", XA[2 + ka] + W + a, H), "vo%d_%d" % (r, h), sent)
+            landed(L("xf", XA[ka] + W + a, H), "vn%d_%d" % (r, h), sent)
+        sent = send([(S("val"), cores[far], L("xf", XA[slot(rank, far)] + W, M)[0], "vf%d" % r)])
+        landed(L("xf", XA[kb] + W, M), "vf%d" % r, sent)
+        dma("y", rolled(XA[2 + kb] + W, XA[2 + ka] + W, M, (2, -2)[kb]), 512 * M)
+        step("near")
+        gather_near(r + 1)
+        step("done")
+        cp(S("ixi", 0, 32), S("idx"))
+        ts(S("ixi", 32, 64), S("ixi", 0, 32), 1, band)
+        ts(S("dnb"), S("ixi", 32, 64), FAR, mul)
+        step("base")
+        ts(S("ixf"), S("ixi", 32, 64), -2.0 * M, mul, 2.0 * M - 1.0 / 32, add)
+        tt(S("base"), S("ixi", 0, 32), S("ixf"), add)
+        if r == 0:
+            step("first2")
+            first_place(3, 2, pair("sw", 1, 0), 0)
+        else:
+            ts(S("ixg"), S("base"), 0.5, mul, 2.0 * M, mn)
 
+    for q in "vsp":
+        last = None
+        for r, name in [(r, name) for r in range(3) for name in ORDER[r][q].split()]:
+            r = r - 1 if name[0] == "-" else r
+            for j, c in enumerate(calls):
+                if c["step"] == (r, name.lstrip("-")) and q in c["cost"]:
+                    c["cost"] = {q: c["cost"][q]}
+                    if last is not None:
+                        c["after"].append((last, -WAKE))
+                    last = j
+    for j, q in put_in_order(calls):
+        calls[j]["emit"](q)
     for sem in ("v", "s", "p", "gp"):
         wait("g", (sem, cnt[sem]))
     for sem, val in owed.items():
         wait("g", (sem, val))
 
 
-DI_EARLY = 5
-XB = [(0, 1024), (1024, 512), (1536, 512)]
-BLOCKS = [(0, 512), (512, 512), (1024, 512), (1536, 256), (1792, 256)]
+TAIL = "e20 e21 w20 w21 z20 z21 dif0 dif1 cmp0 cmp1 hv0 hv1 "
+LATER = {"v": "gra -base f1a place g2a oka tva c2a min0 ts0 tvb mina tsa paa uva "
+              "D0 D1 m n s t minb tsb e w pab uvb z ee fh q0 d0 q1 own m2 d1 s2 n2 t2 " + TAIL,
+         "s": "grb f0a f2a f3a g2b f0b f1b A0 A2 f2b f3b okb c2b B1 B0 B3 B2 ",
+         "p": "o0 o1a x1a o1b x1b grb f1a f2a o2a f3a spa x0a x2a o2b x2b f0b uva f1b f2b f3b spb B0 uvb B2 own "}
+ORDER = [
+    {"v": "half tap00 tap01 tap10 tap11 tap20 tap21 grid tap30 tap31 tap40 tap41 out4 right zz turn0 zc first0 turn1 "
+          "gra tta ttb first1 place oka okb u4 g2a c2a tva min0 ts0 tvb mina tsa paa uva below c2b minb tsb pab uvb "
+          "ua m ee fh s n q0 t q1 e own m2 w s2 z n2 t2 " + TAIL + "idx state1 val0 val1 rv0 turn2 done rv1 t116 first2",
+     "s": "tap00 tap01 tap10 tap11 out0 tap20 tap21 out1 tap30 tap31 tap40 tap41 out2 out3 fx go home near0 cb "
+          "grb u0 u1 u2 u3 g2b dm0 dm1 A0 A1 A2 A3 B0 B1 ub B2 B3 nb gn rows gap0 gap1 hf0 hf1 state0 near t1f",
+     "p": "turn0 o0 o1a o1b turn1 u0 u1 tta ttb u2 u3 fa fb u4 x1a spa o2a o2b x0a x2a x1b spb x2b "
+          "uva A1 A3 uvb B1 B3 own nb gn o3 count val0 val1 turn2"},
+    {"v": LATER["v"] + "idx state1 val0 val1 rv0 done rv1 t116",
+     "s": LATER["s"] + "gn rows gap0 gap1 hf0 hf1 state0 near t1f",
+     "p": LATER["p"] + "gn o3 count val0 val1"},
+    {"v": LATER["v"] + "idx y",
+     "s": LATER["s"] + "yea rows gap0 gap1 hf0 hf1 ex0 ex1 yf",
+     "p": LATER["p"] + "o3 count"},
+]
+SUMMED = (0, -2)
+
+
+def hand_on_x(g, core, T, topo, far, op, k, bits, to_core, xb_at):
+    eng = topo.engines(core, far)
+    halves = [bits(eng[:len(eng) // 2]), bits(eng[len(eng) // 2:])]
+    n = len(eng) // 2
+    for c in range(W // XN):
+        hx = T["hx%d" % c]
+        for q, to, frm in ((g.sync, hx[0:16, :], hx[128:144, :]), (g.scalar, hx[144:160, :], hx[16:32, :])):
+            q.wait_ge(T.sem["hx%d" % c], n)
+            q.dma_start(to, frm).then_inc(T.sem["d%d" % c], 16)
+    for c in range(W // XN):
+        hx = T["hx%d" % c]
+        g.wait_ge(T.sem["hx%d" % c], n)
+        g.remote_dma_fused([RemoteDMATransfer(dst_ids=[to_core(far)], dma_engine_mask=halves[c], remote_sem=T.sem["x%d_%d" % (k, c)],
+                                              src=hx[16:144, :], dst=xb_at(k, 0, c))], local_sem=T.sem["l0"])
+    for c in range(W // XN):
+        hx = T["hx%d" % c]
+        g.wait_ge(T.sem["d%d" % c], 32)
+        g.remote_dma_fused([RemoteDMATransfer(dst_ids=[to_core(op)], dma_engine_mask=halves[j], remote_sem=T.sem["x%d_%d" % (2 + j, c)],
+                                              src=hx[32 - 32 * j:160 - 32 * j, :], dst=xb_at(j, 1, c)) for j in range(2)],
+                           local_sem=T.sem["l0"])
+    g.wait_ge(T.sem["l0"], 3 * n * (W // XN))

from concourse.bass import DstId, RemoteDMATransfer
from concourse.mybir import AluOpType as ALU, ActivationFunctionType as ACT

W, M, TW = 2048, 512, 2560
BIG = float(2.0 ** 96)
TINY = float(2.0 ** -46)
MAGIC = float(3 * 2 ** 22)
FAR = 8192.0
FW = 2 * TW + 8
BW = 2 * W + 16
XN = 1024
BLOCKS = [(0, 512), (512, 512), (1024, 512), (1536, 256), (1792, 256)]

CYCLE, PE_CYCLE, GATHER, SCATTER, WAKE = 0.83, 0.45, 1.56, 3.8, 100.0
ISSUE, DMA_START, LOCAL_RATE, REMOTE_RATE = 300.0, 1700.0, 300.0, 160.0
FIRST_EXP, SPARE, PASSES = 1300.0, 1.0, 6

F32, BF, I32, U16 = "float32", "bfloat16", "int32", "uint16"
SIZE = {F32: 4, BF: 2, I32: 4, U16: 2}
COLS = ("row grp b16 fv fq fb b1 b2 p hi tap lo flag even low keep up down ma tapc mb own t1 fto h0 h1 "
        "flow fin base0 cto lt14 lt10 way0 way1").split()


def _sb(n, dt):
    return ("sbuf", [128, n], dt)


SCRATCH = {
    "msi": _sb(32, I32), "cori": _sb(512, I32), "epsc": _sb(4, F32), "fli": _sb(M, I32), "flb": _sb(M, BF),
    "xo": _sb(W, BF), "ms16": _sb(32, U16), "cor16": _sb(512, U16), "mw": _sb(TW, BF), "gg": _sb(8192, BF),
    "tbo": _sb(TW, BF), "tbn": _sb(2 * TW, BF), "lt": _sb(W, BF), "t2": _sb(W, BF),
    "xb": _sb(2 * BW, BF), "xf": _sb(2 * FW, F32), "eyef": _sb(128, F32), "turn": _sb(128, F32), "rv": _sb(M, F32),
    "ia": _sb(160, I32), "iam": _sb(160, I32), "ir": _sb(64, F32),
    "ci": _sb(12, I32), "cf": _sb(40, F32), "mk": _sb(32, F32), "hc": _sb(48, BF), "m4": _sb(4, F32),
    "dd": _sb(160, BF), "sel": _sb(3 * 128, BF), "fx": _sb(4 * 160, BF), "e64": _sb(128, BF),
    "sf": _sb(5 * 128, BF), "zz": _sb(256, BF), "zc": _sb(144, BF), "cb": _sb(704, BF), "dm": _sb(8 * 144, BF),
    "wq": _sb(20, F32),
    "boi": _sb(16 * 128, BF), "di": _sb(2304, BF), "one": _sb(2304, BF), "ti": _sb(160, I32), "tj": _sb(96, I32),
    "homb": _sb(128, BF), "homu": _sb(64, BF), "em": _sb(128, BF), "nbi": _sb(96, I32), "nb16": _sb(96, U16), "nr16": _sb(64, U16),
    "gr": _sb(1024, BF), "g2": _sb(1024, BF), "gn": _sb(1024, BF), "go": _sb(1536, BF),
    "tt": _sb(1024, BF), "tv": _sb(1024, BF), "tu": _sb(1024, BF), "tw": _sb(2048, BF),
    "pb": _sb(512, BF), "cc": _sb(384, I32), "pn16": _sb(256, U16),
    "t1f": _sb(256, F32), "t116": _sb(640, U16), "c2": _sb(384, F32), "sl": _sb(384, I32), "ts16": _sb(256, U16),
    "okb": _sb(64, BF), "fh": _sb(128, F32), "ee": _sb(128, I32), "pa": _sb(128, I32), "uv": _sb(128, BF),
    "q0": _sb(128, F32), "q1": _sb(128, F32), "own": _sb(128, BF), "base": _sb(32, F32), "idx": _sb(32, U16),
    "ixi": _sb(64, I32), "ixf": _sb(32, F32), "dnb": _sb(32, BF), "ixg": _sb(32, U16),
    "sw": _sb(6 * M, BF), "vw": _sb(6 * M, F32), "gw": _sb(3 * M + 16, F32),
    "dif": _sb(M, F32), "cmpb": _sb(M, BF), "half": _sb(M, F32), "val": _sb(M, F32), "yea": _sb(M, F32),
    "yeo": _sb(M, F32), "newf": _sb(M, F32),
    "aa": _sb(4 * M, F32), "da": _sb(4 * M, F32), "sa": _sb(2 * M, F32), "ea": _sb(2 * M, F32), "z1": _sb(M, F32),
}
for _b in range(8):
    SCRATCH["b%d" % _b] = ("psum", [128, 512], F32)
for _c in range(W // XN):
    SCRATCH["hx%d" % _c] = ("dram", [160, XN], BF)

SEMAPHORES = (["v", "s", "p", "gp"] + ["d%d" % i for i in range(24)] + ["l%d" % i for i in range(36)]
              + ["e%d" % i for i in range(5)]
              + ["tb%d_%d" % (a, c) for a in range(2) for c in range(5)] + ["tc%d" % c for c in range(5)]
              + ["x%d_%d" % (a, c) for a in range(4) for c in range(2)] + ["hx0", "hx1"]
              + ["st%d_%d" % (r, a) for r in range(2) for a in range(2)]
              + ["v%s%d_%d" % (a, r, h) for a in "no" for r in range(2) for h in range(2)] + ["vf0", "vf1"]
              + ["cr%d" % a for a in range(3)])


def in_psum(name):
    return name in SCRATCH and SCRATCH[name][0] == "psum"


def put_in_order(calls):
    n = len(calls)
    before = [dict() for _ in calls]
    seen, last_pe = {}, {}
    for j, c in enumerate(calls):
        for i, extra in c["after"]:
            before[j][i] = extra
        for keys, isw in ((c["reads"], False), (c["writes"], True)):
            for name, lo, hi in keys:
                for a, b, w, i in seen.get(name, []):
                    if a < hi and lo < b and (w or isw):
                        before[j][i] = max(before[j].get(i, 0.0), 0.0)
                if in_psum(name) and "p" in c["cost"]:
                    if name in last_pe and last_pe[name] != j:
                        before[j].setdefault(last_pe[name], 0.0)
                    last_pe[name] = j
        for name, lo, hi in c["writes"]:
            seen[name] = [x for x in seen.get(name, []) if not (lo <= x[0] and x[1] <= hi)] + [(lo, hi, True, j)]
        for name, lo, hi in c["reads"]:
            seen.setdefault(name, []).append((lo, hi, False, j))
        before[j].pop(j, None)
    for j in range(n):
        for i in before[j]:
            before[j][i] += calls[i]["lat"] + WAKE
    for q in "gy":
        js = [j for j, c in enumerate(calls) if q in c["cost"]]
        for i, j in zip(js, js[1:]):
            before[j].setdefault(i, 0.0)
    banks = [sorted({k[0] for k in c["reads"] + c["writes"] if in_psum(k[0])}) for c in calls]

    def place(turns):
        busy, end, on = {}, [0.0] * n, [None] * n
        for j in turns:
            ready = max([0.0] + [end[i] + gap for i, gap in before[j].items()])
            best = None
            for q in calls[j]["cost"]:
                d, t, moved = calls[j]["cost"][q], ready, q != "n"
                while moved:
                    moved = False
                    for k in [q] + banks[j]:
                        spans = busy.get(k, [])
                        for a, b, who in spans[first_after(spans, t - WAKE):]:
                            pad = 0.0 if who == q else WAKE
                            if a - pad >= t + d:
                                break
                            if t < b + pad:
                                t, moved = b + pad, True
                score = t + d * (1 + SPARE if q == "v" else 1)
                if best is None or score < best[0]:
                    best = (score, t, d, q)
            _, t, d, q = best
            for k in [q] + banks[j]:
                spans = busy.setdefault(k, [])
                spans.insert(first_after(spans, t), (t, t + d, q))
            end[j], on[j] = t + d, q
        return end, on

    def first_after(spans, t):
        lo, hi = 0, len(spans)
        while lo < hi:
            mid = (lo + hi) // 2
            lo, hi = (mid + 1, hi) if spans[mid][1] <= t else (lo, mid)
        return lo

    turns, taken = [], set()

    def take(j):
        if j not in taken:
            taken.add(j)
            for i in sorted(before[j]):
                take(i)
            turns.append(j)
        assert j in turns

    for j in [j for j in range(n) if not calls[j]["aside"]] + list(range(n)):
        take(j)
    end, on = place(turns)
    return [(j, on[j]) for j in sorted(range(n), key=lambda j: (end[j] - calls[j]["cost"][on[j]], j))]


def rank_program(g, core, T, topo):
    N = len(T.cores)
    cores = list(T.cores)

    def same_chip(a, b):
        return cores[b] in topo.cores_of(cores[a])

    def slot(src, dst):
        return {1: 0, N - 1: 1, 2: 2}[(src - dst) % N]

    def ring(r):
        up, dn = (r + 1) % N, (r - 1) % N
        return (up, dn, (r + 2) % N) if same_chip(r, up) else (dn, up, (r + 2) % N)

    def helper(r):
        return [c for c in topo.cores_of(cores[ring(r)[1]]) if c not in cores and topo.die(c) == topo.die(cores[r])][0]

    def bits(engines):
        return sum(1 << e for e in engines)

    def to_core(c):
        rid, pid = topo.addr(c, core)
        return DstId(rid=rid, pnc=pid)

    def xb_at(k, second, c):
        a = BW * k + W * second + XN * c
        return T.xb[:, a:a + XN]

    rank = T.rank_of(core)
    if rank is None:
        for r in range(N):
            if helper(r) == core:
                hand_on_x(g, core, T, topo, cores[ring(r)[1]], cores[ring(r)[2]], slot(r, ring(r)[1]), bits, to_core, xb_at)
        return
    near, far, op = ring(rank)
    off_eng = topo.engines(core, cores[far])
    on_eng = [e for e in topo.engines(core, cores[near]) if e not in off_eng]
    NE = len(off_eng)
    ka, kb = slot(near, rank), slot(far, rank)

    def mask_to(c):
        return bits(on_eng if c in topo.cores_of(core) else off_eng)

    Q = {"v": g.vector, "s": g.scalar, "p": g.tensor, "g": g, "y": g.sync}
    SEM = {"v": "v", "s": "s", "p": "p", "g": "gp"}
    cnt = {"v": 0, "s": 0, "p": 0, "gp": 0}
    waited = {q: {} for q in Q}
    recs = {}
    owed = {}
    nxt = {"d": 0, "l": 0, "e": 0}
    calls = []
    pend = []
    now = [0, ""]
    aside = [False]

    def S(name, lo=None, hi=None, step=None, rows=None):
        t = T[name]
        lo = 0 if lo is None else lo
        hi = t.shape[1] if hi is None else hi
        r = slice(None) if rows is None else rows
        ap = t[r, lo:hi] if step is None else t[r, lo:hi:step]
        return (ap, [(name, lo, hi)], [], len(range(lo, hi, step or 1)), name)

    def L(name, lo, n):
        return S(name, lo, lo + n)

    def HBM(ap):
        return (ap, [], [], 0, None)

    def IND(win, off):
        return (win[0].indirect(off[0]), win[1], off[1], 16 * off[3], win[4])

    def wait(q, tok):
        sem, val = tok[0], tok[1]
        if waited[q].get(sem, 0) < val:
            Q[q].wait_ge(T.sem[sem], val)
            waited[q][sem] = val

    def deps(q, eng, reads, writes):
        need = {}
        for keys, isw in ((reads, False), (writes, True)):
            for (n, lo, hi) in keys:
                ps = in_psum(n)
                for (a, b, w, tok) in recs.get(n, []):
                    same = eng is not None and tok[2] == eng
                    if same and eng == "p":
                        continue
                    if (ps and not same) or (a < hi and lo < b and (w or isw)):
                        need[tok[0]] = max(need.get(tok[0], 0), tok[1])
        for sem, val in need.items():
            wait(q, (sem, val))

    def note(reads, writes, tok):
        for (n, lo, hi) in writes:
            recs[n] = [x for x in recs.get(n, []) if not (lo <= x[0] and x[1] <= hi)] + [(lo, hi, True, tok)]
        for (n, lo, hi) in reads:
            keep = [x for x in recs.get(n, []) if not (not x[2] and x[3][0] == tok[0] and lo <= x[0] and x[1] <= hi)]
            recs[n] = keep + [(lo, hi, False, tok)]

    def record(cost, emit, reads, writes, lat=0.0, after=()):
        calls.append(dict(cost=cost, emit=emit, reads=reads, writes=writes, lat=lat, after=list(after), aside=aside[0],
                          step=tuple(now)))
        return len(calls) - 1

    def step(name, k=None):
        now[1] = name if k is None else name + "ab"[k != ka]

    def ap(a):
        return a[0] if isinstance(a, tuple) else a

    def comp(forms, out, ins, twice=False):
        ops = [a for a in ins if isinstance(a, tuple)]
        reads = [k for a in ops for k in a[1] + a[2]] + out[2]
        short = all(SIZE[SCRATCH[a[4]][2]] == 2 for a in [out] + ops[:1])
        cost = {}
        for q in forms:
            if out[2] or (ops and ops[0][2]):
                cost[q] = 60 + out[3] * CYCLE * (SCATTER if out[2] else GATHER)
            elif q == "g":
                cost[q] = 130 + 2 * out[3] * CYCLE
            else:
                cost[q] = out[3] * (2 if twice else 0.5 if short and q == "v" else 1) * CYCLE + 60

        def emit(q):
            sem = SEM[q]
            deps(q, sem, reads, out[1])
            cnt[sem] += 1
            forms[q]().then_inc(T.sem[sem], 1)
            note(reads, out[1], (sem, cnt[sem], sem))
        record(cost, emit, reads, out[1])

    V = g.vector

    def cp(out, a):
        comp({"v": lambda: V.tensor_copy(out[0], a[0])}, out, [a])

    def tt(out, a, b, o):
        comp({"v": lambda: V.tensor_tensor(out[0], a[0], b[0], o)}, out, [a, b], not (in_psum(a[4]) or in_psum(b[4])))

    def ts_call(out, a, s1, o1, s2=None, o2=None):
        if o2 is None:
            return lambda: V.tensor_scalar(out[0], a[0], ap(s1), None, o1)
        return lambda: V.tensor_scalar(out[0], a[0], ap(s1), ap(s2), o1, o2)

    def ts(out, a, s1, o1, s2=None, o2=None):
        comp({"v": ts_call(out, a, s1, o1, s2, o2)}, out, [a, s1, s2])

    def ms(out, c):
        comp({"v": lambda: V.memset(out[0], c)}, out, [])

    def tr(out, a):
        comp({"v": lambda: V.transpose(out[0], a[0])}, out, [a])

    def act_call(out, a, f, scale=None, bias=None):
        kw = {}
        if scale is not None:
            kw["scale"] = ap(scale)
        if bias is not None:
            kw["bias"] = ap(bias)
        return lambda: g.scalar.activation(out[0], a[0], f, **kw)

    def act(out, a, f, scale=None, bias=None):
        comp({"s": act_call(out, a, f, scale, bias)}, out, [a, scale, bias])

    def lin(out, a, scale=None, bias=None, on="sv"):
        forms = {"s": act_call(out, a, ACT.Copy if bias is None else ACT.Identity, scale, bias)}
        if scale is None and bias is None:
            forms["v"] = lambda: V.tensor_copy(out[0], a[0])
        elif bias is None:
            forms["v"] = ts_call(out, a, scale, ALU.mult)
        elif scale is None:
            forms["v"] = ts_call(out, a, bias, ALU.add)
        else:
            forms["v"] = ts_call(out, a, scale, ALU.mult, bias, ALU.add)
        comp({q: forms[q] for q in on}, out, [a, scale, bias])

    def iota(out, pat, base, cmul, small=False):
        kw = {"allow_small_or_imprecise_dtypes": True} if small else {}
        comp({"g": lambda: g.iota(out[0], pat, base, cmul, **kw)}, out, [])

    def select(out, a, *how):
        comp({"g": lambda: g.affine_select(out[0], a[0], *how)}, out, [a])

    def mm(out, l, r, start, stop, inc=False):
        pend.append((out, l, r, start, stop))
        if not inc:
            return
        group = list(pend)
        del pend[:]
        reads = list({k for _, l, r, _, _ in group for k in l[1] + r[1]})
        writes = list({k for o in group for k in o[0][1]})

        def emit(q):
            ins = None
            for o, l, r, st, sp in group:
                deps("p", "p", l[1] + r[1], o[1])
                ins = g.tensor.matmul(o[0], l[0], r[0], st, sp)
            cnt["p"] += 1
            ins.then_inc(T.sem["p"], 1)
            note(reads, writes, ("p", cnt["p"], "p"))
        cost = sum(max(64, r[3]) * (4 if SCRATCH[l[4]][2] == F32 else 1) for _, l, r, _, _ in group) * PE_CYCLE
        record({"p": cost}, emit, reads, writes, 60.0)

    def dma(q, pairs, size, **kw):
        kind = "e" if q == "g" else "d"
        sem = "%s%d" % (kind, nxt[kind])
        nxt[kind] += 1
        rd = [k for _, i in pairs for k in i[1]]
        wr = [k for o, _ in pairs for k in o[1]]

        def emit(q):
            deps(q, None, rd, wr)
            for o, i in pairs:
                Q[q].dma_start(o[0], i[0], **kw).then_inc(T.sem[sem], 16)
            owed[sem] = 16 * len(pairs)
            note(rd, wr, (sem, 16 * len(pairs), None))
        record({q: (2 * ISSUE if q == "g" else 60.0) * len(pairs)}, emit, rd, wr, DMA_START + size / LOCAL_RATE)

    def send(items, before=(), wide=False):
        sem = "l%d" % nxt["l"]
        nxt["l"] += 1
        rd = [k for it in items for k in it[0][1]]
        n = len(on_eng + off_eng) if wide else NE * len(items)

        def emit(q):
            deps("g", None, rd, [])
            for t in before:
                wait("g", t)
            trs = [RemoteDMATransfer(dst_ids=[to_core(d)], dma_engine_mask=bits(on_eng + off_eng) if wide else mask_to(d),
                                     remote_sem=T.sem[rs], src=src[0], dst=land) for src, d, land, rs in items]
            g.remote_dma_fused(trs, local_sem=T.sem[sem])
            owed[sem] = n
            note(rd, [], (sem, n, None))
        src = items[0][0]
        return record({"g": ISSUE}, emit, rd, [], DMA_START + 128 * src[3] * SIZE[SCRATCH[src[4]][2]] / REMOTE_RATE)

    def landed(where, sem, like, extra=0.0, n=NE):
        def emit(q):
            owed[sem] = n
            note([], where[1], (sem, n, None))
        record({"n": 0.0}, emit, [], where[1], 0.0, [(like, extra)])

    def credit(keys, dests):
        for d in dests:
            sem = "l%d" % nxt["l"]
            nxt["l"] += 1

            def emit(q, d=d, sem=sem):
                deps("g", None, [], keys)
                rid, pid = topo.addr(cores[d], core)
                e = (on_eng if same_chip(rank, d) else off_eng)[0]
                g.remote_sem_update(T.sem["cr%d" % slot(rank, d)], T.sem[sem], pid, rid, 1 << e)
                owed[sem] = 1
            record({"g": ISSUE}, emit, [], keys)

    def cr(src):
        sem = "cr%d" % slot(src, rank)
        owed[sem] = 1
        return (sem, 1)

    def B(i, lo=0, hi=512, step=None):
        return S("b%d" % i, lo, hi, step)

    def col(name, j):
        return S(name, j, j + 1)

    def C(name):
        return col("cf", COLS.index(name))

    add, sub, mul, mx, mn = ALU.add, ALU.subtract, ALU.mult, ALU.max, ALU.min
    band, shr, eq = ALU.bitwise_and, ALU.arith_shift_right, ALU.is_equal
    EYE = S("dd", 16, 144)
    LAN = S("tbo", W, TW)
    XA = [0, FW, TW, FW + TW]
    H = M // 2

    dma("y", [(S("msi"), HBM(T.ms[:]))], 0)
    dma("s", [(S("xo", 0, XN), HBM(T.x[:, 0:XN]))], 256 * XN)
    dma("y", [(S("cori"), HBM(T.cor[:]))], 512 * M)
    dma("s", [(S("xo", XN, W), HBM(T.x[:, XN:W]))], 512 * XN)
    dma("y", [(S("fli"), HBM(T.fl[:]))], 1024 * M)
    dma("y", [(col("epsc", 0), HBM(T.eps[:]))], 0)
    IP = col("ci", 8)
    iota(IP, [[0, 1]], 0, 1)
    iota(S("ir"), [[1, 64]], 0, 0, True)
    iota(S("ia"), [[1, 160]], 0, -1)
    iota(S("ixf"), [[32, 32]], 0, 0, True)
    for c in range(W // XN):
        x = L("xo", XN * c, XN)
        sent = send([(x, helper(rank), T["hx%d" % c][16:144, :], "hx%d" % c),
                     (x, cores[near], xb_at(slot(rank, near), 0, c), "x%d_%d" % (slot(rank, near), c))])
        landed(L("xb", BW * ka + XN * c, XN), "x%d_%d" % (ka, c), sent)
        landed(L("xb", BW * kb + XN * c, XN), "x%d_%d" % (kb, c), sent, 2 * DMA_START)
        for k in range(2):
            landed(L("xb", BW * k + W + XN * c, XN), "x%d_%d" % (2 + k, c), sent, 3 * DMA_START)
    iota(S("one"), [[0, 2304]], 1, 0, True)

    aside[0] = True
    step("cb")
    a = 0
    for n, value in ((64, M - FAR), (128, 0), (64, M - FAR), (64, M), (128, W), (64, M), (128, TW), (64, M)):
        lin(L("cb", a, n), L("one", 0, n), float(value))
        a += n
    step("")
    ts(col("ci", 0), IP, 15, band)
    ts(col("ci", 1), IP, 4, shr)
    cp(S("cf", 0, 2), S("ci", 0, 2))
    ts(col("ci", 2), IP, 16, band)
    ts(col("ci", 3), IP, 2, shr, 7, band)
    ts(col("ci", 4), IP, 5, shr)
    ts(col("ci", 5), IP, 3, band)
    ts(col("ci", 6), IP, 1, band)
    ts(col("ci", 7), IP, 2, band)
    cp(S("cf", 2, 9), S("ci", 2, 9))
    ts(S("mk", 0, 16), S("ir", 0, 16), C("row"), eq)
    ts(S("m4"), S("ir", 0, 4), C("fb"), eq)
    for name, bound in (("hi", 4.0), ("tap", 8.0), ("lt10", 10.0), ("lt14", 14.0)):
        ts(C(name), C("row"), bound, ALU.is_lt)
    ts(C("even"), C("b1"), 0.0, eq, C("tap"), mul)
    ts(C("low"), C("b2"), 0.0, eq, C("tap"), mul)
    step("half")
    ts(C("h0"), C("b16"), 0.0, eq)
    ts(C("h1"), C("b16"), 0.0, ALU.is_gt)
    step("")
    for name, a, scale, bias in (
            ("lo", C("hi"), -1.0, C("tap")), ("flag", col("mk", 15), FAR, None),
            ("down", C("even"), -128.0, None),
            ("ma", C("low"), None, col("mk", 15)), ("tapc", C("tap"), None, col("mk", 15)), ("mb", C("low"), -1.0, C("tapc")),
            ("own", col("mk", 3), None, col("mk", 4)), ("t1", C("fv"), 16.0, C("fq")), ("fto", C("p"), -1.0, C("t1")),
            ("flow", C("lt10"), -1.0, C("lt14")),
            ("base0", C("row"), 2.0, -1.0 / 32), ("cto", C("row"), -1.0, 15.0), ("fin", col("mk", 14), -1.0, C("flow")),
            ("way0", col("mk", 10), None, col("mk", 11)), ("way1", col("mk", 12), None, col("mk", 13))):
        lin(C(name), a, scale, bias, "v" if name == "lo" else "s")

    lin(S("hc", 0, 48), S("ir", 0, 48), C("hi"), on="s")
    lin(S("mw", 0, 64), S("ir"), C("lo"), on="v")
    lin(col("hc", 33), col("hc", 32), bias=C("flag"), on="s")
    n = 64
    while n < W:
        lin(S("mw", n, 2 * n), S("mw", 0, n), bias=col("hc", n // 64), on="v")
        n *= 2
    lin(S("mw", W, TW), S("mw", 0, M), bias=col("hc", 33), on="s")
    for j in range(len(calls) - 6, len(calls)):
        calls[j]["aside"] = False
    aside[0] = False
    ts(S("dd"), S("ia"), 16.0, eq)
    cp(S("ms16"), S("msi"))
    ts(L("sf", 512, 128), S("ia", 0, 128), -10.0, add, C("fto"), eq)
    lin(C("keep"), C("even"), bias=col("mk", 15), on="s")
    lin(C("up"), C("even"), 128.0, on="s")
    lin(L("sel", 0, 128), EYE, C("ma"), on="s")
    lin(L("sel", 128, 128), EYE, C("mb"), on="s")
    lin(L("sel", 256, 128), S("dd", 11, 139), C("own"), on="s")
    for b in range(4):
        lin(L("sf", 128 * b, 128), L("sf", 512, 128), col("m4", b), on="s")
    cp(IND(S("mw", 0, W), S("ms16")), S("mw", W, TW))
    cp(S("cor16", 0, 128), S("cori", 0, 128))
    cp(S("cor16", 128, 512), S("cori", 128, 512))
    cp(S("flb"), S("fli"))
    aside[0] = True
    step("zz")
    ts(S("iam"), S("ia"), 127, band)
    for j, by in enumerate((112.0, 24.0)):
        ts(L("zz", 128 * j, 128), S("iam", 0, 128), by, eq, C("tap"), mul)
    step("fx")
    for h in range(2):
        lin(L("fx", 320 * h, 160), S("dd"), C("h%d" % h), on="s")
        lin(L("fx", 320 * h + 160, 160), L("fx", 320 * h, 160), 64.0, on="s")
    step("")
    lin(S("eyef"), EYE, on="s")
    step("zc")
    ts(S("zc"), S("ia", 0, 144), C("cto"), eq, 1.0 / 16, mul)
    ts(S("turn"), S("iam", 0, 128), (112.0, 16.0)[ka], eq)
    step("")
    lin(S("e64"), EYE, 1.0 / 64, on="s")
    lin(S("em"), EYE, -1.0, on="s")
    lin(S("mk", 16, 32), S("mk", 0, 16), 16.0, on="s")
    for q, (a, w, b) in enumerate(((0, 64.0, 4), (1, 64.0, 5), (2, 64.0, 6), (3, 64.0, 7), (8, 64.0, 9), (10, 1.0, 12), (11, 1.0, 13))):
        lin(col("wq", q), col("mk", 16 + a), w, col("mk", 16 + b), "s")
    lin(col("wq", 8), col("wq", 6), 64.0, on="s")
    lin(col("wq", 7), col("mk", 30), FAR, on="s")
    for q in range(8):
        step("dm%d" % (q // 4))
        lin(L("dm", 144 * q, 144), S("zc"), col("wq", 8 if q == 6 else q))
    step("")
    lin(S("base"), S("ixf"), bias=C("base0"), on="s")

    aside[0] = False

    def block_out(c):
        a, n = BLOCKS[c]
        step("out%d" % c)
        lin(L("tbo", a, n), B(c, 0, n), bias=C("down"))
        sent = send([(L("tbo", a, n), cores[d], L("tbn", slot(rank, d) * TW + a, n)[0], "tb%d_%d" % (slot(rank, d), c))
                     for d in (far, near)])
        for k in range(2):
            landed(L("tbn", k * TW + a, n), "tb%d_%d" % (k, c), sent)

    for c, (a, n) in enumerate(BLOCKS):
        for j in range(2):
            step("tap%d%d" % (c, j))
            lin(L("gg", W * (2 + j) + a, n), IND(S("mw", 0, W), L("cor16", 256 * j + a // 16, n // 16)), C("keep"), C("up"), "s")
            tt(L("gg", W * j + a, n), IND(S("mw", 0, W), L("cor16", 256 * j + 128 + a // 16, n // 16)),
               L("gg", W * (2 + j) + a, n), mx)
        mm(B(c, 0, n), L("sel", 256, 128), L("mw", a, n), True, False)
        mm(B(c, 0, n), L("sf", 128 * (a // M), 128), L("flb", a % M, n), False, False, True)
        for j in range(2):
            mm(B(c, 0, n), L("sel", 128 * j, 128), L("gg", W * j + a, n), False, j == 1, True)
        if c:
            block_out(c - 1)
    block_out(len(BLOCKS) - 1)

    def second_table():
        for c, (a, n) in enumerate(BLOCKS):
            sent = send([(L("tbn", kb * TW + a, n), cores[near], L("lt", a, n)[0], "tc%d" % c)], wide=True)
            landed(L("lt", a, n), "tc%d" % c, sent, n=len(on_eng + off_eng))
            b = (4, 7, 6, 4, 7)[c]
            step("u%d" % c)
            for j in range(2):
                mm(B(b, 0, n), L("zz", 128 * j, 128), L("lt", a, n), j == 0, j == 1, j == 1)
            lin(L("t2", a, n), B(b, 0, n))
        select(S("boi"), L("one", 0, 2048), [[16, 8], [0, 16], [1, 16]], eq, 0.0, 0, -1)
        for k in (ka, kb):
            for second in range(2):
                dma("g", [(L("xf", XA[k + 2 * second], W), L("xb", BW * k + W * second, W))], 1024 * W)
        select(S("di"), S("one"), [[16, 9], [1000, 16], [1, 16]], eq, 0.0, -13000, -1)

    def fix(bank, base, terms, lo, hi, src, step=1, opened=False, close=True, inc=False):
        n = (hi - lo) // 16
        for h in range(2):
            k = 0
            for e in range(2):
                for q, w in terms:
                    end = k == 2 * len(terms) - 1
                    fin = end and h == 1
                    mm(B(bank, base + step * h, base + step * (n - 1) + 1, 2 * step),
                       L("fx", 320 * h + 160 * w + 16 - 16 * (e - h), 128), S(src, lo + 16 * e + q, hi, 32),
                       k == 0 and not opened, (fin and close) if opened else end, inc and fin)
                    k += 1

    def PN(r, k):
        return L("pn16", 64 * r + 32 * k, 32)

    def PB(r):
        return L("pb", 128 * r, 128)

    def spread(bank, base, q, src, lo, n, start, stop):
        for i in range(16):
            mm(B(bank, base, base + n), L("dm", 144 * q + 15 - i, 128), S(src, lo + i, lo + 16 * n, 16),
               start and i == 0, stop and i == 15, i == 15)

    def place(bank, r, xbank):
        c = 192 * (r // 3)
        ts(L("cc", c, 64), B(bank, 64, 128), 0.0, mx, 127.0 * 64, mn)
        if xbank == bank:
            ts(L("pb", 128 * r, 64), B(xbank, 0, 64), 0.0, mx, 255.0, mn)
        else:
            ts(L("pb", 128 * r + 64, 64), B(bank, 64, 128), 0.0, mx, 127.0 * 64, mn)
        ts(L("cc", c + 64, 64), L("cc", c, 64), W * 4 - 256, band)
        if xbank == bank:
            ts(L("pb", 128 * r + 64, 64), B(bank, 64, 128), 0.0, mx, 127.0 * 64, mn)
        else:
            ts(L("pb", 128 * r, 64), B(xbank, 0, 64), 0.0, mx, 255.0, mn)
        tt(L("cc", c + 128, 64), L("cc", c + 64, 64), L("pb", 128 * r, 64), add)
        ts(L("pn16", 64 * r, 64), L("cc", c + 128, 64), -1.5, add, 0.25, mul)

    def first_place(bank, r, rows, lo):
        step("turn%d" % r)
        tr(L("tw", lo, M), rows)
        mm(B(bank, 0, 128), EYE, S("homb"), True, False)
        for j, (q, w) in enumerate(((10, 0), (12, 0), (11, 1), (13, 1))):
            fix(bank, 32 * j, [(q, w)], lo, lo + M, "tw", 1, True, j == 3, j == 3)
        step("first%d" % r)
        place(bank, r, bank)

    def pair(name, r, odd, a=0, n=M):
        return S(name, 2 * M * r + 2 * a + odd, 2 * M * r + 2 * a + 2 * n, 2)

    def gather_near(r):
        lin(pair("sw", r, 0), IND(S("tbo", 0, W if r == 0 else TW), S("nb16", 0, 32) if r == 0 else L("nr16", 32 * r - 32, 32)),
            C("flow"), col("mk", 14), "s")

    def rolled(dst, src, n, by):
        s = 16 * (by % 8)
        return [(S("xf", dst, dst + n, rows=slice(a, b)), S("xf", src, src + n, rows=slice(c, c + b - a)))
                for a, b, c in ((0, 128 - s, s), (128 - s, 128, 0))]

    def fill(out, value):
        comp({"s": act_call(out, S("mw", 0, out[3]), ACT.Identity, 0.0, value), "v": lambda: V.memset(out[0], value)},
             out, [S("mw", 0, out[3])])

    aside[0] = True
    step("grid")
    ts(S("tj", 32, 64), S("msi"), 63, band)
    ts(S("tj", 64, 96), S("msi"), 6, shr)
    ts(S("homu"), S("tj", 32, 96), 4.0, mul)
    step("home")
    for j in range(4):
        lin(L("homb", 32 * j, 32), L("homu", 32 * (j // 2), 32), (1.0, 64.0)[j // 2], on="s")
    step("right")
    ts(S("ti", 0, 32), S("msi"), 1.0, add)
    ts(S("ti", 96, 128), S("msi"), W - 64, band)
    ts(S("tj", 0, 32), S("ti", 0, 32), 63, band)
    ts(S("ti", 32, 64), S("msi"), 64.0, add)
    tt(S("nbi", 0, 32), S("tj", 0, 32), S("ti", 96, 128), add)
    ts(S("ti", 64, 96), S("msi"), 63.0, add)
    cp(S("nb16", 0, 32), S("nbi", 0, 32))
    step("below")
    ts(S("ti", 128, 160), S("ti", 64, 96), 63, band)
    ts(S("nbi", 32, 64), S("ti", 32, 64), W - 1, band)
    tt(S("nbi", 64, 96), S("ti", 128, 160), S("ti", 96, 128), add)
    cp(S("nb16", 32, 96), S("nbi", 32, 96))
    step("")
    for k in range(2):
        fill(L("xb", BW * k + 2 * W, 16), -BIG)
        fill(L("xf", FW * k + 2 * TW, 8), -BIG)
    fill(L("gw", 2 * M, 16), BIG)
    aside[0] = False
    step("go")
    lin(S("go", 0, M), IND(S("tbo", 0, W), S("ms16")))
    first_place(1, 0, S("go", 0, M), 0)
    step("near0")
    gather_near(0)
    first_place(5, 1, pair("sw", 0, 0), M)
    second_table()

    BK = {ka: dict(pos=0, flag=1, sec=4, fst=2, u=0, v=1), kb: dict(pos=6, flag=5, sec=7, fst=3, u=2, v=3)}

    def G(j, k):
        return L("gg", 2048 * k + M * j, M)

    def T1(r, i, k):
        return L("t116", 320 * (r % 2) + 64 + 64 * i + 32 * k, 32)

    def second_places(r):
        step("o0")
        xbank = 6 if r else 0
        if r:
            mm(B(6, 0, 64), EYE, L("pb", 128 * r, 64), True, False)
            mm(B(0, 64, 128), EYE, L("pb", 128 * r + 64, 64), True, False, True)
        else:
            mm(B(0, 0, 128), EYE, PB(r), True, False, True)
        if r == 0:
            for k in (ka, kb):
                step("gr", k)
                lin(L("gr", M * k, M), IND(L("tbn", TW * k, W), PN(0, k)))
                step("tt", k)
                tr(L("tt", M * k, M), L("gr", M * k, M))
                fix(0, 64 + 32 * k, [(11 + 2 * k, 1)], M * k, M * k + M, "tt", 1, True, False)
                fix(0, 32 * k, [(10 + 2 * k, 0)], M * k, M * k + M, "tt", 1, True, k == kb, True)
        else:
            for k in (ka, kb):
                step("gr", k)
                lin(L("gr", M * k, M), IND(L("tbn", TW * k, TW), T1(r, -1, k)), C("way%d" % k))
            spread(0, 64, 6, "gr", 0, 64, False, True)
            spread(6, 0, 5, "gr", 0, 64, False, True)
        step("place")
        place(0, 3, xbank)

    def opening(b, r, k, offsets, p):
        tp, ps = (0, 128) if k == ka else (64, 0)
        mm(B(b, 0, 192), EYE, L("cb", offsets + 64 - tp, 192), True, False)
        if r and k == ka and p < 3:
            mm(B(b, 0, 32), EYE, S("dnb"), False, False)
        mm(B(b, ps, ps + 64), S("em"), S("homu"), False, False)
        mm(B(b, ps, ps + 32), EYE, L("pb", 128 * p + 32 * k, 32), False, False)
        mm(B(b, ps + 32, ps + 64), S("e64"), L("pb", 128 * p + 64 + 32 * k, 32), False, False, True)

    def second_visit(r, k):
        bk, lo = BK[k], M * k
        c, tp = (0, 0) if k == ka else (192, 64)
        step("g2", k)
        lin(L("g2", lo, M), IND(S("t2"), PN(3, k)))
        step("tv", k)
        tr(L("tv", lo, M), L("g2", lo, M))
        b = bk["sec"]
        step("o2", k)
        opening(b, r, k, 448 if r else 256, 3)
        if k == ka:
            mm(B(6, 64, 96), EYE, L("cb", 512 if r else 320, 32), True, False, r == 0)
            if r:
                mm(B(6, 64, 96), EYE, S("dnb"), False, False, True)
            step("x0", k)
            fix(6, 64, [(8 * k, 1), (8 * k + 4, 0)], lo, lo + M, "tv", 1, True, True, True)
        step("x2", k)
        for i in range(k == ka, 4):
            fix(b, tp + 32 * i, [(8 * k + i, 1), (8 * k + 4 + i, 0)], lo, lo + M, "tv", 1, True, i == 3, i == 3)

    def missing(r, k):
        b = BK[k]["flag"]
        if r == 0:
            step("f", k)
            fix(b, 0, [(15, 0)], M * k, M * k + M, "tt", inc=True)
        for i in range(4 if r else 0):
            step("f%d" % i, k)
            flags = IND(L("tbn", k * TW, TW), T1(r, i, k))
            if i == SUMMED[k != ka] + 1:
                tt(G(i, k), flags, G(i - 1, k), add)
            else:
                lin(G(i, k), flags)
            if i != SUMMED[k != ka]:
                spread(b, 0, 7, "gg", 2048 * k + M * i, 32, i == (SUMMED[k != ka] == 0), i == 3)

    def choose(r, k):
        bk, lo = BK[k], M * k
        c, tp, e = (0, 0, 0) if k == ka else (192, 64, 64)
        step("ok", k)
        lin(L("okb", 32 * k, 32), B(bk["flag"], 0, 32), 2.0)
        b = bk["fst"]
        step("o1", k)
        opening(b, r, k, 0, r)
        step("x1", k)
        for i in range(4):
            if r == 0:
                fix(b, tp + 32 * i, [(i, 1), (4 + i, 0)], lo, lo + M, "tt", 1, True, False, i == 3)
            else:
                mm(B(b, tp + 32 * i, tp + 32 * i + 32), S("eyef"), L("t1f", 64 * i + 32 * k, 32), False, False, i == 3)
        step("sp", k)
        for i in range(6):
            mm(B(b, 32 * i, 32 * i + 32), EYE, L("okb", 32 * k, 32), False, i == 5, i == 5)
        step("c2", k)
        lin(L("c2", c, 192), B(b, 0, 192))
        a, end = 32 if k == ka else 0, float(2 * (TW if r else W))
        if k == ka:
            step("min0")
            tt(L("sl", 0, 32), B(6, 64, 96), L("c2", 0, 32), mn)
            step("ts0")
            ts(L("ts16", 128 * k, 32), L("sl", 0, 32), end, mn)
        step("min", k)
        tt(L("sl", c + a, 192 - a), B(bk["sec"], a, 192), L("c2", c + a, 192 - a), mn)
        step("ts", k)
        ts(L("ts16", 128 * k + a, 128 - a), L("sl", c + tp + a, 128 - a), end, mn)
        step("pa", k)
        ts(L("pa", e, 64), L("sl", 128 + e, 64), 3, band)
        step("uv", k)
        ts(L("uv", e, 64), L("pa", e, 64), 0.25, mul, TINY, mx)
        for b, a in ((bk["u"], e), (bk["v"], e + 32)):
            for i in range(16):
                mm(B(b, i, M, 16), S("boi", i, 2048, 16), L("uv", a, 32), True, True, i == 15)

    def tap(r, k, i):
        win = L("xf", FW * k, FW) if r else L("xb", BW * k, BW)
        return IND(win, L("ts16", 128 * k + 32 * i, 32))

    def AA(k, j, a=0, n=M):
        return L("aa", M * (2 * k + j) + a, n)

    def DA(k, j, a=0, n=M):
        return L("da", M * (2 * k + j) + a, n)

    def P2(b, a):
        return B(b, a, a + H)

    def whole(**steps):
        for name, operands in steps.items():
            step(name)
            tt(*operands)

    ua, va, ub, vb = BK[ka]["u"], BK[ka]["v"], BK[kb]["u"], BK[kb]["v"]

    for r in range(3):
        last = r == 2
        now[0] = r
        second_places(r)
        for k in (ka, kb):
            missing(r, k)
            second_visit(r, k)
            choose(r, k)
        if r == 0:
            step("nb")
            lin(S("go", M, 3 * M), IND(S("tbo", 0, W), S("nb16", 32, 96)))
            spread(6, 192, 4, "go", M, 64, True, True)
            step("nr")
            cp(S("nr16"), B(6, 192, 256))
        if r == 0:
            for k, name, f, d0, d1, at in ((ka, "A", ACT.Copy, 4, ua, 0), (kb, "B", ACT.Abs, 7, ub, M)):
                a = [G(i, k) for i in range(4)]
                u = L("g2", M * k, M)
                step("u", k)
                lin(u, B(d1))
                for i in range(4):
                    step(name + str(i))
                    act(a[i], tap(r, k, i), f)
                    if i % 2:
                        mm(B((d0, d1)[i // 2]), EYE, a[i], True, False)
                        mm(B((d0, d1)[i // 2]), S("em"), a[i - 1], False, True, True)
                two = "2" * (k == kb)
                whole(**{"m" + two: (B(d0), B(d0), u, mul), "s" + two: (L("sa", at, M), B(d0), a[0], add),
                         "n" + two: (B(d1), B(d1), u, mul), "t" + two: (B(d1), B(d1), a[2], add)})
        else:
            for j in range(2):
                step("A%d" % (2 * j))
                lin(AA(0, j), tap(r, ka, 2 * j))
                step("D%d" % j)
                tt(DA(0, j), tap(r, ka, 2 * j + 1), AA(0, j), sub)
            whole(m=(B(4), B(ua), DA(0, 0), mul), n=(B(ua), B(ua), DA(0, 1), mul),
                  s=(L("sa", 0, M), B(4), AA(0, 0), add), t=(B(ua), B(ua), AA(0, 1), add))
            for j, b in enumerate((7, 4)):
                step("B%d" % (2 * j + 1))
                act(DA(1, j), tap(r, kb, 2 * j + 1), ACT.Abs)
                step("B%d" % (2 * j))
                act(AA(1, j), tap(r, kb, 2 * j), ACT.Abs)
                mm(B(b), S("eyef"), DA(1, j), True, True, True)
            whole(d0=(DA(1, 0), B(7), AA(1, 0), sub), m2=(B(7), B(ub), DA(1, 0), mul), s2=(L("sa", M, M), B(7), AA(1, 0), add),
                  d1=(DA(1, 1), B(4), AA(1, 1), sub), n2=(B(ub), B(ub), DA(1, 1), mul), t2=(B(ub), B(ub), AA(1, 1), add))
        whole(e=(L("ea", 0, M), B(ua), L("sa", 0, M), sub), w=(B(va), B(va), L("ea", 0, M), mul),
              z=(S("z1"), B(va), L("sa", 0, M), add))
        step("ee")
        ts(S("ee"), S("sl", 128, 256), 2 * M - 1, band)
        step("fh")
        ts(S("fh"), S("sl", 128, 256), 0.0, ALU.is_lt, 0.5, mx)
        step("q0")
        ts(B(5, 0, 128), S("ee"), -M - 0.375, add)
        step("q1")
        tt(S("q1"), B(5, 0, 128), S("fh"), mul)
        step("own")
        ts(S("own"), S("q1"), MAGIC, add, -MAGIC, add)
        for i in range(16):
            for j, q in enumerate((10 + 2 * ka, 11 + 2 * ka, 10 + 2 * kb, 11 + 2 * kb)):
                mm(B(5, i, M, 16), S("di", i + 16 * (13 - q), i + 16 * (141 - q), 16), L("own", 32 * j, 32), j == 0, j == 3,
                   i % 4 == 3 and j == 3)
        if r == 1:
            credit(S("xf")[1] + [("tbn", W, TW), ("tbn", TW + W, 2 * TW)], [near, far, op])
        step("rows")
        lin(pair("sw", r, 1), B(5))
        if r == 0:
            select(S("vw", 0, 6 * M, 2), L("xf", XA[ka], 3 * M), [[0, 3 * M]], ALU.is_gt, -BIG, 0, 0)
        if last:
            step("yea")
            act(S("yea"), IND(S("gw", 0, 2 * M + 16), S("ixg")), ACT.Exp, scale=-1.0)
            calls[-1]["cost"]["s"] += FIRST_EXP
            YE = (T.ye[:], [("ye", 0, M)], [], 0, None)
            dma("y", [(YE, S("yea"))], 512 * M)
        else:
            step("gn")
            for k in range(2):
                lin(L("gn", M * k, M), IND(L("tbn", TW * k, W), PN(r + 1, k)))
            for i in range(5):
                spread(6, 192 + 64 * ((i + 1) % 5), i, "gn", 0, 64, True, True)
            step("t1f")
            lin(S("t1f"), B(6, 256, 512))
            step("t116")
            cp(L("t116", 320 * ((r + 1) % 2), 320), B(6, 192, 512))
        step("o3")
        mm(B(6, 0, 32), S("eyef"), S("base"), True, False, True)
        gap0 = M * r + (16 if last else 0)
        for h, a in enumerate((0, H)):
            zb, half = (P2(vb, a), L("half", a, H)) if ka == 0 else (L("z1", a, H), P2(va, a))
            whole(**{"e2%d" % h: (L("ea", M + a, H), P2(ub, a), L("sa", M + a, H), sub),
                     "w2%d" % h: (P2(vb, a), P2(vb, a), L("ea", M + a, H), mul),
                     "z2%d" % h: (P2(vb, a), P2(vb, a), L("sa", M + a, H), add),
                     "dif%d" % h: (L("dif", a, H), L("z1", a, H) if ka == 0 else P2(vb, a), zb, sub)})
            step("gap%d" % h)
            act(L("gw", gap0 + a, H), L("dif", a, H), ACT.Abs)
            step("cmp%d" % h)
            ts(L("cmpb", a, H), L("gw", gap0 + a, H), col("epsc", 0), ALU.is_le)
            step("hf%d" % h)
            lin(half, L("dif", a, H), 0.5)
            step("hv%d" % h)
            tt(pair("vw", r, 1, a, H), zb, half, add)
            if last:
                step("ex%d" % h)
                act(L("yeo", a, H), L("gw", gap0 + a, H), ACT.Exp, scale=-1.0)
        step("count")
        for i in range(16):
            mm(B(6, 0, 32), L("zc", 15 - i, 128), S("cmpb", i, M, 16), False, i == 15, i == 15)
        step("idx")
        ts(S("idx"), B(6, 0, 32), MAGIC, add, -MAGIC, add)
        if last:
            dma("g", [(YE, S("yeo"))], 1024 * M, accum_op=add)
            step("y")
            ts(S("val"), IND(S("vw"), S("idx")), 0.0, mx)
            dma("y", [(HBM(T.y[:]), S("val"))], 512 * M)
            step("yf")
            lin(S("newf"), IND(S("sw"), S("idx")), C("fin"), col("mk", 14))
            for q, rows in (("s", (0, 1, 2)), ("y", (3, 4))):
                dma(q, [(HBM(T.yf[8 * j:8 * j + 8, :]), S("newf", rows=slice(10 + j, 128, 16))) for j in rows], 0)
            break
        for h in range(2):
            step("state%d" % h)
            lin(L("tbo", W + H * h, H), IND(S("sw", 0, 2 * M * (r + 1)), L("idx", 16 * h, 16)))
        sent = send([(LAN, cores[d], L("tbn", slot(rank, d) * TW + W, M)[0], "st%d_%d" % (r, slot(rank, d))) for d in (far, near)],
                    [cr(near), cr(far), cr(op)] if r else [])
        for k in (ka, kb):
            landed(L("tbn", k * TW + W, M), "st%d_%d" % (r, k), sent)
        for h in range(2):
            a = H * h
            step("val%d" % h)
            lin(L("val", a, H), IND(S("vw", 0, 2 * M * (r + 1)), L("idx", 16 * h, 16)))
            mm(B(4 + 3 * h, 0, H), S("turn"), L("val", a, H), True, True, True)
            step("rv%d" % h)
            lin(L("rv", a, H), B(4 + 3 * h, 0, H))
            sent = send([(L("rv", a, H), cores[op], L("xf", XA[2 + ka] + W + a, H)[0], "vo%d_%d" % (r, h)),
                         (L("val", a, H), cores[near], L("xf", XA[slot(rank, near)] + W + a, H)[0], "vn%d_%d" % (r, h))])
            landed(L("xf", XA[2 + ka] + W + a, H), "vo%d_%d" % (r, h), sent)
            landed(L("xf", XA[ka] + W + a, H), "vn%d_%d" % (r, h), sent)
        sent = send([(S("val"), cores[far], L("xf", XA[slot(rank, far)] + W, M)[0], "vf%d" % r)])
        landed(L("xf", XA[kb] + W, M), "vf%d" % r, sent)
        dma("y", rolled(XA[2 + kb] + W, XA[2 + ka] + W, M, (2, -2)[kb]), 512 * M)
        step("near")
        gather_near(r + 1)
        step("done")
        cp(S("ixi", 0, 32), S("idx"))
        ts(S("ixi", 32, 64), S("ixi", 0, 32), 1, band)
        ts(S("dnb"), S("ixi", 32, 64), FAR, mul)
        step("base")
        ts(S("ixf"), S("ixi", 32, 64), -2.0 * M, mul, 2.0 * M - 1.0 / 32, add)
        tt(S("base"), S("ixi", 0, 32), S("ixf"), add)
        if r == 0:
            step("first2")
            first_place(3, 2, pair("sw", 1, 0), 0)
        else:
            ts(S("ixg"), S("base"), 0.5, mul, 2.0 * M, mn)

    for q in "vsp":
        last = None
        for r, name in [(r, name) for r in range(3) for name in ORDER[r][q].split()]:
            r = r - 1 if name[0] == "-" else r
            for j, c in enumerate(calls):
                if c["step"] == (r, name.lstrip("-")) and q in c["cost"]:
                    c["cost"] = {q: c["cost"][q]}
                    if last is not None:
                        c["after"].append((last, -WAKE))
                    last = j
    for j, q in put_in_order(calls):
        calls[j]["emit"](q)
    for sem in ("v", "s", "p", "gp"):
        wait("g", (sem, cnt[sem]))
    for sem, val in owed.items():
        wait("g", (sem, val))


TAIL = "e20 e21 w20 w21 z20 z21 dif0 dif1 cmp0 cmp1 hv0 hv1 "
LATER = {"v": "gra -base f1a place g2a oka tva c2a min0 ts0 tvb mina tsa paa uva "
              "D0 D1 m n s t minb tsb e w pab uvb z ee fh q0 d0 q1 own m2 d1 s2 n2 t2 " + TAIL,
         "s": "grb f0a f2a f3a g2b f0b f1b A0 A2 f2b f3b okb c2b B1 B0 B3 B2 ",
         "p": "o0 o1a x1a o1b x1b grb f1a f2a o2a f3a spa x0a x2a o2b x2b f0b uva f1b f2b f3b spb B0 uvb B2 own "}
ORDER = [
    {"v": "half tap00 tap01 tap10 tap11 tap20 tap21 grid tap30 tap31 tap40 tap41 out4 right zz turn0 zc first0 turn1 "
          "gra tta ttb first1 place oka okb u4 g2a c2a tva min0 ts0 tvb mina tsa paa uva below c2b minb tsb pab uvb "
          "ua m ee fh s n q0 t q1 e own m2 w s2 z n2 t2 " + TAIL + "idx state1 val0 val1 rv0 turn2 done rv1 t116 first2",
     "s": "tap00 tap01 tap10 tap11 out0 tap20 tap21 out1 tap30 tap31 tap40 tap41 out2 out3 fx go home near0 cb "
          "grb u0 u1 u2 u3 g2b dm0 dm1 A0 A1 A2 A3 B0 B1 ub B2 B3 nb gn rows gap0 gap1 hf0 hf1 state0 near t1f",
     "p": "turn0 o0 o1a o1b turn1 u0 u1 tta ttb u2 u3 fa fb u4 x1a spa o2a o2b x0a x2a x1b spb x2b "
          "uva A1 A3 uvb B1 B3 own nb gn o3 count val0 val1 turn2"},
    {"v": LATER["v"] + "idx state1 val0 val1 rv0 done rv1 t116",
     "s": LATER["s"] + "gn rows gap0 gap1 hf0 hf1 state0 near t1f",
     "p": LATER["p"] + "gn o3 count val0 val1"},
    {"v": LATER["v"] + "idx y",
     "s": LATER["s"] + "yea rows gap0 gap1 hf0 hf1 ex0 ex1 yf",
     "p": LATER["p"] + "o3 count"},
]
SUMMED = (0, -2)


def hand_on_x(g, core, T, topo, far, op, k, bits, to_core, xb_at):
    eng = topo.engines(core, far)
    halves = [bits(eng[:len(eng) // 2]), bits(eng[len(eng) // 2:])]
    n = len(eng) // 2
    for c in range(W // XN):
        hx = T["hx%d" % c]
        for q, to, frm in ((g.sync, hx[0:16, :], hx[128:144, :]), (g.scalar, hx[144:160, :], hx[16:32, :])):
            q.wait_ge(T.sem["hx%d" % c], n)
            q.dma_start(to, frm).then_inc(T.sem["d%d" % c], 16)
    for c in range(W // XN):
        hx = T["hx%d" % c]
        g.wait_ge(T.sem["hx%d" % c], n)
        g.remote_dma_fused([RemoteDMATransfer(dst_ids=[to_core(far)], dma_engine_mask=halves[c], remote_sem=T.sem["x%d_%d" % (k, c)],
                                              src=hx[16:144, :], dst=xb_at(k, 0, c))], local_sem=T.sem["l0"])
    for c in range(W // XN):
        hx = T["hx%d" % c]
        g.wait_ge(T.sem["d%d" % c], 32)
        g.remote_dma_fused([RemoteDMATransfer(dst_ids=[to_core(op)], dma_engine_mask=halves[j], remote_sem=T.sem["x%d_%d" % (2 + j, c)],
                                              src=hx[32 - 32 * j:160 - 32 * j, :], dst=xb_at(j, 1, c)) for j in range(2)],
                           local_sem=T.sem["l0"])
    g.wait_ge(T.sem["l0"], 3 * n * (W // XN))
